import numpy as np, ml_dtypes
CORES = [16,17,18,19,32,33,34,35]
N = 8
import mx_ref
BF = ml_dtypes.bfloat16
def gcols(t, e):
    v = np.concatenate([t.reshape(8, 16, -1, 4), np.zeros((8, 16, 1, 4), BF)], axis=2)
    return np.ascontiguousarray(np.stack([v[g][:, e[g]] for g in range(8)])).reshape(128, -1)
def tile(rs):
    return np.stack(rs, axis=2).reshape(128, -1).astype(BF)
def pick(q, e):
    c = np.concatenate([q[0].reshape(128, -1, 4), np.zeros((128, 1, 4), np.uint8)], axis=1); s = np.concatenate([q[1], np.ones((16, 1), np.uint8)], axis=1)
    return (np.ascontiguousarray(c[:, e].reshape(128, -1)), np.ascontiguousarray(s[:, e]))
def join(*qs):
    return (np.concatenate([q[0] for q in qs], axis=1), np.concatenate([q[1] for q in qs], axis=1))
def put(q, e, v):
    c, s = q[0].reshape(128, -1, 4).copy(), q[1].copy(); c[:, e] = v[0].reshape(128, -1, 4); s[:, e] = v[1]
    return (c.reshape(128, -1), s)
def pk(c, s):
    return (np.ascontiguousarray(c), mx_ref.live(s))
def emit(q):
    return q[0], q[1]
def packed(v, rng):
    q = [mx_ref.quantize(np.ascontiguousarray(v[r])) for r in range(N)]
    return np.stack([a for a, b in q]), np.stack([mx_ref.plane(b, rng) for a, b in q])
def values_of_codes():
    e, c = np.zeros((128, 128, 4), np.float32), np.zeros((128, 2, 4), np.uint8)
    e[np.arange(128), np.arange(128), 0] = 1
    c[:127, :, 0] = np.arange(256).reshape(2, 128).T[:127]
    return mx_ref.matmul(mx_ref.quantize(e.reshape(128, 512).astype(BF)), (c.reshape(128, 8), np.full((16, 2), 127, np.uint8))).T.reshape(-1).astype(np.float64)
CODE_VALUE, SCALE_VALUE = values_of_codes(), 2.0 ** (np.arange(256) - 127.0)
def decode(q):
    return (CODE_VALUE[q[0]].reshape(16, 8, -1, 4) * SCALE_VALUE[q[1]][:, None, :, None] + 0.0).reshape(128, -1).astype(np.float32)
def f(rng, *shape):
    return mx_ref.flush((rng.standard_normal(shape, dtype=np.float32) * np.exp2(rng.integers(-2, 3, shape[:-1] + (1,)))).astype(BF))
def wide(rng, *shape, cols=0):
    v = rng.standard_normal(shape, dtype=np.float32) * np.exp2(rng.integers(-12, 13, shape)).astype(np.float32)
    if cols: v *= np.repeat(np.exp2(rng.integers(-cols, cols + 1, shape[:-2] + (1, shape[-1] // 4))) * (rng.random(shape[:-2] + (1, shape[-1] // 4)) > 0.0625), 4, axis=-1).astype(np.float32)
    return mx_ref.flush(v.astype(BF))
C, V, R = 384, 16, 3
STEP = [1, 2, 4]
def match(a, b):
    k = (np.arange(C)[:, None] + np.arange(-V, V + 1)) % C
    return np.argmin(np.abs(a[:, :, None] - b[:, k]), axis=2) - V
def inherit(d, e):
    place = np.arange(C)
    ok = np.take_along_axis(e, (place + d) % C, axis=1) == -d
    before = np.maximum.accumulate(np.where(ok, place, -1), axis=1)
    behind = np.minimum.accumulate(np.where(ok, place, C)[:, ::-1], axis=1)[:, ::-1]
    before, behind = np.where(before < 0, behind, before), np.where(behind == C, before, behind)
    z = np.concatenate([d, np.zeros((8, 1), int)], axis=1)
    return np.take_along_axis(z, before, axis=1), np.take_along_axis(z, behind, axis=1)
def big(v):
    v = v.astype(np.float32)
    v[np.abs(v) < np.float32(2.0 ** -16)] = 0
    return v.astype(BF)
def numbers_of(rng):
    return {"x": big(f(rng, N, 128, 4 * C)), "u": np.array(f(rng, N, 128, 512)), "v": np.array(f(rng, N, 128, 512))}
def weights(rng, still=[]):
    w = np.array(f(rng, N, 128, 2048)).reshape(N, 8, 16, 4, 8, 16, 4)
    for i in still:
        w[:, :, i] = 0
        w[:, :, :, :, :, i] = 0
    c, p = packed(w.reshape(N, 128, 2048), rng)
    return {"wc": c, "ws": p}
def digits(k, n):
    z = k[..., None] & (1 << np.arange(4 * n))
    return np.stack([z[..., 4 * i:4 * i + 4] for i in range(n)], axis=2)
def signs(rng):
    p = rng.permutation(8)
    m = (p // 2) ^ (p % 2 * (N - 1))
    c = np.array([[1.0 - 2 * (bin(r & int(k)).count("1") % 2) for k in m] for r in range(N)])
    return p // 2, c * rng.choice([-1.0, 1.0], 8)
def planted(case, rng):
    a, b = np.zeros(C, int), np.full(C, 100)
    if case < 3:
        a = rng.permutation(C)
        b = np.roll(a, [V, -V, int(rng.integers(-V, V + 1))][case])
    elif 3 < case < 7:
        n = C // (2 * V + 2)
        j = [np.array([0]), np.array([C - 1]), np.arange(n) * (2 * V + 2) + rng.integers(2 * V + 2)][case - 4]
        e = [np.array([-V]), np.array([V]), rng.permutation(np.concatenate([[-V, V], rng.integers(1 - V, V, n - 2)]))][case - 4]
        a[j] = 40
        b[(j + e) % C] = 50
    elif case == 7:
        a, b = rng.integers(0, 40, C), rng.integers(0, 40, C)
    return a, b
def setup_inputs(rng):
    return {**numbers_of(rng), **weights(rng)}
def setup_inputs_ties(rng):
    d = numbers_of(rng)
    x = d["x"].reshape(N, 8, 16, C, 4)
    u = d["u"].reshape(N, 8, 16, 128, 4)
    a = x[0][:, :8, :3].copy()
    a[:, :, 2] = 0
    e = int(rng.integers(N))
    for r in range(N):
        k = np.full(C, rng.integers(2)) if r in (e, e ^ STEP[R - 1]) else rng.permutation(C) % 3
        x[r][:, :8] = a[:, :, k]
    x[e ^ STEP[1]] = 0
    u[1:] = u[0]
    u[:, :, 8:, ::16] = 0
    return {"x": x.reshape(N, 128, 4 * C), "u": u.reshape(N, 128, 512), "v": d["v"], **weights(rng, range(8))}
def setup_inputs_near(rng):
    d = numbers_of(rng)
    o, c = signs(rng)
    x = d["x"].astype(np.float32).reshape(N, 8, 16, C, 4)
    u = d["u"].reshape(N, 128, 128, 4)
    size = np.where(o < 2, 2.0 ** -23, 2.0 ** -27)
    x[:, :, 0] = 0
    x[:, :, 8:] = 0
    x[:, :, 0, :, 0] = (c * (o < 2))[:, :, None]
    x[:, :, 8:10] = digits(rng.integers(0, 256, (N, 8, C)), 2) * size[:, None, None, None]
    x[:, :, 10, :, 0] = rng.integers(8, 16, (N, 8, C)) * (o == 3)[:, None] * 2.0 ** -30
    u[:, :, ::16] = 0
    for g in range(8):
        h, k = 16 * g, 1.0 if o[g] == 0 else 2.0 ** -30
        u[:, h, h, 0] = k
        u[:, h + 8:h + 10, h] = k
        u[:, h + 10, h, 0] = k
    return {"x": x.reshape(N, 128, 4 * C).astype(BF), "u": u.reshape(N, 128, 512), "v": d["v"], **weights(rng, [0, 8, 9, 10, 11, 12, 13, 14, 15])}
def setup_inputs_huge(rng):
    d = numbers_of(rng)
    o, c = signs(rng)
    n = np.stack([rng.permutation(513)[:C] for r in range(N)])
    i = np.argsort(rng.random((N, 512, C)), axis=1)
    x = (-2.0 ** 30 * np.where(i < n[:, None], 1.0, 0.875)).reshape(N, 128, 4, C).transpose(0, 1, 3, 2)
    u = d["u"].reshape(N, 128, 128, 4)
    u[:, :, ::16] = (2.0 ** 30 * c).astype(np.float32).astype(BF)[:, None, :, None]
    return {"x": np.ascontiguousarray(x).astype(np.float32).reshape(N, 128, 4 * C).astype(BF), "u": u.reshape(N, 128, 512), "v": d["v"], **weights(rng, range(16))}
def setup_inputs_lists(rng):
    d = numbers_of(rng)
    s = np.zeros((N, 8, C), int)
    for r in range(N):
        p = r ^ STEP[R - 1]
        if r < p:
            n = rng.permutation(8)
            for g in range(8): s[r, g], s[p, g] = planted(int(n[g]), rng)
    x = d["x"].astype(np.float32).reshape(N, 8, 16, C, 4)
    u = d["u"].reshape(N, 128, 128, 4)
    x[:, :, 8:] = 0
    x[:, :, 8:11] = digits(s, 3)
    u[:, :, ::16] = 0
    for h in range(0, 128, 16): u[:, h + 8:h + 11, h] = 1
    return {"x": x.reshape(N, 128, 4 * C).astype(BF), "u": u.reshape(N, 128, 512), "v": d["v"], **weights(rng, range(8, 16))}
def setup_inputs_spread(rng):
    d = setup_inputs(rng)
    d["x"] = big(wide(rng, N, 128, 4 * C, cols=6))
    return d
def check_inputs(d):
    b = []
    for k in ("x", "u", "v"):
        a = np.abs(d[k].astype(np.float32))
        if not (np.isfinite(a).all() and ((a == 0) | (a >= 2.0 ** -30) & (a <= 2.0 ** 30)).all()): b.append("a value of " + k)
    if ((d["wc"] & 0x7F) == 0x7F).any(): b.append("a code of wc that is no number")
    none, least, most = [emit(mx_ref.quantize(np.full((128, 16), k, np.float32).astype(BF)))[1][0, 0] for k in (0.0, 2.0 ** -30, 2.0 ** 30)]
    for r in range(N):
        s = mx_ref.live(d["ws"][r])
        if ((s != none) & ((s < least) | (s > most))).any(): b.append("a scale of ws")
        if ((s == none)[:, None, :, None] & ((d["wc"][r].reshape(16, 8, -1, 4) & 0x7F) != 0)).any(): b.append("a code of wc under the scale of zeros")
    return b
def reference(x, u, v, wc, ws):
    qu = [mx_ref.quantize(u[r]) for r in range(N)]
    lay = [pk(wc[r], ws[r]) for r in range(N)]
    now = [x[r] for r in range(N)]
    place = np.arange(C)
    y, od = np.zeros((N, 128, C), np.float32), np.zeros((N, 8, 2 * C), np.float32)
    oc, osc = np.zeros((N, 128, 4 * C), np.uint8), np.zeros((N, 16, C), np.uint8)
    for t in range(R):
        q = [mx_ref.quantize(now[r]) for r in range(N)]
        s = [mx_ref.matmul(qu[r], q[r])[::16] for r in range(N)]
        held = [decode(q[r]) for r in range(N)]
        d = [match(s[r], s[r ^ STEP[t]]) for r in range(N)]
        made = []
        for r in range(N):
            e = r ^ STEP[t]
            l, h = inherit(d[r], d[e])
            p = held[e].astype(BF)
            z = ((gcols(p, (place + l) % C).astype(np.float32) + gcols(p, (place + h) % C).astype(np.float32)) * np.float32(0.5)).astype(BF)
            qz = mx_ref.quantize(z)
            made.append(tile([np.maximum(mx_ref.matmul(pick(lay[r], np.arange(128 * b, 128 * b + 128)), qz), np.float32(0.0)) * np.float32(0.03125) + held[r][:, b::4] for b in range(4)]))
            od[r] = np.concatenate([l, h], axis=1)
        now = made
    for r in range(N):
        last = mx_ref.quantize(now[r])
        y[r] = mx_ref.matmul(mx_ref.quantize(v[r]), last)
        oc[r], osc[r] = emit(last)
    return {"y": y, "od": od, "oc": oc, "osc": osc}

@@ -1,0 +1,623 @@
+from concourse.bass import DstId, RemoteDMATransfer
+from concourse.mybir import dt, AluOpType, ActivationFunctionType
+
+ALU = AluOpType
+ACT = ActivationFunctionType
+C, V, R = 384, 16, 3
+NO = 2 * V + 1
+SG = NO + 1
+XW = C + 2 * V
+CH = 8
+FIRST = [2, 3, 2]
+REST = [0, 1, 1]
+CUT = [160, 224, 256, 224]
+TAIL = 0
+NH, NL = 3, 3
+RELAY = True
+PICK = True
+Q4, U8, BF, F32, I32, U16 = "float8_e4m3fn_x4", "uint8", "bfloat16", "float32", "int32", "uint16"
+
+SCRATCH = {"ps": ("psum", [128, 4096], F32)}
+
+
+def _sb(name, n, ty):
+    SCRATCH[name] = ("sbuf", [128, n], ty)
+
+
+def _reach(r):
+    return 2 * V + 64 * FIRST[r]
+
+
+for _r in range(R + 1):
+    _sb("qx%d" % _r, C, Q4)
+    _sb("sx%d" % _r, C, U8)
+for _r in range(R):
+    _sb("lq%d" % _r, C, Q4)
+    _sb("ls%d" % _r, C, U8)
+    _sb("ulq%d" % _r, 8, Q4)
+    _sb("uls%d" % _r, 32, U8)
+    _sb("upq%d" % _r, 128, Q4)
+    _sb("ups%d" % _r, 128, U8)
+for _n, _w, _t in [
+        ("x0", 4 * C, BF), ("x1", 4 * C, BF), ("ut", 512, BF), ("vt", 512, BF),
+        ("uq", 128, Q4), ("us", 128, U8), ("urq", 128, Q4), ("urs", 128, U8), ("vq", 128, Q4), ("vs", 128, U8),
+        ("wq", 512, Q4), ("wp", 512, U8),
+        ("hq", C, Q4), ("hs", C, U8), ("huq", 8, Q4), ("hus", 32, U8),
+        ("pi", 24, I32), ("pa", 24, I32), ("pb", 8, I32), ("iw", 18, F32), ("im", 18, F32), ("ij", 24, F32), ("ik", 16, F32),
+        ("ie", 512, BF), ("ic", 128, F32), ("col", 24, F32), ("wa", 18, F32), ("wb", 18, F32), ("wd", 18, F32),
+        ("sa", 4, F32), ("sb", 4, F32), ("sd", 4, F32), ("ma", 18, F32), ("mb", 18, I32), ("lm", 18, U16),
+        ("crow", 2 * CH * SG, BF), ("ca", 16, F32), ("cb", 16, F32), ("c16", 16, BF), ("cx", C, BF), ("jt", 24, F32),
+        ("rst", CH * SG, F32),
+        ("lu16", 8, U16), ("lu1", 8, U16), ("lrep", 24, U16), ("lw", 18, U16), ("lw3", 10, U16), ("lsc", 6, U16),
+        ("et", 2048, BF), ("eq", 512, Q4), ("es", 512, U8), ("ct", 4 * C, BF), ("cq", C, Q4), ("cs", C, U8),
+        ("ow", 2 * C, F32), ("pw", 2 * C, F32), ("og", 288, F32), ("ba", 288, F32),
+        ("dd", 48 * SG, F32), ("pm", 48 * SG, F32), ("nq", 48 * SG, BF), ("cnt", 48 * SG, BF),
+        ("mt", 4 * (XW + 16), BF), ("mq", XW, Q4), ("ms", XW, U8),
+        ("dpx", XW, BF), ("nd", C, BF), ("exd", C, BF), ("exh", C, BF), ("exl", C, BF),
+        ("kd", 24, F32), ("kh", 24, F32), ("kl", 24, F32), ("fd", 24, U16), ("fh", 24, U16), ("fl", 24, U16),
+        ("ok", C, BF), ("nok", C, BF), ("okd", C, BF), ("l1", C, BF), ("lh", 2 * C, BF),
+        ("pp", 4 * XW, BF), ("gh", 4 * C, BF), ("yt", 4 * C, BF), ("yq", C, Q4), ("ys", C, U8),
+        ("rb", 4 * C, F32), ("yo", C, F32)]:
+    _sb(_n, _w, _t)
+
+NDMA = 8
+SEMAPHORES = (["v", "a", "t", "g", "sent", "out", "hu", "hc0", "hp0", "hc1", "hp1", "xr"] + ["ua%d" % _r for _r in range(R)]
+              + ["xa%d%d" % (_r, _k) for _r in range(R) for _k in range(2)] + ["d%d" % _k for _k in range(NDMA)])
+
+
+def _helper(c, topo):
+    mine = [k for k in topo.cores_of(c) if topo.die(k) == topo.die(c)]
+    other = [k for k in topo.cores_of(c) if topo.die(k) != topo.die(c)]
+    return other[mine.index(c)]
+
+
+def _send(g, T, topo, dst, en, out, in_, sem):
+    rid, pid, _ = topo.addr(dst)
+    g.remote_dma(out, in_, sem, T.sem.sent, pid, rid, sum(1 << e for e in en))
+    return len(en)
+
+
+def _send_u(g, T, topo, dst, en, oq, osc, iq, isc, sem):
+    rid, pid, _ = topo.addr(dst)
+    half = len(en) // 2
+    to = [DstId(rid=rid, pnc=pid)]
+    g.remote_dma_fused([
+        RemoteDMATransfer(dst_ids=to, dma_engine_mask=sum(1 << e for e in en[:half]), remote_sem=sem,
+                          src=iq.bitcast(dt.uint8), dst=oq.bitcast(dt.uint8)),
+        RemoteDMATransfer(dst_ids=to, dma_engine_mask=sum(1 << e for e in en[half:]), remote_sem=sem, src=isc, dst=osc)],
+        local_sem=T.sem.sent)
+    return len(en)
+
+
+def _far(T, topo, c, r):
+    p = T.cores[T.rank_of(c) ^ (1 << r)]
+    h = _helper(c, topo)
+    return RELAY and topo.chip(p) != topo.chip(c) and T.rank_of(h) is None and topo.may_write(h, p) and CUT[r] > _reach(r)
+
+
+def _home(T, topo, c, r):
+    p = T.cores[T.rank_of(c) ^ (1 << r)]
+    return [e for e in topo.engines(c, _helper(c, topo)) if e not in topo.engines(c, p)]
+
+
+def _handed(r):
+    return [(_reach(r), CUT[r])] + ([(C - TAIL, C)] if TAIL else [])
+
+
+def _hand_on(g, core, T, topo):
+    for c in T.cores:
+        for r in range(R):
+            if _helper(c, topo) == core and _far(T, topo, c, r):
+                p = T.cores[T.rank_of(c) ^ (1 << r)]
+                n, en = len(_home(T, topo, c, r)), topo.engines(core, p)
+                g.wait_ge(T.sem.hu, n)
+                sent = _send_u(g, T, topo, p, en, T["ulq%d" % r][:], T["uls%d" % r][:], T.huq[:], T.hus[:], T.sem["ua%d" % r])
+                for k, (a, b) in enumerate(_handed(r)):
+                    g.wait_ge(T.sem["hc%d" % k], n)
+                    sent += _send(g, T, topo, p, en, T["lq%d" % r][:, a:b].bitcast(dt.uint8), T.hq[:, a:b].bitcast(dt.uint8), T.sem.xr)
+                    g.wait_ge(T.sem["hp%d" % k], n)
+                    sent += _send(g, T, topo, p, en, T["ls%d" % r][:, a:b], T.hs[:, a:b], T.sem.xr)
+                g.wait_ge(T.sem.sent, sent)
+
+
+def rank_program(g, core, T, topo):
+    rank = T.rank_of(core)
+    if rank is None:
+        _hand_on(g, core, T, topo)
+        return
+    queue = {"v": g.vector, "a": g.scalar, "t": g.tensor, "g": g, "s": g.sync}
+    count = {"sent": 0, "out": 0}
+    known = {q: {} for q in queue}
+    writer, readers = {}, {}
+    ndma = [0]
+
+    def wait(q, ev):
+        sem, n, seen = ev[0], ev[1], ev[2]
+        if known[q].get(sem, 0) < n:
+            queue[q].wait_ge(T.sem[sem], n)
+            known[q][sem] = n
+            for s in seen:
+                if known[q].get(s, 0) < seen[s]:
+                    known[q][s] = seen[s]
+
+    def order(q, r, w):
+        evs = []
+        for k in r:
+            if k in writer:
+                evs.append(writer[k])
+            if k.startswith("ps"):
+                evs.extend(e for e in readers.get(k, []) if e[0] != q)
+        for k in w:
+            if k in writer:
+                evs.append(writer[k])
+            evs.extend(readers.get(k, []))
+        evs.sort(key=lambda e: -e[1])
+        for e in evs:
+            wait(q, e)
+
+    def note(ev, r, w):
+        for k in r:
+            readers.setdefault(k, []).append(ev)
+        for k in w:
+            writer[k] = ev
+            readers[k] = []
+
+    def op(q, r, w, call):
+        order(q, r, w)
+        call(queue[q]).then_inc(T.sem[q], 1)
+        count[q] = count.get(q, 0) + 1
+        note((q, count[q], dict(known[q])), r, w)
+
+    def dma(q, r, w, out, in_):
+        order(q, r, w)
+        s = "d%d" % ndma[0]
+        ndma[0] += 1
+        queue[q].dma_start(out, in_).then_inc(T.sem[s], 16)
+        count[s] = 16
+        note((s, 16, dict(known[q])), r, w)
+
+    def put(q, r, out, in_):
+        order(q, r, [])
+        queue[q].dma_start(out, in_).then_inc(T.sem.out, 16)
+        count["out"] += 16
+
+    def arrives(sem, n, w):
+        count[sem] = n
+        note((sem, n, {}), [], w)
+
+    def words(ap):
+        return ap.bitcast(dt.uint32)
+
+    def raw(ap):
+        return ap.bitcast(dt.uint8)
+
+    def bank(b, n, a=0):
+        return T.ps[:, 512 * b + a:512 * b + a + n]
+
+    def ts(out, in0, s1, s2, o0, o1, r, w):
+        if o1 is None:
+            op("v", r, w, lambda e: e.tensor_scalar(out, in0, s1, None, o0))
+        else:
+            op("v", r, w, lambda e: e.tensor_scalar(out, in0, s1, s2, o0, o1))
+
+    def tt(out, in0, in1, o, r, w):
+        op("v", r, w, lambda e: e.tensor_tensor(out, in0, in1, o))
+
+    def cp(out, in_, r, w):
+        op("v", r, w, lambda e: e.tensor_copy(out, in_))
+
+    def fill(out, c, w):
+        op("v", [], w, lambda e: e.memset(out, c))
+
+    def scan(out, d0, d1, init, o0, o1, r, w):
+        op("v", r, w, lambda e: e.tensor_tensor_scan(out, d0, d1, init, o0, o1))
+
+    def quant(q, s, in_, r, w):
+        op("v", r, w, lambda e: e.quantize_mx(q, s, in_))
+
+    def act(out, in_, f, r, w, **kw):
+        op("a", r, w, lambda e: e.activation(out, in_, f, **kw))
+
+    def mm(b, n, lq, ls, rq, rs, r):
+        op("t", r, ["ps%d" % b], lambda e: e.matmul_mx(bank(b, n), lq, ls, rq, rs, True, True))
+
+    def iota(name, out, pattern, base, cm):
+        if name == "pi":
+            op("g", [], [name], lambda e: e.iota(out, pattern, base, cm))
+        else:
+            op("g", [], [name], lambda e: e.iota(out, pattern, base, cm, allow_small_or_imprecise_dtypes=True))
+
+    mate = [T.cores[rank ^ (1 << r)] for r in range(R)]
+
+    def piece(r, k):
+        return (0, CUT[r]) if k == 0 else (CUT[r], C)
+
+    def ship_u(r):
+        order("g", ["urq", "urs"], [])
+        if _far(T, topo, core, r):
+            count["sent"] += _send_u(g, T, topo, _helper(core, topo), _home(T, topo, core, r), T.huq[:], T.hus[:],
+                                     T.urq[:, 0:8], T.urs[:, 0:32], T.sem.hu)
+            arrives("ua%d" % r, len(topo.engines(_helper(mate[r], topo), core)), ["ul%d" % r])
+        else:
+            count["sent"] += _send_u(g, T, topo, mate[r], topo.engines(core, mate[r]), T["ulq%d" % r][:], T["uls%d" % r][:],
+                                     T.urq[:, 0:8], T.urs[:, 0:32], T.sem["ua%d" % r])
+            arrives("ua%d" % r, len(topo.engines(mate[r], core)), ["ul%d" % r])
+
+    def ship_x(r, k, between=None):
+        a, b = piece(r, k)
+        q, s = T["qx%d" % r], T["sx%d" % r]
+        order("g", ["qx%d%d" % (r, k)], [])
+        far = _far(T, topo, core, r) and k < len(_handed(r))
+        if far:
+            b, z = _handed(r)[k]
+        sem, en = T.sem["xa%d%d" % (r, k)], topo.engines(core, mate[r])
+        count["sent"] += _send(g, T, topo, mate[r], en, raw(T["lq%d" % r][:, a:b]), raw(q[:, a:b]), sem)
+        if between:
+            between()
+        count["sent"] += _send(g, T, topo, mate[r], en, T["ls%d" % r][:, a:b], s[:, a:b], sem)
+        arrives("xa%d%d" % (r, k), 2 * len(topo.engines(mate[r], core)), ["lx%d%d" % (r, k)])
+        if far:
+            h, en = _helper(core, topo), _home(T, topo, core, r)
+            count["sent"] += _send(g, T, topo, h, en, raw(T.hq[:, b:z]), raw(q[:, b:z]), T.sem["hc%d" % k])
+            count["sent"] += _send(g, T, topo, h, en, T.hs[:, b:z], s[:, b:z], T.sem["hp%d" % k])
+            arrives("xr", 2 * len(_handed(r)) * len(topo.engines(_helper(mate[r], topo), core)), ["lx%d2" % r])
+
+    def spread_u(r):
+        cp(words(T["upq%d" % r][:]), words(T["ulq%d" % r][:]).indirect(T.lu1[:]), ["ul%d" % r, "lu1"], ["upq%d" % r])
+        act(T["ups%d" % r][:], T["uls%d" % r][:, 0:8].indirect(T.lu1[:]), ACT.Copy, ["ul%d" % r, "lu1"], ["ups%d" % r])
+
+    def quant_x(r, k, tile, key):
+        a, b = piece(r, k)
+        quant(T["qx%d" % r][:, a:b], T["sx%d" % r][:, a:b], tile[:, 4 * a:4 * b], key, ["qx%d%d" % (r, k)])
+
+    PL, PL1, PLH, M0, M1, PF, C8, CB, T1, MC, S0, X1, X2, X3, X4, X5, JC = [T.col[:, k:k + 1] for k in range(17)]
+
+    def span(r, k):
+        return (0, _reach(r)) if k == 0 else (_reach(r), C)
+
+    def own_mm(r, k, b0, b1):
+        a, b = span(r, k)
+        for bb in (b0, b1):
+            mm(bb, b - a, T.urq[:], T.urs[:], T["qx%d" % r][:, a:b], T["sx%d" % r][:, a:b],
+               ["urq", "urs"] + ["qx%d%d" % (r, i) for i in range(k + 1)])
+
+    def landed(r, k):
+        return ["lx%d0" % r] if k == 0 else ["lx%d%d" % (r, i) for i in range(3)]
+
+    def far_mm(r, k, b0, b1):
+        a, b = span(r, k)
+        for bb in (b1, b0):
+            mm(bb, b - a, T["upq%d" % r][:], T["ups%d" % r][:], T["lq%d" % r][:, a:b], T["ls%d" % r][:, a:b],
+               ["upq%d" % r, "ups%d" % r] + landed(r, k))
+
+    def evac_b(name, r, k, bk, m):
+        a, b = span(r, k)
+        ts(T[name][:, a:b], bank(bk, b - a), m, None, ALU.mult, None, ["ps%d" % bk, "mask"],
+           [name + "b0", name + "b1"] if k == 0 else [name + "b1"])
+
+    def evac_a(name, r, k, bk, m):
+        a, b = span(r, k)
+        act(T[name][:, C + a:C + b], bank(bk, b - a), ACT.Identity, ["ps%d" % bk, "mask"],
+            [name + "a0", name + "a1"] if k == 0 else [name + "a1"], scale=m)
+
+    def cut(name, r, k):
+        n = 3 * FIRST[r]
+        return T[name][:].indirect(T.lw[:, 0:n] if k == 0 else T.lw[:, n:18] if n % 2 == 0 else T.lw3[:, 0:18 - n])
+
+    def rows(name):
+        return [name + x for x in ("b0", "a0", "b1", "a1")] + ["lw", "lw3"]
+
+    def cols(name, r, k):
+        return T[name][:, 0:48 * FIRST[r]] if k == 0 else T[name][:, 48 * FIRST[r]:288]
+
+    def chunks(name, r, k):
+        return [name + "%d" % i for i in (range(FIRST[r]) if k == 0 else range(FIRST[r], 6))]
+
+    def own_windows(r, k):
+        act(cols("og", r, k), cut("ow", r, k), ACT.Copy, rows("ow"), chunks("og", r, k))
+
+    def windows(r, k):
+        tt(cols("ba", r, k), cut("pw", r, k), cols("og", r, k), ALU.add, rows("pw") + chunks("og", r, k), chunks("ba", r, k))
+
+    dma("s", [], ["ut"], T.ut[:], T.u[:])
+    dma("a", [], ["x00"], T.x0[:, 0:4 * CUT[0]], T.x[:, 0:4 * CUT[0]])
+    dma("s", [], ["x01"], T.x0[:, 4 * CUT[0]:4 * C], T.x[:, 4 * CUT[0]:4 * C])
+    iota("pi", T.pi[:], [[0, 24]], 0, 1)
+    iota("iw", T.iw[:], [[64, 6], [-16, 3]], 0, 0)
+    iota("ie", T.ie[:], [[1, 512]], 0, -4)
+    iota("ic", T.ic[:], [[1, 8], [0, 16]], 0, 0)
+    ts(T.pb[:], T.pi[:, 0:8], 7, None, ALU.bitwise_and, None, ["pi"], ["pb"])
+    ts(T.pa[:], T.pi[:], 15, None, ALU.bitwise_and, None, ["pi"], ["pa"])
+    cp(PF, T.pi[:, 0:1], ["pi"], ["pf"])
+    ts(T.lu16[:], T.pb[:], 16.0, None, ALU.mult, None, ["pb"], ["lu16"])
+    cp(PL, T.pa[:, 0:1], ["pa"], ["pl"])
+    cp(T.lu1[:], T.pb[:], ["pb"], ["lu1"])
+    cp(T.lrep[:], T.pa[:], ["pa"], ["lrep"])
+    ts(C8, PF, PL, 0.5, ALU.subtract, ALU.mult, ["pf", "pl"], ["c8"])
+    ts(M0, PL, 8.0, None, ALU.is_lt, None, ["pl"], ["m0"])
+    ts(T1, PL, 2.0, 1.0, ALU.mult, ALU.add, ["pl"], ["t1"])
+    ts(M1, PL, 8.0, None, ALU.is_ge, None, ["pl", "m0"], ["mask"])
+    ts(CB, C8, PL, 39.0, ALU.subtract, ALU.add, ["c8", "pl"], ["cb8"])
+    ts(S0, C8, PL, float(V), ALU.add, ALU.add, ["c8", "pl"], ["s0"])
+    ts(T1, T1, M1, None, ALU.mult, None, ["t1", "mask"], ["t1"])
+    ts(T.wa[:, 0:9], T.iw[:, 0:9], CB, None, ALU.add, None, ["iw", "cb8"], ["wa0"])
+    ts(T.wa[:, 9:12], T.iw[:, 15:18], CB, None, ALU.add, None, ["iw", "cb8"], ["wa1"])
+    ts(T.wa[:, 12:18], T.iw[:, 9:15], CB, None, ALU.add, None, ["iw", "cb8"], ["wa2"])
+    ts(MC, M1, float(C), None, ALU.mult, None, ["mask"], ["mc"])
+    ts(T.wa[:, 2:18:3], T.wa[:, 2:18:3], T1, None, ALU.add, None, ["wa0", "wa1", "wa2", "t1"], ["wa0", "wa1", "wa2"])
+    ts(T.sa[:, 0:1], M1, 56.0, S0, ALU.mult, ALU.add, ["mask", "s0"], ["sa0"])
+    ts(T.wb[:], T.wa[:], float(C), -float(C), ALU.is_ge, ALU.mult, ["wa0"], ["wb"])
+    ts(T.sa[:, 1:2], M1, 184.0, S0, ALU.mult, ALU.add, ["mask", "s0"], ["sa1"])
+    tt(T.wd[:], T.wa[:], T.wb[:], ALU.add, ["wa0", "wb"], ["wd"])
+    ts(X1, PF, 64.0, M1, ALU.is_ge, ALU.mult, ["pf", "mask"], ["x1"])
+    ts(T.wd[:, 2:18:3], T.wd[:, 2:18:3], MC, None, ALU.add, None, ["wd", "mc"], ["wd"])
+    ts(X3, PF, 96.0, float(C), ALU.is_ge, ALU.mult, ["pf"], ["x3"])
+    cp(T.lw[:], T.wd[:], ["wd"], ["lw"])
+    cp(T.lw3[:, 0:9], T.wd[:, 9:18], ["wd"], ["lw3"])
+    quant(T.uq[:], T.us[:], T.ut[:], ["ut"], ["uq"])
+    quant_x(0, 0, T.x0, ["x00"])
+    cp(words(T.urq[:]), words(T.uq[:]).indirect(T.lu16[:]), ["uq", "lu16"], ["urq"])
+    act(T.urs[:], T.us[:].indirect(T.lu16[:]), ACT.Copy, ["uq", "lu16"], ["urs"])
+    ship_x(0, 0, lambda: ship_u(0))
+    quant_x(0, 1, T.x0, ["x01"])
+    ship_x(0, 1)
+    iota("im", T.im[:], [[16, 18]], 0, 0)
+    iota("ij", T.ij[:], [[16, 24]], V, 0)
+    iota("ik", T.ik[:], [[1, 16]], 0, 0)
+    ship_u(1)
+    ship_u(2)
+    dma("s", [], ["wq"], raw(T.wq[:]), T.wc[:])
+    dma("s", [], ["wp"], T.wp[:], T.ws[:])
+    dma("s", [], ["vt"], T.vt[:], T.v[:])
+    own_mm(0, 0, 6, 7)
+    own_mm(0, 1, 4, 5)
+    tiles = ["et0", "et1", "et2", "et3"]
+    for b in range(4):
+        ts(T.et[:, 512 * b:512 * (b + 1)], T.ie[:], float(b), None, ALU.is_equal, None, ["ie"], ["et%d" % b])
+        if b < 2:
+            evac_b("ow", 0, b, 6 - 2 * b, M1)
+            evac_a("ow", 0, b, 7 - 2 * b, M0)
+    own_windows(0, 0)
+    own_windows(0, 1)
+    act(T.pw[:], T.et[:, 0:2 * C], ACT.Identity, tiles, ["pwb0", "pwa0", "pwb1", "pwa1"], scale=0.0)
+    act(T.ct[:], T.et[:, 0:4 * C], ACT.Identity, tiles, ["ct0", "ct1", "ct2"], scale=0.0)
+    fill(T.rst[:], 0.0, ["rst"])
+    fill(T.crow[:], 1.0, ["crow"])
+    fill(T.dd[:, 0:48 * SG:SG], 1e29, ["fill"])
+    fill(T.rst[:, 0:CH * SG:SG], 1e29, ["rst"])
+    fill(T.crow[:, NO:2 * CH * SG:SG], -float(V), ["crow"])
+    fill(T.mt[:], 0.0, ["mt"])
+    ts(T.sb[:, 0:1], T.sa[:, 1:2], 128.0, None, ALU.add, None, ["sa1"], ["sb"])
+    ts(X2, C8, -456.0, X1, ALU.add, ALU.mult, ["c8", "x1"], ["x2"])
+    ts(T.sd[:, 0:1], T.sb[:, 0:1], float(C), -float(C), ALU.is_ge, ALU.mult, ["sb"], ["sd"])
+    ts(X4, X3, M1, X2, ALU.mult, ALU.add, ["x3", "x2", "mask"], ["x4"])
+    ts(T.sb[:, 1:2], T.sb[:, 0:1], T.sd[:, 0:1], None, ALU.add, None, ["sb", "sd"], ["sb1"])
+    ts(X5, X4, PL, float(XW), ALU.add, ALU.add, ["x4", "pl"], ["x5"])
+    ts(T.lsc[:, 0:1], T.sa[:, 0:1], float(V), 4.0, ALU.add, ALU.mult, ["sa0"], ["lsc0"])
+    ts(T.lsc[:, 1:2], T.sb[:, 1:2], float(V), 4.0, ALU.add, ALU.mult, ["sb1"], ["lsc2"])
+    ts(T.lsc[:, 2:3], T.sa[:, 0:1], float(V + 192), 4.0, ALU.add, ALU.mult, ["sa0"], ["lsc3"])
+    ts(T.lsc[:, 4:5], X5, 4.0, None, ALU.mult, None, ["x5"], ["lsc1"])
+    ts(PLH, PL, -16.5, None, ALU.add, None, ["pl"], ["plh"])
+    ts(PL1, PL, 1.0, None, ALU.add, None, ["pl"], ["pl1"])
+    ts(JC, PL, 15.0, -64.0, ALU.is_lt, ALU.mult, ["pl"], ["jc"])
+    quant(T.eq[:], T.es[:], T.et[:], tiles, ["eq"])
+    spread_u(0)
+
+    def late_constants():
+        ts(T.ma[:], T.im[:], PLH, 1.0 / SG, ALU.add, ALU.mult, ["im", "plh"], ["ma"])
+        ts(T.ct[:, 0:512:4], T.ic[:], 8.0, PL, ALU.add, ALU.is_equal, ["ic", "pl"], ["ct0"])
+        cp(T.mb[:], T.ma[:], ["ma"], ["mb"])
+        ts(T.ct[:, 512:1024:4], T.ic[:], PL, None, ALU.is_equal, None, ["ic", "pl"], ["ct1"])
+        ts(T.lm[:], T.mb[:], float(SG), float(NO), ALU.mult, ALU.add, ["mb"], ["lm"])
+        ts(T.ct[:, 1024:1536:4], T.ic[:], PL, -1.0, ALU.is_equal, ALU.mult, ["ic", "pl"], ["ct2"])
+
+    def last_constants():
+        ts(T.ca[:], T.ik[:], PL, -1000.0, ALU.is_equal, ALU.mult, ["ik", "pl"], ["ca"])
+        ts(T.cb[:], T.ik[:], PL1, 64.0, ALU.is_equal, ALU.mult, ["ik", "pl1"], ["cb"])
+        ts(T.jt[:], T.ij[:], JC, PL, ALU.add, ALU.add, ["ij", "jc", "pl"], ["jt"])
+        tt(T.c16[:], T.ca[:], T.cb[:], ALU.add, ["ca", "cb"], ["c16"])
+        quant(T.cq[:], T.cs[:], T.ct[:], ["ct0", "ct1", "ct2"], ["cq"])
+
+    def diffs(k):
+        for q in range(CH):
+            s, o = CH * k + q, 48 * k
+            act(T.dd[:, SG * s + 1:SG * s + SG], T.ba[:, o + 7 - q:o + 40 - q], ACT.Abs, ["ba%d" % k], ["dd%d" % s],
+                bias=T.ba[:, o + 40 + q:o + 41 + q], scale=-1.0)
+
+    def made(k):
+        return ["fill"] + ["dd%d" % s for s in range(CH * k, CH * k + CH)]
+
+    def least(k):
+        a, b = CH * SG * k, CH * SG * (k + 1)
+        scan(T.pm[:, a:b], T.rst[:], T.dd[:, a:b], 0.0, ALU.add, ALU.min, ["rst"] + made(k), ["pm%d" % k])
+
+    def above(k):
+        a, b = CH * SG * k, CH * SG * (k + 1)
+        if PICK:
+            tt(T.nq[:, a:b], T.pm[:, a:b].indirect(T.lm[:, 0:CH * SG // 16]), T.dd[:, a:b], ALU.not_equal,
+               ["pm%d" % k, "lm"] + made(k), ["nq%d" % k])
+        else:
+            tt(T.nq[:, a:b], T.pm[:, a:b], T.dd[:, a:b], ALU.not_equal, ["pm%d" % k] + made(k), ["nq%d" % k])
+
+    def run(k0, k1):
+        a, b = CH * SG * k0, CH * SG * k1
+        scan(T.cnt[:, a:b], T.nq[:, a:b], T.crow[:, 0:b - a], 0.0, ALU.mult, ALU.add,
+             ["crow"] + ["nq%d" % k for k in range(k0, k1)], ["cnt%d" % k for k in range(k0, k1)])
+
+    def sixteenth(ex, row, key):
+        scan(T[ex][:], T.cx[:], row, 0.0, ALU.add, ALU.max, ["cx", key], [ex])
+
+    def place(kf, ex):
+        tt(T[kf][:], T[ex][:, 15:C:16], T.jt[:], ALU.add, [ex, "jt"], [kf])
+
+    def offsets(off, kf):
+        cp(T[off][:], T[kf][:], [kf], [off])
+
+    def unpack(q, s, keys):
+        for b in range(4):
+            mm(b, C, T.eq[:, 128 * b:128 * b + 128], T.es[:, 128 * b:128 * b + 128], q[:], s[:], ["eq"] + keys)
+
+    def evac_p(b):
+        o = XW * b
+        act(T.pp[:, o + V:o + V + C], bank(b, C), ACT.Identity, ["ps%d" % b], ["ppm%d" % b], scale=0.5)
+        act(T.pp[:, o:o + V], bank(b, V, C - V), ACT.Identity, ["ps%d" % b], ["ppa%d" % b], scale=0.5)
+        act(T.pp[:, o + V + C:o + XW], bank(b, V), ACT.Identity, ["ps%d" % b], ["ppz%d" % b], scale=0.5)
+
+    def plane(b):
+        return ["ppm%d" % b, "ppa%d" % b, "ppz%d" % b]
+
+    def take_h(r, k, b):
+        a, z = piece(r, k)
+        act(T.gh[:, C * b + a:C * b + z], T.pp[:, XW * b:XW * (b + 1)].indirect(T.fh[:, a // 16:z // 16]),
+            ACT.Copy, plane(b) + ["fh"], ["gh%d%d" % (k, b)])
+
+    def take_l(r, k, b):
+        a, z = piece(r, k)
+        tt(T.yt[:, 4 * a + b:4 * z:4], T.pp[:, XW * b:XW * (b + 1)].indirect(T.fl[:, a // 16:z // 16]),
+           T.gh[:, C * b + a:C * b + z], ALU.add, plane(b) + ["fl", "gh%d%d" % (k, b)], ["yt%d%d" % (k, b)])
+
+    def quant_y(r, k):
+        a, z = piece(r, k)
+        quant(T.yq[:, a:z], T.ys[:, a:z], T.yt[:, 4 * a:4 * z], ["yt%d%d" % (k, i) for i in range(4)], ["yq%d" % k])
+
+    def layer(r, k, b):
+        a, z = piece(r, k)
+        mm(4 + b, z - a, T.wq[:, 128 * b:128 * b + 128], T.wp[:, 128 * b:128 * b + 128], T.yq[:, a:z], T.ys[:, a:z],
+           ["wq", "wp", "yq%d" % k])
+
+    def relu(r, k, b):
+        a, z = piece(r, k)
+        act(T.rb[:, C * b + a:C * b + z], bank(4 + b, z - a), ACT.Relu, ["ps%d" % (4 + b)], ["rb%d%d" % (k, b)], scale=0.03125)
+
+    def add(r, k, b):
+        a, z = piece(r, k)
+        tt(T.x1[:, 4 * a + b:4 * z:4], T.rb[:, C * b + a:C * b + z], bank(b, z - a, a), ALU.add,
+           ["rb%d%d" % (k, b), "ps%d" % b], ["x1%d%d" % (k, b)])
+
+    def store(k, bk):
+        a, z = piece(R, k)
+        key = "qx%d%d" % (R, k)
+        mm(bk, z - a, T.vq[:], T.vs[:], T["qx%d" % R][:, a:z], T["sx%d" % R][:, a:z], ["vq", key])
+        put("s", [key], T.oc[:, 4 * a:4 * z], raw(T["qx%d" % R][:, a:z]))
+        for i in range(4):
+            put("s", [key], T.osc[4 * i:4 * i + 4, a:z], T["sx%d" % R][32 * i:32 * i + 4, a:z])
+
+    def store_y(k, bk):
+        a, z = piece(R, k)
+        act(T.yo[:, a:z], bank(bk, z - a), ACT.Copy, ["ps%d" % bk], ["yo%d" % k])
+        put("a", ["yo%d" % k], T.y[:, a:z], T.yo[:, a:z])
+
+    for r in range(R):
+        far_mm(r, 0, 4, 5)
+        evac_b("pw", r, 0, 4, M0)
+        evac_a("pw", r, 0, 5, M1)
+        windows(r, 0)
+        far_mm(r, 1, 6, 7)
+        if r == 0:
+            late_constants()
+            evac_b("pw", r, 1, 6, M0)
+        for k in range(6):
+            diffs(k)
+            if k == REST[r]:
+                if r > 0:
+                    evac_b("pw", r, 1, 6, M0)
+                evac_a("pw", r, 1, 7, M1)
+            least(k)
+            if k == REST[r]:
+                windows(r, 1)
+                unpack(T["lq%d" % r], T["ls%d" % r], landed(r, 1))
+            if k in (2, 4):
+                run(k - 2, k)
+            if k == 5:
+                run(4, 5)
+            above(k)
+            if k == 0 and r == 0:
+                last_constants()
+            if k == 4:
+                cp(T.mt[:].indirect(T.lsc[:, 4:5]), T.cnt[:, 16 * SG + NO:32 * SG:SG], ["cnt2", "cnt3", "lsc1"], ["mt"])
+        run(5, 6)
+        for b in range(3):
+            evac_p(b)
+        cp(T.mt[:].indirect(T.lsc[:, 0:3]), T.cnt[:, NO:48 * SG:SG], ["cnt%d" % k for k in range(6)] + ["lsc0", "lsc2", "lsc3"], ["mt"])
+        quant(T.mq[:], T.ms[:], T.mt[:, 0:4 * XW], ["mt"], ["mq"])
+        mm(4, XW, T.cq[:, 0:128], T.cs[:, 0:128], T.mq[:], T.ms[:], ["cq", "mq"])
+        mm(5, C, T.cq[:, 128:256], T.cs[:, 128:256], T.mq[:, V:V + C], T.ms[:, V:V + C], ["cq", "mq"])
+        mm(6, C, T.cq[:, 256:384], T.cs[:, 256:384], T.mq[:, V:V + C], T.ms[:, V:V + C], ["cq", "mq"])
+        if r == 0:
+            cp(T.cx[:], T.c16[:].indirect(T.lrep[:]), ["c16", "lrep"], ["cx"])
+        elif r == 1:
+            quant(T.vq[:], T.vs[:], T.vt[:], ["vt"], ["vq"])
+        act(T.dpx[:], bank(4, XW), ACT.Copy, ["ps4"], ["dpx"])
+        act(T.nd[:], bank(6, C), ACT.Copy, ["ps6"], ["nd"])
+        sixteenth("exd", bank(5, C), "ps5")
+        place("kd", "exd")
+        offsets("fd", "kd")
+        evac_p(3)
+        unpack(T["qx%d" % r], T["sx%d" % r], ["qx%d0" % r, "qx%d1" % r])
+        tt(T.ok[:], T.dpx[:].indirect(T.fd[:]), T.nd[:], ALU.is_equal, ["dpx", "fd", "nd"], ["ok"])
+        act(T.nok[:], T.ok[:], ACT.Identity, ["ok"], ["nok"], bias=1.0, scale=-1.0)
+        tt(T.okd[:], T.ok[:], bank(5, C), ALU.mult, ["ok", "ps5"], ["okd"])
+        scan(T.l1[:], T.nok[:], T.okd[:], 0.0, ALU.mult, ALU.add, ["nok", "okd"], ["l1"])
+        scan(T.lh[:, 2 * C - 1:C - 1:-1], T.nok[:, ::-1], T.okd[:, ::-1], T.l1[:, C - 1:C], ALU.mult, ALU.add, ["nok", "okd", "l1"], ["h"])
+        sixteenth("exh", T.lh[:, C:2 * C], "h")
+        place("kh", "exh")
+        scan(T.lh[:, 0:C], T.nok[:], T.okd[:], T.lh[:, C:C + 1], ALU.mult, ALU.add, ["nok", "okd", "h"], ["l"])
+        offsets("fh", "kh")
+        sixteenth("exl", T.lh[:, 0:C], "l")
+        place("kl", "exl")
+        offsets("fl", "kl")
+        if r == R - 1:
+            dma("g", ["l", "h"], [], T.od[:], T.lh[0:128:16, :])
+        n = r + 1
+        for b in range(4):
+            take_h(n, 0, b)
+        for b in range(NH):
+            take_h(n, 1, b)
+        for b in range(4):
+            take_l(n, 0, b)
+        quant_y(n, 0)
+        for b in range(4):
+            layer(n, 0, b)
+        for b in range(NL):
+            take_l(n, 1, b)
+        for b in range(4):
+            relu(n, 0, b)
+        for b in range(NH, 4):
+            take_h(n, 1, b)
+        for b in range(4):
+            add(n, 0, b)
+        quant_x(n, 0, T.x1, ["x10%d" % b for b in range(4)])
+        if n < R:
+            ship_x(n, 0)
+            own_mm(n, 0, 6, 7)
+        else:
+            store(0, 6)
+        for b in range(NL, 4):
+            take_l(n, 1, b)
+        quant_y(n, 1)
+        if n < R:
+            evac_a("ow", n, 0, 7, M0)
+            evac_b("ow", n, 0, 6, M1)
+            spread_u(n)
+        else:
+            store_y(0, 6)
+        for b in range(4):
+            layer(n, 1, b)
+            relu(n, 1, b)
+        if n < R:
+            own_windows(n, 0)
+        for b in range(4):
+            add(n, 1, b)
+        quant_x(n, 1, T.x1, ["x11%d" % b for b in range(4)])
+        if n < R:
+            ship_x(n, 1)
+            own_mm(n, 1, 6, 7)
+            evac_b("ow", n, 1, 6, M1)
+            evac_a("ow", n, 1, 7, M0)
+            own_windows(n, 1)
+        else:
+            store(1, 7)
+            store_y(1, 7)
+    for s in count:
+        if count[s] and max(known[q].get(s, 0) for q in known) < count[s]:
+            g.wait_ge(T.sem[s], count[s])

@@ -7,14 +7,15 @@ C, V, R = 384, 16, 3
 NO = 2 * V + 1
 SG = NO + 1
 XW = C + 2 * V
-CH = 8
-FIRST = [2, 3, 2]
-REST = [0, 1, 1]
-CUT = [160, 224, 256, 224]
-TAIL = 0
-NH, NL = 3, 3
-RELAY = True
-PICK = True
+ST = 16
+NS = 3
+CUT = [0, 160, 288, 384]
+SC = [8, 8]
+SUB = 64
+BIG = 1e29
+RUNS = [[(0, 160, 0), (160, 384, 0)],
+        [(0, 160, 0), (160, 288, 0), (288, 384, 0)],
+        [(0, 160, 0), (160, 288, 0), (288, 384, 0)]]
 Q4, U8, BF, F32, I32, U16 = "float8_e4m3fn_x4", "uint8", "bfloat16", "float32", "int32", "uint16"
 
 SCRATCH = {"ps": ("psum", [128, 4096], F32)}
@@ -24,13 +25,9 @@ def _sb(name, n, ty):
     SCRATCH[name] = ("sbuf", [128, n], ty)
 
 
-def _reach(r):
-    return 2 * V + 64 * FIRST[r]
-
-
 for _r in range(R + 1):
-    _sb("qx%d" % _r, C, Q4)
-    _sb("sx%d" % _r, C, U8)
+    _sb("qx%d" % _r, XW, Q4)
+    _sb("sx%d" % _r, XW, U8)
 for _r in range(R):
     _sb("lq%d" % _r, C, Q4)
     _sb("ls%d" % _r, C, U8)
@@ -39,30 +36,31 @@ for _r in range(R):
     _sb("upq%d" % _r, 128, Q4)
     _sb("ups%d" % _r, 128, U8)
 for _n, _w, _t in [
-        ("x0", 4 * C, BF), ("x1", 4 * C, BF), ("ut", 512, BF), ("vt", 512, BF),
+        ("x0", 4 * C, BF), ("x1", 4 * XW, BF), ("ut", 512, BF), ("vt", 512, BF),
         ("uq", 128, Q4), ("us", 128, U8), ("urq", 128, Q4), ("urs", 128, U8), ("vq", 128, Q4), ("vs", 128, U8),
-        ("wq", 512, Q4), ("wp", 512, U8),
-        ("hq", C, Q4), ("hs", C, U8), ("huq", 8, Q4), ("hus", 32, U8),
-        ("pi", 24, I32), ("pa", 24, I32), ("pb", 8, I32), ("iw", 18, F32), ("im", 18, F32), ("ij", 24, F32), ("ik", 16, F32),
-        ("ie", 512, BF), ("ic", 128, F32), ("col", 24, F32), ("wa", 18, F32), ("wb", 18, F32), ("wd", 18, F32),
-        ("sa", 4, F32), ("sb", 4, F32), ("sd", 4, F32), ("ma", 18, F32), ("mb", 18, I32), ("lm", 18, U16),
-        ("crow", 2 * CH * SG, BF), ("ca", 16, F32), ("cb", 16, F32), ("c16", 16, BF), ("cx", C, BF), ("jt", 24, F32),
-        ("rst", CH * SG, F32),
-        ("lu16", 8, U16), ("lu1", 8, U16), ("lrep", 24, U16), ("lw", 18, U16), ("lw3", 10, U16), ("lsc", 6, U16),
-        ("et", 2048, BF), ("eq", 512, Q4), ("es", 512, U8), ("ct", 4 * C, BF), ("cq", C, Q4), ("cs", C, U8),
-        ("ow", 2 * C, F32), ("pw", 2 * C, F32), ("og", 288, F32), ("ba", 288, F32),
-        ("dd", 48 * SG, F32), ("pm", 48 * SG, F32), ("nq", 48 * SG, BF), ("cnt", 48 * SG, BF),
-        ("mt", 4 * (XW + 16), BF), ("mq", XW, Q4), ("ms", XW, U8),
-        ("dpx", XW, BF), ("nd", C, BF), ("exd", C, BF), ("exh", C, BF), ("exl", C, BF),
-        ("kd", 24, F32), ("kh", 24, F32), ("kl", 24, F32), ("fd", 24, U16), ("fh", 24, U16), ("fl", 24, U16),
+        ("wq", 512, Q4), ("wp", 512, U8), ("hq", C, Q4), ("hs", C, U8),
+        ("pi", 8, I32), ("pa", 8, I32), ("pb", 8, I32), ("pc", 8, I32), ("pd", 8, I32),
+        ("iw", 12, F32), ("im", SG, F32), ("ik", 24, F32), ("iy", 96, F32),
+        ("ie", 512, BF), ("ic", 128, F32), ("col", 24, F32), ("wb", 12, F32), ("wd", 12, F32),
+        ("ma", SG, F32), ("mb", SG, I32), ("lm", SG, U16), ("crow", ST * SG, BF), ("rst", ST * SG, F32),
+        ("ca", 16, F32), ("cb", 16, F32), ("cc", 16, F32), ("cd", 16, F32), ("kd", C, F32),
+        ("ya", 4, F32), ("yb", 4, F32), ("yc", 4, F32), ("yd", 4, F32), ("ky", C, BF),
+        ("lu16", 8, U16), ("lu1", 8, U16), ("lw", 12, U16), ("la", 6, U16), ("lsc", 4, U16),
+        ("et", 2048, BF), ("eq", 512, Q4), ("es", 512, U8), ("ct", 1024, BF), ("cq", 256, Q4), ("cs", 256, U8),
+        ("ow", C, F32), ("pw", 2 * C, F32), ("og", 192, F32), ("ba", 192, F32),
+        ("dd", 48 * SG, F32), ("pm", 48 * SG, F32), ("gt", 48 * (SG + 8), BF), ("cnt", 48 * SG, BF), ("sj", 48 * SG, BF), ("acc", 48, F32),
+        ("mt", 4 * C, BF), ("mq", C, Q4), ("ms", C, U8),
+        ("dpx", XW, BF), ("nd", C, BF), ("exd", C, F32), ("exh", C, BF), ("exl", C, BF),
+        ("fd", 24, U16), ("fh", 96, U16), ("fl", 96, U16),
         ("ok", C, BF), ("nok", C, BF), ("okd", C, BF), ("l1", C, BF), ("lh", 2 * C, BF),
-        ("pp", 4 * XW, BF), ("gh", 4 * C, BF), ("yt", 4 * C, BF), ("yq", C, Q4), ("ys", C, U8),
+        ("pp", 4 * XW, BF), ("gh", 4 * C, BF), ("yt", 4 * XW, BF), ("yq", XW, Q4), ("ys", XW, U8),
         ("rb", 4 * C, F32), ("yo", C, F32)]:
     _sb(_n, _w, _t)
 
 NDMA = 8
-SEMAPHORES = (["v", "a", "t", "g", "sent", "out", "hu", "hc0", "hp0", "hc1", "hp1", "xr"] + ["ua%d" % _r for _r in range(R)]
-              + ["xa%d%d" % (_r, _k) for _r in range(R) for _k in range(2)] + ["d%d" % _k for _k in range(NDMA)])
+SEMAPHORES = (["v", "a", "t", "g", "sent", "out"] + ["ua%d" % _r for _r in range(R)]
+              + ["xa%d%d" % (_r, _k) for _r in range(R) for _k in range(len(RUNS[_r]))]
+              + ["h%s%d" % (_c, _k) for _c in "cp" for _k in range(4)] + ["d%d" % _k for _k in range(NDMA)])
 
 
 def _helper(c, topo):
@@ -92,16 +90,12 @@ def _send_u(g, T, topo, dst, en, oq, osc, iq, isc, sem):
 def _far(T, topo, c, r):
     p = T.cores[T.rank_of(c) ^ (1 << r)]
     h = _helper(c, topo)
-    return RELAY and topo.chip(p) != topo.chip(c) and T.rank_of(h) is None and topo.may_write(h, p) and CUT[r] > _reach(r)
+    return topo.chip(p) != topo.chip(c) and T.rank_of(h) is None and topo.may_write(h, p)
 
 
 def _home(T, topo, c, r):
     p = T.cores[T.rank_of(c) ^ (1 << r)]
     return [e for e in topo.engines(c, _helper(c, topo)) if e not in topo.engines(c, p)]
-
-
-def _handed(r):
-    return [(_reach(r), CUT[r])] + ([(C - TAIL, C)] if TAIL else [])
 
 
 def _hand_on(g, core, T, topo):
@@ -110,14 +104,16 @@ def _hand_on(g, core, T, topo):
             if _helper(c, topo) == core and _far(T, topo, c, r):
                 p = T.cores[T.rank_of(c) ^ (1 << r)]
                 n, en = len(_home(T, topo, c, r)), topo.engines(core, p)
-                g.wait_ge(T.sem.hu, n)
-                sent = _send_u(g, T, topo, p, en, T["ulq%d" % r][:], T["uls%d" % r][:], T.huq[:], T.hus[:], T.sem["ua%d" % r])
-                for k, (a, b) in enumerate(_handed(r)):
-                    g.wait_ge(T.sem["hc%d" % k], n)
-                    sent += _send(g, T, topo, p, en, T["lq%d" % r][:, a:b].bitcast(dt.uint8), T.hq[:, a:b].bitcast(dt.uint8), T.sem.xr)
-                    g.wait_ge(T.sem["hp%d" % k], n)
-                    sent += _send(g, T, topo, p, en, T["ls%d" % r][:, a:b], T.hs[:, a:b], T.sem.xr)
-                g.wait_ge(T.sem.sent, sent)
+                sent = 0
+                for k, (a, b, via) in enumerate(RUNS[r]):
+                    if via:
+                        sem = T.sem["xa%d%d" % (r, k)]
+                        g.wait_ge(T.sem["hc%d" % k], n)
+                        sent += _send(g, T, topo, p, en, T["lq%d" % r][:, a:b].bitcast(dt.uint8), T.hq[:, a:b].bitcast(dt.uint8), sem)
+                        g.wait_ge(T.sem["hp%d" % k], n)
+                        sent += _send(g, T, topo, p, en, T["ls%d" % r][:, a:b], T.hs[:, a:b], sem)
+                if sent:
+                    g.wait_ge(T.sem.sent, sent)
 
 
 def rank_program(g, core, T, topo):
@@ -229,395 +225,423 @@ def rank_program(g, core, T, topo):
 
     mate = [T.cores[rank ^ (1 << r)] for r in range(R)]
 
-    def piece(r, k):
-        return (0, CUT[r]) if k == 0 else (CUT[r], C)
+    def keys(name, n):
+        return ["%s%d" % (name, i) for i in range(n)]
+
+    def ahead(k):
+        return CUT[k], max(CUT[k + 1], CUT[k] + 128)
+
+    def behind(k):
+        return min(CUT[k], CUT[k + 1] - 128), CUT[k + 1]
+
+    def xkeys(r, a, b):
+        return ["qx%d%d" % (r, k) for k in range(NS) if CUT[k] < b and a < CUT[k + 1]]
+
+    def landed(r, a, b):
+        return ["lx%d%d" % (r, k) for k, run in enumerate(RUNS[r]) if run[0] < b and a < run[1]]
 
     def ship_u(r):
         order("g", ["urq", "urs"], [])
-        if _far(T, topo, core, r):
-            count["sent"] += _send_u(g, T, topo, _helper(core, topo), _home(T, topo, core, r), T.huq[:], T.hus[:],
-                                     T.urq[:, 0:8], T.urs[:, 0:32], T.sem.hu)
-            arrives("ua%d" % r, len(topo.engines(_helper(mate[r], topo), core)), ["ul%d" % r])
-        else:
-            count["sent"] += _send_u(g, T, topo, mate[r], topo.engines(core, mate[r]), T["ulq%d" % r][:], T["uls%d" % r][:],
-                                     T.urq[:, 0:8], T.urs[:, 0:32], T.sem["ua%d" % r])
-            arrives("ua%d" % r, len(topo.engines(mate[r], core)), ["ul%d" % r])
+        count["sent"] += _send_u(g, T, topo, mate[r], topo.engines(core, mate[r]), T["ulq%d" % r][:], T["uls%d" % r][:],
+                                 T.urq[:, 0:8], T.urs[:, 0:32], T.sem["ua%d" % r])
+        arrives("ua%d" % r, len(topo.engines(mate[r], core)), ["ul%d" % r])
 
-    def ship_x(r, k, between=None):
-        a, b = piece(r, k)
+    def ship(r, k, between=None):
+        a, b, via = RUNS[r][k]
         q, s = T["qx%d" % r], T["sx%d" % r]
-        order("g", ["qx%d%d" % (r, k)], [])
-        far = _far(T, topo, core, r) and k < len(_handed(r))
-        if far:
-            b, z = _handed(r)[k]
-        sem, en = T.sem["xa%d%d" % (r, k)], topo.engines(core, mate[r])
-        count["sent"] += _send(g, T, topo, mate[r], en, raw(T["lq%d" % r][:, a:b]), raw(q[:, a:b]), sem)
+        order("g", xkeys(r, a, b), [])
+        sem = "xa%d%d" % (r, k)
+        if via and _far(T, topo, core, r):
+            h, en = _helper(core, topo), _home(T, topo, core, r)
+            count["sent"] += _send(g, T, topo, h, en, raw(T.hq[:, a:b]), raw(q[:, a:b]), T.sem["hc%d" % k])
+            count["sent"] += _send(g, T, topo, h, en, T.hs[:, a:b], s[:, a:b], T.sem["hp%d" % k])
+            arrives(sem, 2 * len(topo.engines(_helper(mate[r], topo), core)), ["lx%d%d" % (r, k)])
+            return
+        en = topo.engines(core, mate[r])
+        count["sent"] += _send(g, T, topo, mate[r], en, raw(T["lq%d" % r][:, a:b]), raw(q[:, a:b]), T.sem[sem])
         if between:
             between()
-        count["sent"] += _send(g, T, topo, mate[r], en, T["ls%d" % r][:, a:b], s[:, a:b], sem)
-        arrives("xa%d%d" % (r, k), 2 * len(topo.engines(mate[r], core)), ["lx%d%d" % (r, k)])
-        if far:
-            h, en = _helper(core, topo), _home(T, topo, core, r)
-            count["sent"] += _send(g, T, topo, h, en, raw(T.hq[:, b:z]), raw(q[:, b:z]), T.sem["hc%d" % k])
-            count["sent"] += _send(g, T, topo, h, en, T.hs[:, b:z], s[:, b:z], T.sem["hp%d" % k])
-            arrives("xr", 2 * len(_handed(r)) * len(topo.engines(_helper(mate[r], topo), core)), ["lx%d2" % r])
+        count["sent"] += _send(g, T, topo, mate[r], en, T["ls%d" % r][:, a:b], s[:, a:b], T.sem[sem])
+        arrives(sem, 2 * len(topo.engines(mate[r], core)), ["lx%d%d" % (r, k)])
+
+    def ship_piece(r, k):
+        for i, run in enumerate(RUNS[r]):
+            if CUT[k] < run[1] <= CUT[k + 1]:
+                ship(r, i)
 
     def spread_u(r):
         cp(words(T["upq%d" % r][:]), words(T["ulq%d" % r][:]).indirect(T.lu1[:]), ["ul%d" % r, "lu1"], ["upq%d" % r])
         act(T["ups%d" % r][:], T["uls%d" % r][:, 0:8].indirect(T.lu1[:]), ACT.Copy, ["ul%d" % r, "lu1"], ["ups%d" % r])
 
-    def quant_x(r, k, tile, key):
-        a, b = piece(r, k)
-        quant(T["qx%d" % r][:, a:b], T["sx%d" % r][:, a:b], tile[:, 4 * a:4 * b], key, ["qx%d%d" % (r, k)])
+    PL, M0, M1, PA, PB, PM, AM, CD, CY, T1, T2 = [T.col[:, k:k + 1] for k in range(11)]
 
-    PL, PL1, PLH, M0, M1, PF, C8, CB, T1, MC, S0, X1, X2, X3, X4, X5, JC = [T.col[:, k:k + 1] for k in range(17)]
+    def own_mm(r, k):
+        a, b = behind(k)
+        mm(7, b - a, T.urq[:], T.urs[:], T["qx%d" % r][:, a:b], T["sx%d" % r][:, a:b], ["urq", "urs"] + xkeys(r, a, b))
 
-    def span(r, k):
-        return (0, _reach(r)) if k == 0 else (_reach(r), C)
+    def own_row(k):
+        a, b = CUT[k], CUT[k + 1]
+        act(T.ow[:, a:b], bank(7, b - a, a - behind(k)[0]), ACT.Copy, ["ps7"], ["ow%d" % k])
 
-    def own_mm(r, k, b0, b1):
-        a, b = span(r, k)
-        for bb in (b0, b1):
-            mm(bb, b - a, T.urq[:], T.urs[:], T["qx%d" % r][:, a:b], T["sx%d" % r][:, a:b],
-               ["urq", "urs"] + ["qx%d%d" % (r, i) for i in range(k + 1)])
+    def own_windows(s):
+        row = T.ow[:, 0:CUT[s + 1]]
+        act(T.og[:, 64 * s:64 * s + 48], row.indirect(T.lw[:, 4 * s:4 * s + 3]), ACT.Identity,
+            keys("ow", s + 1) + ["lw", "mask"], ["ogb%d" % s], scale=M1)
+        act(T.og[:, 64 * s + 48:64 * s + 64], row.indirect(T.la[:, 2 * s:2 * s + 1]), ACT.Identity,
+            keys("ow", s + 1) + ["la", "mask"], ["oga%d" % s], scale=M0)
 
-    def landed(r, k):
-        return ["lx%d0" % r] if k == 0 else ["lx%d%d" % (r, i) for i in range(3)]
+    def far_mm(r, k, b):
+        a, z = behind(k)
+        mm(b, z - a, T["upq%d" % r][:], T["ups%d" % r][:], T["lq%d" % r][:, a:z], T["ls%d" % r][:, a:z],
+           ["upq%d" % r, "ups%d" % r] + landed(r, a, z))
 
-    def far_mm(r, k, b0, b1):
-        a, b = span(r, k)
-        for bb in (b1, b0):
-            mm(bb, b - a, T["upq%d" % r][:], T["ups%d" % r][:], T["lq%d" % r][:, a:b], T["ls%d" % r][:, a:b],
-               ["upq%d" % r, "ups%d" % r] + landed(r, k))
+    def far_row(k, b, half, q):
+        a, z = CUT[k], CUT[k + 1]
+        out, in_, m = T.pw[:, C * half + a:C * half + z], bank(b, z - a, a - behind(k)[0]), (M0, M1)[half]
+        if q == "v":
+            ts(out, in_, m, None, ALU.mult, None, ["ps%d" % b, "mask"], ["pw%d" % half])
+        else:
+            act(out, in_, ACT.Identity, ["ps%d" % b, "mask"], ["pw%d" % half], scale=m)
 
-    def evac_b(name, r, k, bk, m):
-        a, b = span(r, k)
-        ts(T[name][:, a:b], bank(bk, b - a), m, None, ALU.mult, None, ["ps%d" % bk, "mask"],
-           [name + "b0", name + "b1"] if k == 0 else [name + "b1"])
+    def windows(s):
+        tt(T.ba[:, 64 * s:64 * s + 64], T.pw[:].indirect(T.lw[:, 4 * s:4 * s + 4]), T.og[:, 64 * s:64 * s + 64], ALU.add,
+           ["pw0", "pw1", "lw", "ogb%d" % s, "oga%d" % s], ["ba%d" % s])
 
-    def evac_a(name, r, k, bk, m):
-        a, b = span(r, k)
-        act(T[name][:, C + a:C + b], bank(bk, b - a), ACT.Identity, ["ps%d" % bk, "mask"],
-            [name + "a0", name + "a1"] if k == 0 else [name + "a1"], scale=m)
+    def zero(t, a, z, w):
+        for i in range(a, z, 512):
+            n = min(512, z - i)
+            act(t[:, i:i + n], T.ie[:, 0:n], ACT.Identity, ["ie"], w if i + n == z else [], scale=0.0)
 
-    def cut(name, r, k):
-        n = 3 * FIRST[r]
-        return T[name][:].indirect(T.lw[:, 0:n] if k == 0 else T.lw[:, n:18] if n % 2 == 0 else T.lw3[:, 0:18 - n])
+    def every16(i):
+        ts(T.kd[:, i:C:16], T.ik[:], T.ca[:, i:i + 1], T.cd[:, i:i + 1], ALU.mult, ALU.add, ["ik", "ca", "cdd"], ["kd%d" % i])
 
-    def rows(name):
-        return [name + x for x in ("b0", "a0", "b1", "a1")] + ["lw", "lw3"]
-
-    def cols(name, r, k):
-        return T[name][:, 0:48 * FIRST[r]] if k == 0 else T[name][:, 48 * FIRST[r]:288]
-
-    def chunks(name, r, k):
-        return [name + "%d" % i for i in (range(FIRST[r]) if k == 0 else range(FIRST[r], 6))]
-
-    def own_windows(r, k):
-        act(cols("og", r, k), cut("ow", r, k), ACT.Copy, rows("ow"), chunks("og", r, k))
-
-    def windows(r, k):
-        tt(cols("ba", r, k), cut("pw", r, k), cols("og", r, k), ALU.add, rows("pw") + chunks("og", r, k), chunks("ba", r, k))
-
+    dma("a", [], ["x00"], T.x0[:, 0:4 * CUT[1]], T.x[:, 0:4 * CUT[1]])
     dma("s", [], ["ut"], T.ut[:], T.u[:])
-    dma("a", [], ["x00"], T.x0[:, 0:4 * CUT[0]], T.x[:, 0:4 * CUT[0]])
-    dma("s", [], ["x01"], T.x0[:, 4 * CUT[0]:4 * C], T.x[:, 4 * CUT[0]:4 * C])
-    iota("pi", T.pi[:], [[0, 24]], 0, 1)
-    iota("iw", T.iw[:], [[64, 6], [-16, 3]], 0, 0)
+    dma("s", [], ["x01"], T.x0[:, 4 * CUT[1]:4 * C], T.x[:, 4 * CUT[1]:4 * C])
+    iota("pi", T.pi[:], [[0, 8]], 0, 1)
+    iota("iw", T.iw[:], [[128, 3], [16, 4]], 0, 1)
+    iota("ik", T.ik[:], [[1, 24]], 0, 0)
     iota("ie", T.ie[:], [[1, 512]], 0, -4)
     iota("ic", T.ic[:], [[1, 8], [0, 16]], 0, 0)
-    ts(T.pb[:], T.pi[:, 0:8], 7, None, ALU.bitwise_and, None, ["pi"], ["pb"])
+    iota("im", T.im[:], [[16, SG]], 0, 0)
+    iota("iy", T.iy[:], [[4, 96]], 0, 0)
+    fill(T.rst[:], 0.0, ["rst"])
+    fill(T.crow[:], 1.0, ["crow"])
+    fill(T.dd[:, 0:48 * SG:SG], BIG, ["fill"])
+    ts(T.pb[:], T.pi[:], 7, None, ALU.bitwise_and, None, ["pi"], ["pb"])
     ts(T.pa[:], T.pi[:], 15, None, ALU.bitwise_and, None, ["pi"], ["pa"])
-    cp(PF, T.pi[:, 0:1], ["pi"], ["pf"])
+    ts(T.pc[:], T.pi[:], 3, None, ALU.bitwise_and, None, ["pi"], ["pc"])
+    ts(T.pd[:], T.pi[:], 2, 3, ALU.arith_shift_right, ALU.bitwise_and, ["pi"], ["pd"])
     ts(T.lu16[:], T.pb[:], 16.0, None, ALU.mult, None, ["pb"], ["lu16"])
     cp(PL, T.pa[:, 0:1], ["pa"], ["pl"])
     cp(T.lu1[:], T.pb[:], ["pb"], ["lu1"])
-    cp(T.lrep[:], T.pa[:], ["pa"], ["lrep"])
-    ts(C8, PF, PL, 0.5, ALU.subtract, ALU.mult, ["pf", "pl"], ["c8"])
+    cp(PB, T.pc[:, 0:1], ["pc"], ["pbc"])
+    cp(PA, T.pd[:, 0:1], ["pd"], ["pac"])
+    ts(T.iw[:, 3:12:4], T.iw[:, 3:12:4], -32.0, None, ALU.add, None, ["iw"], ["iw"])
     ts(M0, PL, 8.0, None, ALU.is_lt, None, ["pl"], ["m0"])
-    ts(T1, PL, 2.0, 1.0, ALU.mult, ALU.add, ["pl"], ["t1"])
+    fill(T.rst[:, 0:ST * SG:SG], BIG, ["rst"])
+    ts(T.wb[:], T.iw[:], float(C), -float(C), ALU.is_ge, ALU.mult, ["iw"], ["wb"])
     ts(M1, PL, 8.0, None, ALU.is_ge, None, ["pl", "m0"], ["mask"])
-    ts(CB, C8, PL, 39.0, ALU.subtract, ALU.add, ["c8", "pl"], ["cb8"])
-    ts(S0, C8, PL, float(V), ALU.add, ALU.add, ["c8", "pl"], ["s0"])
-    ts(T1, T1, M1, None, ALU.mult, None, ["t1", "mask"], ["t1"])
-    ts(T.wa[:, 0:9], T.iw[:, 0:9], CB, None, ALU.add, None, ["iw", "cb8"], ["wa0"])
-    ts(T.wa[:, 9:12], T.iw[:, 15:18], CB, None, ALU.add, None, ["iw", "cb8"], ["wa1"])
-    ts(T.wa[:, 12:18], T.iw[:, 9:15], CB, None, ALU.add, None, ["iw", "cb8"], ["wa2"])
-    ts(MC, M1, float(C), None, ALU.mult, None, ["mask"], ["mc"])
-    ts(T.wa[:, 2:18:3], T.wa[:, 2:18:3], T1, None, ALU.add, None, ["wa0", "wa1", "wa2", "t1"], ["wa0", "wa1", "wa2"])
-    ts(T.sa[:, 0:1], M1, 56.0, S0, ALU.mult, ALU.add, ["mask", "s0"], ["sa0"])
-    ts(T.wb[:], T.wa[:], float(C), -float(C), ALU.is_ge, ALU.mult, ["wa0"], ["wb"])
-    ts(T.sa[:, 1:2], M1, 184.0, S0, ALU.mult, ALU.add, ["mask", "s0"], ["sa1"])
-    tt(T.wd[:], T.wa[:], T.wb[:], ALU.add, ["wa0", "wb"], ["wd"])
-    ts(X1, PF, 64.0, M1, ALU.is_ge, ALU.mult, ["pf", "mask"], ["x1"])
-    ts(T.wd[:, 2:18:3], T.wd[:, 2:18:3], MC, None, ALU.add, None, ["wd", "mc"], ["wd"])
-    ts(X3, PF, 96.0, float(C), ALU.is_ge, ALU.mult, ["pf"], ["x3"])
+    fill(T.crow[:, 0:ST * SG:SG], -17.0, ["crow"])
+    tt(T.wd[:], T.iw[:], T.wb[:], ALU.add, ["iw", "wb"], ["wd"])
+    ts(T1, PL, 0.0, 16.0, ALU.is_equal, ALU.mult, ["pl"], ["t1"])
+    ts(T2, PA, 0.0, 4.0, ALU.is_equal, ALU.mult, ["pac"], ["t2"])
     cp(T.lw[:], T.wd[:], ["wd"], ["lw"])
-    cp(T.lw3[:, 0:9], T.wd[:, 9:18], ["wd"], ["lw3"])
+    cp(T.la[:, 0:6:2], T.wd[:, 3:12:4], ["wd"], ["la"])
+    ts(T.lsc[:, 0:3], T.wd[:, 3:12:4], 4.0, None, ALU.mult, None, ["wd"], ["lsc"])
+    ts(T.lw[:, 3:12:4], T.wd[:, 3:12:4], float(C), None, ALU.add, None, ["wd"], ["lw"])
+    ts(PM, PL, T1, -1.0, ALU.add, ALU.add, ["pl", "t1"], ["pm"])
+    ts(AM, PA, T2, -1.0, ALU.add, ALU.add, ["pac", "t2"], ["am"])
+    ts(CD, T1, 64.0, -64.0, ALU.mult, ALU.add, ["t1"], ["cd"])
+    ts(CY, T2, 224.0, PB, ALU.mult, ALU.add, ["t2", "pbc"], ["cy0"])
+    ts(T.ca[:], T.ik[:, 0:16], PL, None, ALU.is_equal, None, ["ik", "pl"], ["ca"])
+    ts(T.cb[:], T.ik[:, 0:16], PM, -1024.0, ALU.is_equal, ALU.mult, ["ik", "pm"], ["cb"])
+    ts(T.ya[:], T.ik[:, 0:4], PA, None, ALU.is_equal, None, ["ik", "pac"], ["ya"])
+    ts(T.yb[:], T.ik[:, 0:4], AM, -224.0, ALU.is_equal, ALU.mult, ["ik", "am"], ["yb"])
+    ts(T1, PL, 80.0, None, ALU.add, None, ["pl"], ["t1"])
+    ts(T2, PA, 32.0, None, ALU.add, None, ["pac"], ["t2"])
+    ts(T.ik[:], T.ik[:], 16.0, None, ALU.mult, None, ["ik"], ["ik"])
+    ts(CY, CY, -64.0, None, ALU.add, None, ["cy0"], ["cy"])
+    ts(T.cc[:], T.ca[:], T1, None, ALU.mult, None, ["ca", "t1"], ["cc"])
+    ts(T.yc[:], T.ya[:], T2, None, ALU.mult, None, ["ya", "t2"], ["yc"])
+    zero(T.pw, 0, 2 * C, ["pw0", "pw1"])
+    zero(T.ct, 0, 1024, ["ct0", "ct1"])
+    quant(T.qx0[:, 0:CUT[1]], T.sx0[:, 0:CUT[1]], T.x0[:, 0:4 * CUT[1]], ["x00"], ["qx00"])
     quant(T.uq[:], T.us[:], T.ut[:], ["ut"], ["uq"])
-    quant_x(0, 0, T.x0, ["x00"])
+    tt(T.cd[:], T.cc[:], T.cb[:], ALU.add, ["cc", "cb"], ["cdd"])
+    tt(T.yd[:], T.yc[:], T.yb[:], ALU.add, ["yc", "yb"], ["yd"])
     cp(words(T.urq[:]), words(T.uq[:]).indirect(T.lu16[:]), ["uq", "lu16"], ["urq"])
     act(T.urs[:], T.us[:].indirect(T.lu16[:]), ACT.Copy, ["uq", "lu16"], ["urs"])
-    ship_x(0, 0, lambda: ship_u(0))
-    quant_x(0, 1, T.x0, ["x01"])
-    ship_x(0, 1)
-    iota("im", T.im[:], [[16, 18]], 0, 0)
-    iota("ij", T.ij[:], [[16, 24]], V, 0)
-    iota("ik", T.ik[:], [[1, 16]], 0, 0)
+    ship(0, 0, lambda: ship_u(0))
+    for i in range(8):
+        every16(i)
+    quant(T.qx0[:, CUT[1]:C], T.sx0[:, CUT[1]:C], T.x0[:, 4 * CUT[1]:4 * C], ["x01"], ["qx01", "qx02"])
+    ship(0, 1)
     ship_u(1)
     ship_u(2)
-    dma("s", [], ["wq"], raw(T.wq[:]), T.wc[:])
+    dma("s", ["ul0"], ["wq"], raw(T.wq[:]), T.wc[:])
     dma("s", [], ["wp"], T.wp[:], T.ws[:])
     dma("s", [], ["vt"], T.vt[:], T.v[:])
-    own_mm(0, 0, 6, 7)
-    own_mm(0, 1, 4, 5)
-    tiles = ["et0", "et1", "et2", "et3"]
+    for k in range(NS):
+        own_mm(0, k)
+        own_row(k)
+        own_windows(k)
+    zero(T.mt, 0, 4 * C, ["mt"])
+    zero(T.x1, 4 * C, 4 * XW, ["x1z"])
+    zero(T.yt, 4 * C, 4 * XW, ["ytz"])
+    tiles = keys("et", 4)
+    ts(T.ma[:], T.im[:], PL, None, ALU.add, None, ["im", "pl"], ["ma"])
     for b in range(4):
         ts(T.et[:, 512 * b:512 * (b + 1)], T.ie[:], float(b), None, ALU.is_equal, None, ["ie"], ["et%d" % b])
-        if b < 2:
-            evac_b("ow", 0, b, 6 - 2 * b, M1)
-            evac_a("ow", 0, b, 7 - 2 * b, M0)
-    own_windows(0, 0)
-    own_windows(0, 1)
-    act(T.pw[:], T.et[:, 0:2 * C], ACT.Identity, tiles, ["pwb0", "pwa0", "pwb1", "pwa1"], scale=0.0)
-    act(T.ct[:], T.et[:, 0:4 * C], ACT.Identity, tiles, ["ct0", "ct1", "ct2"], scale=0.0)
-    fill(T.rst[:], 0.0, ["rst"])
-    fill(T.crow[:], 1.0, ["crow"])
-    fill(T.dd[:, 0:48 * SG:SG], 1e29, ["fill"])
-    fill(T.rst[:, 0:CH * SG:SG], 1e29, ["rst"])
-    fill(T.crow[:, NO:2 * CH * SG:SG], -float(V), ["crow"])
-    fill(T.mt[:], 0.0, ["mt"])
-    ts(T.sb[:, 0:1], T.sa[:, 1:2], 128.0, None, ALU.add, None, ["sa1"], ["sb"])
-    ts(X2, C8, -456.0, X1, ALU.add, ALU.mult, ["c8", "x1"], ["x2"])
-    ts(T.sd[:, 0:1], T.sb[:, 0:1], float(C), -float(C), ALU.is_ge, ALU.mult, ["sb"], ["sd"])
-    ts(X4, X3, M1, X2, ALU.mult, ALU.add, ["x3", "x2", "mask"], ["x4"])
-    ts(T.sb[:, 1:2], T.sb[:, 0:1], T.sd[:, 0:1], None, ALU.add, None, ["sb", "sd"], ["sb1"])
-    ts(X5, X4, PL, float(XW), ALU.add, ALU.add, ["x4", "pl"], ["x5"])
-    ts(T.lsc[:, 0:1], T.sa[:, 0:1], float(V), 4.0, ALU.add, ALU.mult, ["sa0"], ["lsc0"])
-    ts(T.lsc[:, 1:2], T.sb[:, 1:2], float(V), 4.0, ALU.add, ALU.mult, ["sb1"], ["lsc2"])
-    ts(T.lsc[:, 2:3], T.sa[:, 0:1], float(V + 192), 4.0, ALU.add, ALU.mult, ["sa0"], ["lsc3"])
-    ts(T.lsc[:, 4:5], X5, 4.0, None, ALU.mult, None, ["x5"], ["lsc1"])
-    ts(PLH, PL, -16.5, None, ALU.add, None, ["pl"], ["plh"])
-    ts(PL1, PL, 1.0, None, ALU.add, None, ["pl"], ["pl1"])
-    ts(JC, PL, 15.0, -64.0, ALU.is_lt, ALU.mult, ["pl"], ["jc"])
+        if b == 0:
+            ts(T.ma[:], T.ma[:], -16.5, 1.0 / SG, ALU.add, ALU.mult, ["ma"], ["ma"])
+        if b == 1:
+            cp(T.mb[:], T.ma[:], ["ma"], ["mb"])
+    ts(T.lm[:], T.mb[:], float(SG), float(NO), ALU.mult, ALU.add, ["mb"], ["lm"])
+    ts(T.ct[:, 0:512:4], T.ic[:], 8.0, PL, ALU.add, ALU.is_equal, ["ic", "pl"], ["ct0"])
+    ts(T.ct[:, 512:1024:4], T.ic[:], PL, None, ALU.is_equal, None, ["ic", "pl"], ["ct1"])
     quant(T.eq[:], T.es[:], T.et[:], tiles, ["eq"])
+    quant(T.cq[:], T.cs[:], T.ct[:], ["ct0", "ct1"], ["cq"])
+    for i in range(8, 16):
+        every16(i)
     spread_u(0)
 
-    def late_constants():
-        ts(T.ma[:], T.im[:], PLH, 1.0 / SG, ALU.add, ALU.mult, ["im", "plh"], ["ma"])
-        ts(T.ct[:, 0:512:4], T.ic[:], 8.0, PL, ALU.add, ALU.is_equal, ["ic", "pl"], ["ct0"])
-        cp(T.mb[:], T.ma[:], ["ma"], ["mb"])
-        ts(T.ct[:, 512:1024:4], T.ic[:], PL, None, ALU.is_equal, None, ["ic", "pl"], ["ct1"])
-        ts(T.lm[:], T.mb[:], float(SG), float(NO), ALU.mult, ALU.add, ["mb"], ["lm"])
-        ts(T.ct[:, 1024:1536:4], T.ic[:], PL, -1.0, ALU.is_equal, ALU.mult, ["ic", "pl"], ["ct2"])
+    def late():
+        for k in range(1, NS):
+            a, z = CUT[k] // 4, CUT[k + 1] // 4
+            ts(T.iy[:, a:z], T.iy[:, a:z], -float(CUT[k]), None, ALU.add, None, ["iy"], ["iy%d" % k])
+        for i in range(4):
+            ts(T.ky[:, i:C:4], T.iy[:], T.ya[:, i:i + 1], T.yd[:, i:i + 1], ALU.mult, ALU.add, ["iy", "iy1", "iy2", "ya", "yd"], ["ky%d" % i])
 
-    def last_constants():
-        ts(T.ca[:], T.ik[:], PL, -1000.0, ALU.is_equal, ALU.mult, ["ik", "pl"], ["ca"])
-        ts(T.cb[:], T.ik[:], PL1, 64.0, ALU.is_equal, ALU.mult, ["ik", "pl1"], ["cb"])
-        ts(T.jt[:], T.ij[:], JC, PL, ALU.add, ALU.add, ["ij", "jc", "pl"], ["jt"])
-        tt(T.c16[:], T.ca[:], T.cb[:], ALU.add, ["ca", "cb"], ["c16"])
-        quant(T.cq[:], T.cs[:], T.ct[:], ["ct0", "ct1", "ct2"], ["cq"])
+    def diffs(a, b):
+        for n in range(a, b):
+            s, q = divmod(n, ST)
+            o = 64 * s
+            act(T.dd[:, SG * n + 1:SG * n + SG], T.ba[:, o + q:o + q + NO], ACT.Abs, ["ba%d" % s], ["dd%d" % n],
+                bias=T.ba[:, o + 48 + q:o + 49 + q], scale=-1.0)
 
-    def diffs(k):
-        for q in range(CH):
-            s, o = CH * k + q, 48 * k
-            act(T.dd[:, SG * s + 1:SG * s + SG], T.ba[:, o + 7 - q:o + 40 - q], ACT.Abs, ["ba%d" % k], ["dd%d" % s],
-                bias=T.ba[:, o + 40 + q:o + 41 + q], scale=-1.0)
+    def slots(name, a, b):
+        return ["%s%d" % (name, n) for n in range(a, b)]
 
-    def made(k):
-        return ["fill"] + ["dd%d" % s for s in range(CH * k, CH * k + CH)]
+    def least(a, b):
+        scan(T.pm[:, SG * a:SG * b], T.rst[:, 0:SG * (b - a)], T.dd[:, SG * a:SG * b], 0.0, ALU.add, ALU.min,
+             ["rst", "fill"] + slots("dd", a, b), slots("pm", a, b))
 
-    def least(k):
-        a, b = CH * SG * k, CH * SG * (k + 1)
-        scan(T.pm[:, a:b], T.rst[:], T.dd[:, a:b], 0.0, ALU.add, ALU.min, ["rst"] + made(k), ["pm%d" % k])
+    def above(a, b):
+        w = 8 if b - a <= 8 else ST
+        c = (w - b + a) * SG // 32 * 2
+        lo = SG * (b - w) + 16 * c
+        tt(T.gt[:, lo + b * 8:SG * b + b * 8], T.pm[:, SG * (b - w):SG * b].indirect(T.lm[:, c:w * SG // 16]), T.dd[:, lo:SG * b],
+           ALU.not_equal, slots("pm", b - w, b) + slots("dd", b - w, b) + ["lm", "fill"], ["gt%d" % b])
 
-    def above(k):
-        a, b = CH * SG * k, CH * SG * (k + 1)
-        if PICK:
-            tt(T.nq[:, a:b], T.pm[:, a:b].indirect(T.lm[:, 0:CH * SG // 16]), T.dd[:, a:b], ALU.not_equal,
-               ["pm%d" % k, "lm"] + made(k), ["nq%d" % k])
-        else:
-            tt(T.nq[:, a:b], T.pm[:, a:b], T.dd[:, a:b], ALU.not_equal, ["pm%d" % k] + made(k), ["nq%d" % k])
+    def back(t, a, b):
+        return t[:, b - 1:a - 1:-1] if a else t[:, b - 1::-1]
 
-    def run(k0, k1):
-        a, b = CH * SG * k0, CH * SG * k1
-        scan(T.cnt[:, a:b], T.nq[:, a:b], T.crow[:, 0:b - a], 0.0, ALU.mult, ALU.add,
-             ["crow"] + ["nq%d" % k for k in range(k0, k1)], ["cnt%d" % k for k in range(k0, k1)])
+    def tally(a, b):
+        scan(back(T.cnt, SG * a, SG * b), back(T.gt, SG * a + b * 8, SG * b + b * 8), back(T.crow, 0, SG * (b - a)), 0.0,
+             ALU.mult, ALU.add, ["crow", "gt%d" % b], slots("cnt", a, b))
 
-    def sixteenth(ex, row, key):
-        scan(T[ex][:], T.cx[:], row, 0.0, ALU.add, ALU.max, ["cx", key], [ex])
+    def signs(a, b):
+        for n in range(a, b):
+            act(T.sj[:, SG * n + 1:SG * n + SG], T.pm[:, SG * n + 1:SG * n + SG], ACT.Sign, ["pm%d" % n], ["acc%d" % n],
+                bias=T.pm[:, SG * n + NO:SG * n + SG], scale=-1.0, accum_out=T.acc[:, n:n + 1])
 
-    def place(kf, ex):
-        tt(T[kf][:], T[ex][:, 15:C:16], T.jt[:], ALU.add, [ex, "jt"], [kf])
+    def counted(a, b):
+        act(T.cnt[:, SG * a:SG * b:SG], T.acc[:, a:b], ACT.Identity, slots("acc", a, b), slots("cnt", a, b),
+            bias=-float(V), scale=-1.0)
 
-    def offsets(off, kf):
-        cp(T[off][:], T[kf][:], [kf], [off])
-
-    def unpack(q, s, keys):
+    def unpack(q, s, r):
         for b in range(4):
-            mm(b, C, T.eq[:, 128 * b:128 * b + 128], T.es[:, 128 * b:128 * b + 128], q[:], s[:], ["eq"] + keys)
+            mm(b, C, T.eq[:, 128 * b:128 * b + 128], T.es[:, 128 * b:128 * b + 128], q[:, 0:C], s[:, 0:C], ["eq"] + r)
 
     def evac_p(b):
-        o = XW * b
-        act(T.pp[:, o + V:o + V + C], bank(b, C), ACT.Identity, ["ps%d" % b], ["ppm%d" % b], scale=0.5)
-        act(T.pp[:, o:o + V], bank(b, V, C - V), ACT.Identity, ["ps%d" % b], ["ppa%d" % b], scale=0.5)
-        act(T.pp[:, o + V + C:o + XW], bank(b, V), ACT.Identity, ["ps%d" % b], ["ppz%d" % b], scale=0.5)
+        act(T.pp[:, 4 * V + b:4 * (V + C):4], bank(b, C), ACT.Identity, ["ps%d" % b], ["pp%d" % b], scale=0.5)
 
-    def plane(b):
-        return ["ppm%d" % b, "ppa%d" % b, "ppz%d" % b]
+    def pick(row, ex, key):
+        scan(T[ex][:], row, T.ky[:], -224.0, ALU.max, ALU.add, keys("ky", 4) + [key], [ex])
 
-    def take_h(r, k, b):
-        a, z = piece(r, k)
-        act(T.gh[:, C * b + a:C * b + z], T.pp[:, XW * b:XW * (b + 1)].indirect(T.fh[:, a // 16:z // 16]),
-            ACT.Copy, plane(b) + ["fh"], ["gh%d%d" % (k, b)])
+    def offsets(off, ex):
+        ts(T[off][:], T[ex][:, 3:C:4], 4.0, CY, ALU.mult, ALU.add, [ex, "cy"], [off])
 
-    def take_l(r, k, b):
-        a, z = piece(r, k)
-        tt(T.yt[:, 4 * a + b:4 * z:4], T.pp[:, XW * b:XW * (b + 1)].indirect(T.fl[:, a // 16:z // 16]),
-           T.gh[:, C * b + a:C * b + z], ALU.add, plane(b) + ["fl", "gh%d%d" % (k, b)], ["yt%d%d" % (k, b)])
+    parts = [(0, 0, SUB), (0, SUB, CUT[1]), (1, CUT[1], CUT[2]), (2, CUT[2], CUT[3])]
+    plane = keys("pp", 4) + ["ppa", "ppz"]
 
-    def quant_y(r, k):
-        a, z = piece(r, k)
-        quant(T.yq[:, a:z], T.ys[:, a:z], T.yt[:, 4 * a:4 * z], ["yt%d%d" % (k, i) for i in range(4)], ["yq%d" % k])
+    def source(i, off):
+        k, a, z = parts[i]
+        return T.pp[:, 4 * CUT[k]:4 * (CUT[k + 1] + 2 * V)].indirect(T[off][:, a // 4:z // 4])
 
-    def layer(r, k, b):
-        a, z = piece(r, k)
-        mm(4 + b, z - a, T.wq[:, 128 * b:128 * b + 128], T.wp[:, 128 * b:128 * b + 128], T.yq[:, a:z], T.ys[:, a:z],
-           ["wq", "wp", "yq%d" % k])
+    def take_h(i):
+        k, a, z = parts[i]
+        act(T.gh[:, 4 * a:4 * z], source(i, "fh"), ACT.Copy, plane + ["fh"], ["gh%d" % i])
 
-    def relu(r, k, b):
-        a, z = piece(r, k)
-        act(T.rb[:, C * b + a:C * b + z], bank(4 + b, z - a), ACT.Relu, ["ps%d" % (4 + b)], ["rb%d%d" % (k, b)], scale=0.03125)
+    def take_l(i):
+        k, a, z = parts[i]
+        tt(T.yt[:, 4 * a:4 * z], source(i, "fl"), T.gh[:, 4 * a:4 * z], ALU.add, plane + ["fl", "gh%d" % i], ["yt%d" % i])
 
-    def add(r, k, b):
-        a, z = piece(r, k)
-        tt(T.x1[:, 4 * a + b:4 * z:4], T.rb[:, C * b + a:C * b + z], bank(b, z - a, a), ALU.add,
-           ["rb%d%d" % (k, b), "ps%d" % b], ["x1%d%d" % (k, b)])
+    def quant_y(k):
+        a, z = ahead(k)
+        quant(T.yq[:, a:z], T.ys[:, a:z], T.yt[:, 4 * a:4 * z], ["ytz"] + ["yt%d" % i for i in range(4) if parts[i][0] == k], ["yq%d" % k])
 
-    def store(k, bk):
-        a, z = piece(R, k)
-        key = "qx%d%d" % (R, k)
-        mm(bk, z - a, T.vq[:], T.vs[:], T["qx%d" % R][:, a:z], T["sx%d" % R][:, a:z], ["vq", key])
-        put("s", [key], T.oc[:, 4 * a:4 * z], raw(T["qx%d" % R][:, a:z]))
-        for i in range(4):
-            put("s", [key], T.osc[4 * i:4 * i + 4, a:z], T["sx%d" % R][32 * i:32 * i + 4, a:z])
+    def layers(k):
+        a, z = ahead(k)
+        for b in range(4):
+            mm(7 - b, z - a, T.wq[:, 128 * b:128 * b + 128], T.wp[:, 128 * b:128 * b + 128], T.yq[:, a:z], T.ys[:, a:z],
+               ["wq", "wp", "yq%d" % k])
 
-    def store_y(k, bk):
-        a, z = piece(R, k)
-        act(T.yo[:, a:z], bank(bk, z - a), ACT.Copy, ["ps%d" % bk], ["yo%d" % k])
-        put("a", ["yo%d" % k], T.y[:, a:z], T.yo[:, a:z])
+    def relus(k, b0, b1):
+        a, z = CUT[k], CUT[k + 1]
+        for b in range(b0, b1):
+            act(T.rb[:, C * b + a:C * b + z], bank(7 - b, z - a), ACT.Relu, ["ps%d" % (7 - b)], ["rb%d%d" % (k, b)], scale=0.03125)
+
+    def adds(k, b0, b1):
+        a, z = CUT[k], CUT[k + 1]
+        for b in range(b0, b1):
+            tt(T.x1[:, 4 * a + b:4 * z:4], T.rb[:, C * b + a:C * b + z], bank(b, z - a, a), ALU.add,
+               ["rb%d%d" % (k, b), "ps%d" % b], ["x1%d%d" % (k, b)])
+
+    def quant_x(r, k):
+        a, z = ahead(k)
+        quant(T["qx%d" % r][:, a:z], T["sx%d" % r][:, a:z], T.x1[:, 4 * a:4 * z], ["x1z"] + keys("x1%d" % k, 4), ["qx%d%d" % (r, k)])
+
+    def onward(r, k):
+        if r < R:
+            ship_piece(r, k)
+            return
+        a, z = CUT[k], CUT[k + 1]
+        q, s = T["qx%d" % R], T["sx%d" % R]
+        put("s", xkeys(R, a, z), T.oc[:, 4 * a:4 * z], raw(q[:, a:z]))
+        if k == NS - 1:
+            for i in range(4):
+                put("sa"[i // 2], xkeys(R, 0, C), T.osc[4 * i:4 * i + 4, :], s[32 * i:32 * i + 4, 0:C])
+
+    def scores(r, k):
+        if r < R:
+            own_mm(r, k)
+        else:
+            a, z = behind(k)
+            mm(7, z - a, T.vq[:], T.vs[:], T["qx%d" % R][:, a:z], T["sx%d" % R][:, a:z], ["vq"] + xkeys(R, a, z))
+
+    def rows(r, k):
+        if r < R:
+            own_row(k)
+            own_windows(k)
+            return
+        a, z = CUT[k], CUT[k + 1]
+        act(T.yo[:, a:z], bank(7, z - a, a - behind(k)[0]), ACT.Copy, ["ps7"], ["yo%d" % k])
+        put("a" if k == NS - 1 else "s", ["yo%d" % k], T.y[:, a:z], T.yo[:, a:z])
 
     for r in range(R):
-        far_mm(r, 0, 4, 5)
-        evac_b("pw", r, 0, 4, M0)
-        evac_a("pw", r, 0, 5, M1)
-        windows(r, 0)
-        far_mm(r, 1, 6, 7)
-        if r == 0:
-            late_constants()
-            evac_b("pw", r, 1, 6, M0)
-        for k in range(6):
-            diffs(k)
-            if k == REST[r]:
-                if r > 0:
-                    evac_b("pw", r, 1, 6, M0)
-                evac_a("pw", r, 1, 7, M1)
-            least(k)
-            if k == REST[r]:
-                windows(r, 1)
-                unpack(T["lq%d" % r], T["ls%d" % r], landed(r, 1))
-            if k in (2, 4):
-                run(k - 2, k)
-            if k == 5:
-                run(4, 5)
-            above(k)
-            if k == 0 and r == 0:
-                last_constants()
-            if k == 4:
-                cp(T.mt[:].indirect(T.lsc[:, 4:5]), T.cnt[:, 16 * SG + NO:32 * SG:SG], ["cnt2", "cnt3", "lsc1"], ["mt"])
-        run(5, 6)
-        for b in range(3):
+        far_mm(r, 0, 4)
+        far_mm(r, 0, 5)
+        far_row(0, 4, 0, "v")
+        far_row(0, 5, 1, "a")
+        windows(0)
+        if r > 0:
+            rows(r, NS - 1)
+        else:
+            late()
+        for s in range(NS - 1):
+            a, m, z = ST * s, ST * s + SC[s], ST * (s + 1)
+            diffs(a, m)
+            least(a, m)
+            far_mm(r, s + 1, 5 + s)
+            far_row(s + 1, 5 + s, 0, "v")
+            far_row(s + 1, 5 + s, 1, "v")
+            if s > 0:
+                tally(ST * (s - 1) + SC[s - 1], a)
+            windows(s + 1)
+            diffs(m, m + 3)
+            if s > 0:
+                counted(ST * (s - 1), ST * (s - 1) + SC[s - 1])
+            diffs(m + 3, z)
+            least(m, z)
+            signs(a, m)
+            above(m, z)
+        a, m, e, z = 32, 36, 44, 48
+        diffs(a, a + 3)
+        counted(ST, ST + SC[1])
+        diffs(a + 3, m)
+        tally(ST + SC[1], a)
+        least(a, m)
+        diffs(m, e)
+        least(m, e)
+        diffs(e, z)
+        above(a, m)
+        least(e, z)
+        signs(m, e)
+        unpack(T["lq%d" % r], T["ls%d" % r], landed(r, 0, C))
+        tally(a, m)
+        above(e, z)
+        evac_p(0)
+        counted(m, e)
+        tally(e, z)
+        for b in range(1, 3):
             evac_p(b)
-        cp(T.mt[:].indirect(T.lsc[:, 0:3]), T.cnt[:, NO:48 * SG:SG], ["cnt%d" % k for k in range(6)] + ["lsc0", "lsc2", "lsc3"], ["mt"])
-        quant(T.mq[:], T.ms[:], T.mt[:, 0:4 * XW], ["mt"], ["mq"])
-        mm(4, XW, T.cq[:, 0:128], T.cs[:, 0:128], T.mq[:], T.ms[:], ["cq", "mq"])
-        mm(5, C, T.cq[:, 128:256], T.cs[:, 128:256], T.mq[:, V:V + C], T.ms[:, V:V + C], ["cq", "mq"])
-        mm(6, C, T.cq[:, 256:384], T.cs[:, 256:384], T.mq[:, V:V + C], T.ms[:, V:V + C], ["cq", "mq"])
-        if r == 0:
-            cp(T.cx[:], T.c16[:].indirect(T.lrep[:]), ["c16", "lrep"], ["cx"])
-        elif r == 1:
+        cp(T.mt[:].indirect(T.lsc[:, 0:3]), T.cnt[:, 0:48 * SG:SG], slots("cnt", 0, 48) + ["lsc"], ["mt"])
+        quant(T.mq[:], T.ms[:], T.mt[:], ["mt"], ["mq"])
+        mm(5, C, T.cq[:, 128:256], T.cs[:, 128:256], T.mq[:], T.ms[:], ["cq", "mq"])
+        mm(4, C, T.cq[:, 0:128], T.cs[:, 0:128], T.mq[:], T.ms[:], ["cq", "mq"])
+        if r + 1 < R:
+            spread_u(r + 1)
+        else:
             quant(T.vq[:], T.vs[:], T.vt[:], ["vt"], ["vq"])
-        act(T.dpx[:], bank(4, XW), ACT.Copy, ["ps4"], ["dpx"])
-        act(T.nd[:], bank(6, C), ACT.Copy, ["ps6"], ["nd"])
-        sixteenth("exd", bank(5, C), "ps5")
-        place("kd", "exd")
-        offsets("fd", "kd")
+        scan(T.exd[:], bank(5, C), T.kd[:], -1024.0, ALU.max, ALU.add, keys("kd", 16) + ["ps5"], ["exd"])
+        act(T.dpx[:, V:V + C], bank(4, C), ACT.Copy, ["ps4"], ["dpm"])
+        act(T.dpx[:, 0:V], bank(4, V, C - V), ACT.Copy, ["ps4"], ["dpa"])
+        act(T.dpx[:, V + C:XW], bank(4, V), ACT.Copy, ["ps4"], ["dpz"])
+        ts(T.nd[:], bank(5, C), -1.0, None, ALU.mult, None, ["ps5"], ["nd"])
+        ts(T.fd[:], T.exd[:, 15:C:16], CD, None, ALU.add, None, ["exd", "cd"], ["fd"])
         evac_p(3)
-        unpack(T["qx%d" % r], T["sx%d" % r], ["qx%d0" % r, "qx%d1" % r])
-        tt(T.ok[:], T.dpx[:].indirect(T.fd[:]), T.nd[:], ALU.is_equal, ["dpx", "fd", "nd"], ["ok"])
+        unpack(T["qx%d" % r], T["sx%d" % r], xkeys(r, 0, C))
+        tt(T.ok[:], T.dpx[:].indirect(T.fd[:]), T.nd[:], ALU.is_equal, ["dpm", "dpa", "dpz", "fd", "nd"], ["ok"])
+        act(T.pp[:, 0:4 * V], T.pp[:, 4 * C:4 * (C + V)], ACT.Copy, keys("pp", 4), ["ppa"])
         act(T.nok[:], T.ok[:], ACT.Identity, ["ok"], ["nok"], bias=1.0, scale=-1.0)
+        act(T.pp[:, 4 * (C + V):4 * XW], T.pp[:, 4 * V:8 * V], ACT.Copy, keys("pp", 4), ["ppz"])
         tt(T.okd[:], T.ok[:], bank(5, C), ALU.mult, ["ok", "ps5"], ["okd"])
         scan(T.l1[:], T.nok[:], T.okd[:], 0.0, ALU.mult, ALU.add, ["nok", "okd"], ["l1"])
         scan(T.lh[:, 2 * C - 1:C - 1:-1], T.nok[:, ::-1], T.okd[:, ::-1], T.l1[:, C - 1:C], ALU.mult, ALU.add, ["nok", "okd", "l1"], ["h"])
-        sixteenth("exh", T.lh[:, C:2 * C], "h")
-        place("kh", "exh")
+        pick(T.lh[:, C:2 * C], "exh", "h")
         scan(T.lh[:, 0:C], T.nok[:], T.okd[:], T.lh[:, C:C + 1], ALU.mult, ALU.add, ["nok", "okd", "h"], ["l"])
-        offsets("fh", "kh")
-        sixteenth("exl", T.lh[:, 0:C], "l")
-        place("kl", "exl")
-        offsets("fl", "kl")
+        offsets("fh", "exh")
+        pick(T.lh[:, 0:C], "exl", "l")
+        offsets("fl", "exl")
         if r == R - 1:
             dma("g", ["l", "h"], [], T.od[:], T.lh[0:128:16, :])
         n = r + 1
-        for b in range(4):
-            take_h(n, 0, b)
-        for b in range(NH):
-            take_h(n, 1, b)
-        for b in range(4):
-            take_l(n, 0, b)
-        quant_y(n, 0)
-        for b in range(4):
-            layer(n, 0, b)
-        for b in range(NL):
-            take_l(n, 1, b)
-        for b in range(4):
-            relu(n, 0, b)
-        for b in range(NH, 4):
-            take_h(n, 1, b)
-        for b in range(4):
-            add(n, 0, b)
-        quant_x(n, 0, T.x1, ["x10%d" % b for b in range(4)])
-        if n < R:
-            ship_x(n, 0)
-            own_mm(n, 0, 6, 7)
-        else:
-            store(0, 6)
-        for b in range(NL, 4):
-            take_l(n, 1, b)
-        quant_y(n, 1)
-        if n < R:
-            evac_a("ow", n, 0, 7, M0)
-            evac_b("ow", n, 0, 6, M1)
-            spread_u(n)
-        else:
-            store_y(0, 6)
-        for b in range(4):
-            layer(n, 1, b)
-            relu(n, 1, b)
-        if n < R:
-            own_windows(n, 0)
-        for b in range(4):
-            add(n, 1, b)
-        quant_x(n, 1, T.x1, ["x11%d" % b for b in range(4)])
-        if n < R:
-            ship_x(n, 1)
-            own_mm(n, 1, 6, 7)
-            evac_b("ow", n, 1, 6, M1)
-            evac_a("ow", n, 1, 7, M0)
-            own_windows(n, 1)
-        else:
-            store(1, 7)
-            store_y(1, 7)
+        for i in range(3):
+            take_h(i)
+        take_l(0)
+        take_l(1)
+        quant_y(0)
+        layers(0)
+        relus(0, 0, 4)
+        take_h(3)
+        take_l(2)
+        adds(0, 0, 4)
+        quant_y(1)
+        quant_x(n, 0)
+        onward(n, 0)
+        layers(1)
+        relus(1, 0, 1)
+        scores(n, 0)
+        relus(1, 1, 4)
+        take_l(3)
+        rows(n, 0)
+        adds(1, 0, 1)
+        quant_y(2)
+        adds(1, 1, 4)
+        quant_x(n, 1)
+        onward(n, 1)
+        layers(2)
+        relus(2, 0, 1)
+        scores(n, 1)
+        relus(2, 1, 4)
+        rows(n, 1)
+        adds(2, 0, 4)
+        quant_x(n, 2)
+        onward(n, 2)
+        scores(n, 2)
+    rows(R, NS - 1)
     for s in count:
         if count[s] and max(known[q].get(s, 0) for q in known) < count[s]:
             g.wait_ge(T.sem[s], count[s])

@@ -10,12 +10,16 @@ XW = C + 2 * V
 ST = 16
 NS = 3
 CUT = [0, 160, 288, 384]
-SC = [8, 8]
-SUB = 64
+PLACE = [224, 0, 128]
+SC = [7, 8]
+LAST = (38, 44)
+SUB = 80
 BIG = 1e29
-RUNS = [[(0, 160, 0), (160, 384, 0)],
-        [(0, 160, 0), (160, 288, 0), (288, 384, 0)],
-        [(0, 160, 0), (160, 288, 0), (288, 384, 0)]]
+CORES = 64
+NO_, ODD, EVEN, ALL = (0, 0), (0, 1), (1, 0), (1, 1)
+RUNS = [[(0, 160, NO_), (160, 384, NO_)],
+        [(0, 160, NO_), (160, 288, NO_), (288, 384, NO_)],
+        [(0, 160, ODD), (160, 288, EVEN), (288, 384, ALL)]]
 Q4, U8, BF, F32, I32, U16 = "float8_e4m3fn_x4", "uint8", "bfloat16", "float32", "int32", "uint16"
 
 SCRATCH = {"ps": ("psum", [128, 4096], F32)}
@@ -38,12 +42,12 @@ for _r in range(R):
 for _n, _w, _t in [
         ("x0", 4 * C, BF), ("x1", 4 * XW, BF), ("ut", 512, BF), ("vt", 512, BF),
         ("uq", 128, Q4), ("us", 128, U8), ("urq", 128, Q4), ("urs", 128, U8), ("vq", 128, Q4), ("vs", 128, U8),
-        ("wq", 512, Q4), ("wp", 512, U8), ("hq", C, Q4), ("hs", C, U8),
+        ("wq", 512, Q4), ("wp", 512, U8), ("hq", C, Q4), ("hs", C, U8), ("huq", 8, Q4), ("hus", 32, U8),
         ("pi", 8, I32), ("pa", 8, I32), ("pb", 8, I32), ("pc", 8, I32), ("pd", 8, I32),
         ("iw", 12, F32), ("im", SG, F32), ("ik", 24, F32), ("iy", 96, F32),
         ("ie", 512, BF), ("ic", 128, F32), ("col", 24, F32), ("wb", 12, F32), ("wd", 12, F32),
         ("ma", SG, F32), ("mb", SG, I32), ("lm", SG, U16), ("crow", ST * SG, BF), ("rst", ST * SG, F32),
-        ("ca", 16, F32), ("cb", 16, F32), ("cc", 16, F32), ("cd", 16, F32), ("kd", C, F32),
+        ("ca", 16, F32), ("cb", 16, F32), ("cc", 16, F32), ("cd", 16, F32), ("ir", 24, F32), ("kd", C, F32),
         ("ya", 4, F32), ("yb", 4, F32), ("yc", 4, F32), ("yd", 4, F32), ("ky", C, BF),
         ("lu16", 8, U16), ("lu1", 8, U16), ("lw", 12, U16), ("la", 6, U16), ("lsc", 4, U16),
         ("et", 2048, BF), ("eq", 512, Q4), ("es", 512, U8), ("ct", 1024, BF), ("cq", 256, Q4), ("cs", 256, U8),
@@ -52,21 +56,27 @@ for _n, _w, _t in [
         ("mt", 4 * C, BF), ("mq", C, Q4), ("ms", C, U8),
         ("dpx", XW, BF), ("nd", C, BF), ("exd", C, F32), ("exh", C, BF), ("exl", C, BF),
         ("fd", 24, U16), ("fh", 96, U16), ("fl", 96, U16),
-        ("ok", C, BF), ("nok", C, BF), ("okd", C, BF), ("l1", C, BF), ("lh", 2 * C, BF),
+        ("ok", C, BF), ("nok", C, BF), ("okd", C, BF), ("l1", C, BF), ("h1", C, BF), ("lh", 2 * C, BF),
         ("pp", 4 * XW, BF), ("gh", 4 * C, BF), ("yt", 4 * XW, BF), ("yq", XW, Q4), ("ys", XW, U8),
         ("rb", 4 * C, F32), ("yo", C, F32)]:
     _sb(_n, _w, _t)
 
 NDMA = 8
-SEMAPHORES = (["v", "a", "t", "g", "sent", "out"] + ["ua%d" % _r for _r in range(R)]
+SEMAPHORES = (["v", "a", "t", "g", "sent", "out", "hu"] + ["ua%d" % _r for _r in range(R)]
               + ["xa%d%d" % (_r, _k) for _r in range(R) for _k in range(len(RUNS[_r]))]
-              + ["h%s%d" % (_c, _k) for _c in "cp" for _k in range(4)] + ["d%d" % _k for _k in range(NDMA)])
+              + ["h%s%d" % (_c, _k) for _c in "cp" for _k in range(len(RUNS[R - 1]))] + ["d%d" % _k for _k in range(NDMA)])
 
 
-def _helper(c, topo):
+def _helper(T, topo, c, r):
+    p = T.cores[T.rank_of(c) ^ (1 << r)]
+    if topo.chip(p) == topo.chip(c):
+        return None
     mine = [k for k in topo.cores_of(c) if topo.die(k) == topo.die(c)]
-    other = [k for k in topo.cores_of(c) if topo.die(k) != topo.die(c)]
-    return other[mine.index(c)]
+    far = [k for k in range(CORES) if topo.mates(topo.chip(k), topo.chip(p)) and topo.die(k) == topo.die(c) and topo.may_write(k, p)]
+    able = [k for k in mine if topo.may_write(k, far[0])]
+    if c in able:
+        return far[able.index(c)]
+    return [k for k in topo.cores_of(c) if topo.die(k) != topo.die(c)][mine.index(c)]
 
 
 def _send(g, T, topo, dst, en, out, in_, sem):
@@ -87,33 +97,28 @@ def _send_u(g, T, topo, dst, en, oq, osc, iq, isc, sem):
     return len(en)
 
 
-def _far(T, topo, c, r):
-    p = T.cores[T.rank_of(c) ^ (1 << r)]
-    h = _helper(c, topo)
-    return topo.chip(p) != topo.chip(c) and T.rank_of(h) is None and topo.may_write(h, p)
-
-
 def _home(T, topo, c, r):
     p = T.cores[T.rank_of(c) ^ (1 << r)]
-    return [e for e in topo.engines(c, _helper(c, topo)) if e not in topo.engines(c, p)]
+    en = topo.engines(c, _helper(T, topo, c, r))
+    return [e for e in en if e not in topo.engines(c, p)] or en
 
 
 def _hand_on(g, core, T, topo):
     for c in T.cores:
         for r in range(R):
-            if _helper(c, topo) == core and _far(T, topo, c, r):
+            if _helper(T, topo, c, r) == core:
                 p = T.cores[T.rank_of(c) ^ (1 << r)]
                 n, en = len(_home(T, topo, c, r)), topo.engines(core, p)
-                sent = 0
+                g.wait_ge(T.sem.hu, n)
+                sent = _send_u(g, T, topo, p, en, T["ulq%d" % r][:], T["uls%d" % r][:], T.huq[:], T.hus[:], T.sem["ua%d" % r])
                 for k, (a, b, via) in enumerate(RUNS[r]):
-                    if via:
+                    if via[T.rank_of(c) % 2]:
                         sem = T.sem["xa%d%d" % (r, k)]
                         g.wait_ge(T.sem["hc%d" % k], n)
                         sent += _send(g, T, topo, p, en, T["lq%d" % r][:, a:b].bitcast(dt.uint8), T.hq[:, a:b].bitcast(dt.uint8), sem)
                         g.wait_ge(T.sem["hp%d" % k], n)
                         sent += _send(g, T, topo, p, en, T["ls%d" % r][:, a:b], T.hs[:, a:b], sem)
-                if sent:
-                    g.wait_ge(T.sem.sent, sent)
+                g.wait_ge(T.sem.sent, sent)
 
 
 def rank_program(g, core, T, topo):
@@ -228,6 +233,12 @@ def rank_program(g, core, T, topo):
     def keys(name, n):
         return ["%s%d" % (name, i) for i in range(n)]
 
+    def slots(name, a, b):
+        return ["%s%d" % (name, n) for n in range(a, b)]
+
+    def cols(name, a, b):
+        return slots(name, a // 16, b // 16)
+
     def ahead(k):
         return CUT[k], max(CUT[k + 1], CUT[k] + 128)
 
@@ -242,6 +253,11 @@ def rank_program(g, core, T, topo):
 
     def ship_u(r):
         order("g", ["urq", "urs"], [])
+        h = _helper(T, topo, core, r)
+        if h is not None:
+            count["sent"] += _send_u(g, T, topo, h, _home(T, topo, core, r), T.huq[:], T.hus[:], T.urq[:, 0:8], T.urs[:, 0:32], T.sem.hu)
+            arrives("ua%d" % r, len(topo.engines(_helper(T, topo, mate[r], r), core)), ["ul%d" % r])
+            return
         count["sent"] += _send_u(g, T, topo, mate[r], topo.engines(core, mate[r]), T["ulq%d" % r][:], T["uls%d" % r][:],
                                  T.urq[:, 0:8], T.urs[:, 0:32], T.sem["ua%d" % r])
         arrives("ua%d" % r, len(topo.engines(mate[r], core)), ["ul%d" % r])
@@ -251,11 +267,11 @@ def rank_program(g, core, T, topo):
         q, s = T["qx%d" % r], T["sx%d" % r]
         order("g", xkeys(r, a, b), [])
         sem = "xa%d%d" % (r, k)
-        if via and _far(T, topo, core, r):
-            h, en = _helper(core, topo), _home(T, topo, core, r)
+        if via[rank % 2]:
+            h, en = _helper(T, topo, core, r), _home(T, topo, core, r)
             count["sent"] += _send(g, T, topo, h, en, raw(T.hq[:, a:b]), raw(q[:, a:b]), T.sem["hc%d" % k])
             count["sent"] += _send(g, T, topo, h, en, T.hs[:, a:b], s[:, a:b], T.sem["hp%d" % k])
-            arrives(sem, 2 * len(topo.engines(_helper(mate[r], topo), core)), ["lx%d%d" % (r, k)])
+            arrives(sem, 2 * len(topo.engines(_helper(T, topo, mate[r], r), core)), ["lx%d%d" % (r, k)])
             return
         en = topo.engines(core, mate[r])
         count["sent"] += _send(g, T, topo, mate[r], en, raw(T["lq%d" % r][:, a:b]), raw(q[:, a:b]), T.sem[sem])
@@ -273,7 +289,7 @@ def rank_program(g, core, T, topo):
         cp(words(T["upq%d" % r][:]), words(T["ulq%d" % r][:]).indirect(T.lu1[:]), ["ul%d" % r, "lu1"], ["upq%d" % r])
         act(T["ups%d" % r][:], T["uls%d" % r][:, 0:8].indirect(T.lu1[:]), ACT.Copy, ["ul%d" % r, "lu1"], ["ups%d" % r])
 
-    PL, M0, M1, PA, PB, PM, AM, CD, CY, T1, T2 = [T.col[:, k:k + 1] for k in range(11)]
+    PL, M0, M1, PA, PB, PM, AM, CD, CY, T1, T2, T3, T4 = [T.col[:, k:k + 1] for k in range(13)]
 
     def own_mm(r, k):
         a, b = behind(k)
@@ -313,11 +329,13 @@ def rank_program(g, core, T, topo):
             act(t[:, i:i + n], T.ie[:, 0:n], ACT.Identity, ["ie"], w if i + n == z else [], scale=0.0)
 
     def every16(i):
-        ts(T.kd[:, i:C:16], T.ik[:], T.ca[:, i:i + 1], T.cd[:, i:i + 1], ALU.mult, ALU.add, ["ik", "ca", "cdd"], ["kd%d" % i])
+        ts(T.kd[:, i:C:16], T.ir[:], T.ca[:, i:i + 1], T.cd[:, i:i + 1], ALU.mult, ALU.add, keys("ir", 3) + ["ca", "cdd"], ["kd%d" % i])
 
-    dma("a", [], ["x00"], T.x0[:, 0:4 * CUT[1]], T.x[:, 0:4 * CUT[1]])
+    CHECK = [(256, C), (0, 96), (96, 256)]
+
+    dma("a", [], ["x00"], T.x0[:, 0:4 * CUT[1]], T.x[:, 4 * PLACE[0]:4 * C])
     dma("s", [], ["ut"], T.ut[:], T.u[:])
-    dma("s", [], ["x01"], T.x0[:, 4 * CUT[1]:4 * C], T.x[:, 4 * CUT[1]:4 * C])
+    dma("s", [], ["x01"], T.x0[:, 4 * CUT[1]:4 * C], T.x[:, 0:4 * PLACE[0]])
     iota("pi", T.pi[:], [[0, 8]], 0, 1)
     iota("iw", T.iw[:], [[128, 3], [16, 4]], 0, 1)
     iota("ik", T.ik[:], [[1, 24]], 0, 0)
@@ -325,9 +343,7 @@ def rank_program(g, core, T, topo):
     iota("ic", T.ic[:], [[1, 8], [0, 16]], 0, 0)
     iota("im", T.im[:], [[16, SG]], 0, 0)
     iota("iy", T.iy[:], [[4, 96]], 0, 0)
-    fill(T.rst[:], 0.0, ["rst"])
     fill(T.crow[:], 1.0, ["crow"])
-    fill(T.dd[:, 0:48 * SG:SG], BIG, ["fill"])
     ts(T.pb[:], T.pi[:], 7, None, ALU.bitwise_and, None, ["pi"], ["pb"])
     ts(T.pa[:], T.pi[:], 15, None, ALU.bitwise_and, None, ["pi"], ["pa"])
     ts(T.pc[:], T.pi[:], 3, None, ALU.bitwise_and, None, ["pi"], ["pc"])
@@ -337,9 +353,10 @@ def rank_program(g, core, T, topo):
     cp(T.lu1[:], T.pb[:], ["pb"], ["lu1"])
     cp(PB, T.pc[:, 0:1], ["pc"], ["pbc"])
     cp(PA, T.pd[:, 0:1], ["pd"], ["pac"])
+    ts(T.lsc[:, 0:3], T.iw[:, 0:12:4], 4.0, None, ALU.mult, None, ["iw"], ["lsc"])
     ts(T.iw[:, 3:12:4], T.iw[:, 3:12:4], -32.0, None, ALU.add, None, ["iw"], ["iw"])
     ts(M0, PL, 8.0, None, ALU.is_lt, None, ["pl"], ["m0"])
-    fill(T.rst[:, 0:ST * SG:SG], BIG, ["rst"])
+    fill(T.dd[:, 0:48 * SG:SG], BIG, ["fill"])
     ts(T.wb[:], T.iw[:], float(C), -float(C), ALU.is_ge, ALU.mult, ["iw"], ["wb"])
     ts(M1, PL, 8.0, None, ALU.is_ge, None, ["pl", "m0"], ["mask"])
     fill(T.crow[:, 0:ST * SG:SG], -17.0, ["crow"])
@@ -348,33 +365,26 @@ def rank_program(g, core, T, topo):
     ts(T2, PA, 0.0, 4.0, ALU.is_equal, ALU.mult, ["pac"], ["t2"])
     cp(T.lw[:], T.wd[:], ["wd"], ["lw"])
     cp(T.la[:, 0:6:2], T.wd[:, 3:12:4], ["wd"], ["la"])
-    ts(T.lsc[:, 0:3], T.wd[:, 3:12:4], 4.0, None, ALU.mult, None, ["wd"], ["lsc"])
-    ts(T.lw[:, 3:12:4], T.wd[:, 3:12:4], float(C), None, ALU.add, None, ["wd"], ["lw"])
-    ts(PM, PL, T1, -1.0, ALU.add, ALU.add, ["pl", "t1"], ["pm"])
-    ts(AM, PA, T2, -1.0, ALU.add, ALU.add, ["pac", "t2"], ["am"])
-    ts(CD, T1, 64.0, -64.0, ALU.mult, ALU.add, ["t1"], ["cd"])
-    ts(CY, T2, 224.0, PB, ALU.mult, ALU.add, ["t2", "pbc"], ["cy0"])
     ts(T.ca[:], T.ik[:, 0:16], PL, None, ALU.is_equal, None, ["ik", "pl"], ["ca"])
-    ts(T.cb[:], T.ik[:, 0:16], PM, -1024.0, ALU.is_equal, ALU.mult, ["ik", "pm"], ["cb"])
-    ts(T.ya[:], T.ik[:, 0:4], PA, None, ALU.is_equal, None, ["ik", "pac"], ["ya"])
-    ts(T.yb[:], T.ik[:, 0:4], AM, -224.0, ALU.is_equal, ALU.mult, ["ik", "am"], ["yb"])
-    ts(T1, PL, 80.0, None, ALU.add, None, ["pl"], ["t1"])
-    ts(T2, PA, 32.0, None, ALU.add, None, ["pac"], ["t2"])
-    ts(T.ik[:], T.ik[:], 16.0, None, ALU.mult, None, ["ik"], ["ik"])
-    ts(CY, CY, -64.0, None, ALU.add, None, ["cy0"], ["cy"])
-    ts(T.cc[:], T.ca[:], T1, None, ALU.mult, None, ["ca", "t1"], ["cc"])
-    ts(T.yc[:], T.ya[:], T2, None, ALU.mult, None, ["ya", "t2"], ["yc"])
+    ts(T.lw[:, 3:12:4], T.wd[:, 3:12:4], float(C), None, ALU.add, None, ["wd"], ["lw"])
     zero(T.pw, 0, 2 * C, ["pw0", "pw1"])
-    zero(T.ct, 0, 1024, ["ct0", "ct1"])
+    zero(T.rst, 0, ST * SG, ["rst"])
     quant(T.qx0[:, 0:CUT[1]], T.sx0[:, 0:CUT[1]], T.x0[:, 0:4 * CUT[1]], ["x00"], ["qx00"])
     quant(T.uq[:], T.us[:], T.ut[:], ["ut"], ["uq"])
-    tt(T.cd[:], T.cc[:], T.cb[:], ALU.add, ["cc", "cb"], ["cdd"])
-    tt(T.yd[:], T.yc[:], T.yb[:], ALU.add, ["yc", "yb"], ["yd"])
+    ts(PM, PL, T1, -1.0, ALU.add, ALU.add, ["pl", "t1"], ["pm"])
+    ts(AM, PA, T2, -1.0, ALU.add, ALU.add, ["pac", "t2"], ["am"])
     cp(words(T.urq[:]), words(T.uq[:]).indirect(T.lu16[:]), ["uq", "lu16"], ["urq"])
     act(T.urs[:], T.us[:].indirect(T.lu16[:]), ACT.Copy, ["uq", "lu16"], ["urs"])
     ship(0, 0, lambda: ship_u(0))
-    for i in range(8):
-        every16(i)
+    ts(CD, T1, 64.0, -64.0, ALU.mult, ALU.add, ["t1"], ["cd"])
+    ts(CY, T2, 224.0, PB, ALU.mult, ALU.add, ["t2", "pbc"], ["cy0"])
+    ts(T.cb[:], T.ik[:, 0:16], PM, -1024.0, ALU.is_equal, ALU.mult, ["ik", "pm"], ["cb"])
+    ts(T.ya[:], T.ik[:, 0:4], PA, None, ALU.is_equal, None, ["ik", "pac"], ["ya"])
+    ts(T.yb[:], T.ik[:, 0:4], AM, -224.0, ALU.is_equal, ALU.mult, ["ik", "am"], ["yb"])
+    ts(T3, PL, 80.0, None, ALU.add, None, ["pl"], ["t3"])
+    ts(T4, PA, 32.0, None, ALU.add, None, ["pac"], ["t4"])
+    for i, (a, z) in enumerate(CHECK):
+        ts(T.ir[:, a // 16:z // 16], T.ik[:, a // 16:z // 16], 16.0, -float(a), ALU.mult, ALU.add, ["ik"], ["ir%d" % i])
     quant(T.qx0[:, CUT[1]:C], T.sx0[:, CUT[1]:C], T.x0[:, 4 * CUT[1]:4 * C], ["x01"], ["qx01", "qx02"])
     ship(0, 1)
     ship_u(1)
@@ -382,15 +392,22 @@ def rank_program(g, core, T, topo):
     dma("s", ["ul0"], ["wq"], raw(T.wq[:]), T.wc[:])
     dma("s", [], ["wp"], T.wp[:], T.ws[:])
     dma("s", [], ["vt"], T.vt[:], T.v[:])
+    zero(T.ct, 0, 1024, ["ct0", "ct1"])
     for k in range(NS):
         own_mm(0, k)
         own_row(k)
         own_windows(k)
-    zero(T.mt, 0, 4 * C, ["mt"])
+    zero(T.mt, 0, 4 * C, ["mta", "mtb"])
     zero(T.x1, 4 * C, 4 * XW, ["x1z"])
     zero(T.yt, 4 * C, 4 * XW, ["ytz"])
-    tiles = keys("et", 4)
+    ts(CY, CY, -64.0, None, ALU.add, None, ["cy0"], ["cy"])
+    ts(T.cc[:], T.ca[:], T3, None, ALU.mult, None, ["ca", "t3"], ["cc"])
+    ts(T.yc[:], T.ya[:], T4, None, ALU.mult, None, ["ya", "t4"], ["yc"])
+    fill(T.rst[:, 0:ST * SG:SG], BIG, ["rst"])
     ts(T.ma[:], T.im[:], PL, None, ALU.add, None, ["im", "pl"], ["ma"])
+    tt(T.cd[:], T.cc[:], T.cb[:], ALU.add, ["cc", "cb"], ["cdd"])
+    tt(T.yd[:], T.yc[:], T.yb[:], ALU.add, ["yc", "yb"], ["yd"])
+    tiles = keys("et", 4)
     for b in range(4):
         ts(T.et[:, 512 * b:512 * (b + 1)], T.ie[:], float(b), None, ALU.is_equal, None, ["ie"], ["et%d" % b])
         if b == 0:
@@ -402,16 +419,16 @@ def rank_program(g, core, T, topo):
     ts(T.ct[:, 512:1024:4], T.ic[:], PL, None, ALU.is_equal, None, ["ic", "pl"], ["ct1"])
     quant(T.eq[:], T.es[:], T.et[:], tiles, ["eq"])
     quant(T.cq[:], T.cs[:], T.ct[:], ["ct0", "ct1"], ["cq"])
-    for i in range(8, 16):
+    for i in range(16):
         every16(i)
     spread_u(0)
 
     def late():
-        for k in range(1, NS):
-            a, z = CUT[k] // 4, CUT[k + 1] // 4
-            ts(T.iy[:, a:z], T.iy[:, a:z], -float(CUT[k]), None, ALU.add, None, ["iy"], ["iy%d" % k])
+        for k in (0, 2):
+            a, z = PLACE[k] // 4, (PLACE[k] + CUT[k + 1] - CUT[k]) // 4
+            ts(T.iy[:, a:z], T.iy[:, a:z], -float(PLACE[k]), None, ALU.add, None, ["iy"], ["iy%d" % k])
         for i in range(4):
-            ts(T.ky[:, i:C:4], T.iy[:], T.ya[:, i:i + 1], T.yd[:, i:i + 1], ALU.mult, ALU.add, ["iy", "iy1", "iy2", "ya", "yd"], ["ky%d" % i])
+            ts(T.ky[:, i:C:4], T.iy[:], T.ya[:, i:i + 1], T.yd[:, i:i + 1], ALU.mult, ALU.add, ["iy", "iy0", "iy2", "ya", "yd"], ["ky%d" % i])
 
     def diffs(a, b):
         for n in range(a, b):
@@ -419,9 +436,6 @@ def rank_program(g, core, T, topo):
             o = 64 * s
             act(T.dd[:, SG * n + 1:SG * n + SG], T.ba[:, o + q:o + q + NO], ACT.Abs, ["ba%d" % s], ["dd%d" % n],
                 bias=T.ba[:, o + 48 + q:o + 49 + q], scale=-1.0)
-
-    def slots(name, a, b):
-        return ["%s%d" % (name, n) for n in range(a, b)]
 
     def least(a, b):
         scan(T.pm[:, SG * a:SG * b], T.rst[:, 0:SG * (b - a)], T.dd[:, SG * a:SG * b], 0.0, ALU.add, ALU.min,
@@ -450,6 +464,52 @@ def rank_program(g, core, T, topo):
         act(T.cnt[:, SG * a:SG * b:SG], T.acc[:, a:b], ACT.Identity, slots("acc", a, b), slots("cnt", a, b),
             bias=-float(V), scale=-1.0)
 
+    PART = {"a": (0, 256, 0, 2), "b": (256, C, 2, 3)}
+    HELD = {"a": [(240, C, 0), (0, 112, 144)], "b": [(112, 240, 16)]}
+
+    def lay(p):
+        a, z, s0, s1 = PART[p]
+        cp(T.mt[:, 0:4 * z].indirect(T.lsc[:, s0:s1]), T.cnt[:, ST * SG * s0:ST * SG * s1:SG],
+           slots("cnt", ST * s0, ST * s1) + ["lsc"], ["mta", "mt" + p])
+
+    def pack(p):
+        a, z, s0, s1 = PART[p]
+        quant(T.mq[:, a:z], T.ms[:, a:z], T.mt[:, 4 * a:4 * z], ["mt" + p], ["mq" + p])
+        a = min(a, 240)
+        for b, c in ((4, 128), (6, 0)):
+            mm(b + (p == "b"), z - a, T.cq[:, c:c + 128], T.cs[:, c:c + 128], T.mq[:, a:z], T.ms[:, a:z], ["cq", "mqa", "mq" + p])
+
+    def sixteenth(p):
+        b = 4 + (p == "b")
+        for a, z, o in HELD[p]:
+            scan(T.exd[:, a:z], bank(b, z - a, o), T.kd[:, a:z], -1024.0, ALU.max, ALU.add, keys("kd", 16) + ["ps%d" % b], cols("exd", a, z))
+
+    def minus(p, q):
+        b = 4 + (p == "b")
+        for a, z, o in HELD[p]:
+            if q == "v":
+                ts(T.nd[:, a:z], bank(b, z - a, o), -1.0, None, ALU.mult, None, ["ps%d" % b], cols("nd", a, z))
+            else:
+                act(T.nd[:, a:z], bank(b, z - a, o), ACT.Identity, ["ps%d" % b], cols("nd", a, z), scale=-1.0)
+
+    def theirs(p):
+        for a, z, o in {"a": [(256, XW, 0), (0, 128, 128)], "b": [(128, 256, 16)]}[p]:
+            act(T.dpx[:, a:z], bank(6 + (p == "b"), z - a, o), ACT.Copy, ["ps%d" % (6 + (p == "b"))], cols("dp", a, z))
+
+    def reach(a, z):
+        ts(T.fd[:, a // 16:z // 16], T.exd[:, a + 15:z:16], CD, None, ALU.add, None, cols("exd", a, z) + ["cd"], cols("fd", a, z))
+
+    def check(i):
+        a, z = CHECK[i]
+        tt(T.ok[:, a:z], T.dpx[:, a:z + 2 * V].indirect(T.fd[:, a // 16:z // 16]), T.nd[:, a:z], ALU.is_equal,
+           cols("dp", a, z + 2 * V) + cols("fd", a, z) + cols("nd", a, z), cols("ok", a, z))
+
+    def kept(a, z, b, o):
+        tt(T.okd[:, a:z], T.ok[:, a:z], bank(b, z - a, o), ALU.mult, cols("ok", a, z) + ["ps%d" % b], cols("okd", a, z))
+
+    def other(a, z):
+        act(T.nok[:, a:z], T.ok[:, a:z], ACT.Identity, cols("ok", a, z), cols("nok", a, z), bias=1.0, scale=-1.0)
+
     def unpack(q, s, r):
         for b in range(4):
             mm(b, C, T.eq[:, 128 * b:128 * b + 128], T.es[:, 128 * b:128 * b + 128], q[:, 0:C], s[:, 0:C], ["eq"] + r)
@@ -457,30 +517,34 @@ def rank_program(g, core, T, topo):
     def evac_p(b):
         act(T.pp[:, 4 * V + b:4 * (V + C):4], bank(b, C), ACT.Identity, ["ps%d" % b], ["pp%d" % b], scale=0.5)
 
+    def carry(out, init, r, w, rev):
+        a, b = (T.nok[:, ::-1], T.okd[:, ::-1]) if rev else (T.nok[:], T.okd[:])
+        scan(out, a, b, init, ALU.mult, ALU.add, cols("nok", 0, C) + cols("okd", 0, C) + r, w)
+
     def pick(row, ex, key):
         scan(T[ex][:], row, T.ky[:], -224.0, ALU.max, ALU.add, keys("ky", 4) + [key], [ex])
 
     def offsets(off, ex):
         ts(T[off][:], T[ex][:, 3:C:4], 4.0, CY, ALU.mult, ALU.add, [ex, "cy"], [off])
 
-    parts = [(0, 0, SUB), (0, SUB, CUT[1]), (1, CUT[1], CUT[2]), (2, CUT[2], CUT[3])]
     plane = keys("pp", 4) + ["ppa", "ppz"]
 
-    def source(i, off):
-        k, a, z = parts[i]
-        return T.pp[:, 4 * CUT[k]:4 * (CUT[k + 1] + 2 * V)].indirect(T[off][:, a // 4:z // 4])
+    def source(k, a, z, off):
+        o = PLACE[k] - CUT[k]
+        return T.pp[:, 4 * CUT[k]:4 * (CUT[k + 1] + 2 * V)].indirect(T[off][:, (a + o) // 4:(z + o) // 4])
 
-    def take_h(i):
-        k, a, z = parts[i]
-        act(T.gh[:, 4 * a:4 * z], source(i, "fh"), ACT.Copy, plane + ["fh"], ["gh%d" % i])
+    def take_h(k, a, z, q="a"):
+        if q == "a":
+            act(T.gh[:, 4 * a:4 * z], source(k, a, z, "fh"), ACT.Copy, plane + ["fh"], cols("gh", a, z))
+        else:
+            cp(T.gh[:, 4 * a:4 * z], source(k, a, z, "fh"), plane + ["fh"], cols("gh", a, z))
 
-    def take_l(i):
-        k, a, z = parts[i]
-        tt(T.yt[:, 4 * a:4 * z], source(i, "fl"), T.gh[:, 4 * a:4 * z], ALU.add, plane + ["fl", "gh%d" % i], ["yt%d" % i])
+    def take_l(k, a, z):
+        tt(T.yt[:, 4 * a:4 * z], source(k, a, z, "fl"), T.gh[:, 4 * a:4 * z], ALU.add, plane + ["fl"] + cols("gh", a, z), cols("yt", a, z))
 
     def quant_y(k):
         a, z = ahead(k)
-        quant(T.yq[:, a:z], T.ys[:, a:z], T.yt[:, 4 * a:4 * z], ["ytz"] + ["yt%d" % i for i in range(4) if parts[i][0] == k], ["yq%d" % k])
+        quant(T.yq[:, a:z], T.ys[:, a:z], T.yt[:, 4 * a:4 * z], ["ytz"] + cols("yt", CUT[k], CUT[k + 1]), ["yq%d" % k])
 
     def layers(k):
         a, z = ahead(k)
@@ -507,12 +571,13 @@ def rank_program(g, core, T, topo):
         if r < R:
             ship_piece(r, k)
             return
-        a, z = CUT[k], CUT[k + 1]
+        a, z, o = CUT[k], CUT[k + 1], PLACE[k]
         q, s = T["qx%d" % R], T["sx%d" % R]
-        put("s", xkeys(R, a, z), T.oc[:, 4 * a:4 * z], raw(q[:, a:z]))
-        if k == NS - 1:
+        put("s", xkeys(R, a, z), T.oc[:, 4 * o:4 * (o + z - a)], raw(q[:, a:z]))
+        if k != 1:
+            a, o = (a, o) if k == 0 else (CUT[1], 0)
             for i in range(4):
-                put("sa"[i // 2], xkeys(R, 0, C), T.osc[4 * i:4 * i + 4, :], s[32 * i:32 * i + 4, 0:C])
+                put("sa"[i // 2 * (k > 0)], xkeys(R, a, z), T.osc[4 * i:4 * i + 4, o:o + z - a], s[32 * i:32 * i + 4, a:z])
 
     def scores(r, k):
         if r < R:
@@ -528,7 +593,7 @@ def rank_program(g, core, T, topo):
             return
         a, z = CUT[k], CUT[k + 1]
         act(T.yo[:, a:z], bank(7, z - a, a - behind(k)[0]), ACT.Copy, ["ps7"], ["yo%d" % k])
-        put("a" if k == NS - 1 else "s", ["yo%d" % k], T.y[:, a:z], T.yo[:, a:z])
+        put("a" if k == NS - 1 else "s", ["yo%d" % k], T.y[:, PLACE[k]:PLACE[k] + z - a], T.yo[:, a:z])
 
     for r in range(R):
         far_mm(r, 0, 4)
@@ -544,9 +609,9 @@ def rank_program(g, core, T, topo):
             a, m, z = ST * s, ST * s + SC[s], ST * (s + 1)
             diffs(a, m)
             least(a, m)
-            far_mm(r, s + 1, 5 + s)
-            far_row(s + 1, 5 + s, 0, "v")
-            far_row(s + 1, 5 + s, 1, "v")
+            far_mm(r, s + 1, 6 - s)
+            far_row(s + 1, 6 - s, 0, "v")
+            far_row(s + 1, 6 - s, 1, "v")
             if s > 0:
                 tally(ST * (s - 1) + SC[s - 1], a)
             windows(s + 1)
@@ -557,66 +622,76 @@ def rank_program(g, core, T, topo):
             least(m, z)
             signs(a, m)
             above(m, z)
-        a, m, e, z = 32, 36, 44, 48
+        a, (m, e), z = 2 * ST, LAST, 3 * ST
         diffs(a, a + 3)
         counted(ST, ST + SC[1])
         diffs(a + 3, m)
         tally(ST + SC[1], a)
         least(a, m)
         diffs(m, e)
+        unpack(T["lq%d" % r], T["ls%d" % r], landed(r, 0, C))
+        lay("a")
         least(m, e)
         diffs(e, z)
-        above(a, m)
+        pack("a")
         least(e, z)
-        signs(m, e)
-        unpack(T["lq%d" % r], T["ls%d" % r], landed(r, 0, C))
-        tally(a, m)
+        signs(a, m)
         above(e, z)
-        evac_p(0)
-        counted(m, e)
+        signs(m, e)
+        sixteenth("a")
         tally(e, z)
-        for b in range(1, 3):
+        counted(a, e)
+        theirs("a")
+        minus("a", "a")
+        lay("b")
+        reach(240, C)
+        reach(0, 112)
+        pack("b")
+        for b in range(2):
             evac_p(b)
-        cp(T.mt[:].indirect(T.lsc[:, 0:3]), T.cnt[:, 0:48 * SG:SG], slots("cnt", 0, 48) + ["lsc"], ["mt"])
-        quant(T.mq[:], T.ms[:], T.mt[:], ["mt"], ["mq"])
-        mm(5, C, T.cq[:, 128:256], T.cs[:, 128:256], T.mq[:], T.ms[:], ["cq", "mq"])
-        mm(4, C, T.cq[:, 0:128], T.cs[:, 0:128], T.mq[:], T.ms[:], ["cq", "mq"])
+        check(0)
+        check(1)
+        sixteenth("b")
+        theirs("b")
+        minus("b", "v")
+        kept(256, C, 4, 16)
+        reach(112, 240)
+        other(256, C)
+        other(0, 96)
+        kept(0, 96, 4, 144)
+        check(2)
+        evac_p(2)
         if r + 1 < R:
             spread_u(r + 1)
         else:
             quant(T.vq[:], T.vs[:], T.vt[:], ["vt"], ["vq"])
-        scan(T.exd[:], bank(5, C), T.kd[:], -1024.0, ALU.max, ALU.add, keys("kd", 16) + ["ps5"], ["exd"])
-        act(T.dpx[:, V:V + C], bank(4, C), ACT.Copy, ["ps4"], ["dpm"])
-        act(T.dpx[:, 0:V], bank(4, V, C - V), ACT.Copy, ["ps4"], ["dpa"])
-        act(T.dpx[:, V + C:XW], bank(4, V), ACT.Copy, ["ps4"], ["dpz"])
-        ts(T.nd[:], bank(5, C), -1.0, None, ALU.mult, None, ["ps5"], ["nd"])
-        ts(T.fd[:], T.exd[:, 15:C:16], CD, None, ALU.add, None, ["exd", "cd"], ["fd"])
+        other(96, 256)
+        kept(96, 240, 5, 0)
+        kept(240, 256, 4, 0)
         evac_p(3)
-        unpack(T["qx%d" % r], T["sx%d" % r], xkeys(r, 0, C))
-        tt(T.ok[:], T.dpx[:].indirect(T.fd[:]), T.nd[:], ALU.is_equal, ["dpm", "dpa", "dpz", "fd", "nd"], ["ok"])
         act(T.pp[:, 0:4 * V], T.pp[:, 4 * C:4 * (C + V)], ACT.Copy, keys("pp", 4), ["ppa"])
-        act(T.nok[:], T.ok[:], ACT.Identity, ["ok"], ["nok"], bias=1.0, scale=-1.0)
         act(T.pp[:, 4 * (C + V):4 * XW], T.pp[:, 4 * V:8 * V], ACT.Copy, keys("pp", 4), ["ppz"])
-        tt(T.okd[:], T.ok[:], bank(5, C), ALU.mult, ["ok", "ps5"], ["okd"])
-        scan(T.l1[:], T.nok[:], T.okd[:], 0.0, ALU.mult, ALU.add, ["nok", "okd"], ["l1"])
-        scan(T.lh[:, 2 * C - 1:C - 1:-1], T.nok[:, ::-1], T.okd[:, ::-1], T.l1[:, C - 1:C], ALU.mult, ALU.add, ["nok", "okd", "l1"], ["h"])
+        unpack(T["qx%d" % r], T["sx%d" % r], xkeys(r, 0, C))
+        carry(T.l1[:], 0.0, [], ["l1"], False)
+        carry(T.h1[:, ::-1], 0.0, [], ["h1"], True)
+        carry(T.lh[:, 2 * C - 1:C - 1:-1], T.l1[:, C - 1:C], ["l1"], ["h"], True)
+        carry(T.lh[:, 0:C], T.h1[:, 0:1], ["h1"], ["l"], False)
         pick(T.lh[:, C:2 * C], "exh", "h")
-        scan(T.lh[:, 0:C], T.nok[:], T.okd[:], T.lh[:, C:C + 1], ALU.mult, ALU.add, ["nok", "okd", "h"], ["l"])
-        offsets("fh", "exh")
         pick(T.lh[:, 0:C], "exl", "l")
+        offsets("fh", "exh")
         offsets("fl", "exl")
         if r == R - 1:
             dma("g", ["l", "h"], [], T.od[:], T.lh[0:128:16, :])
         n = r + 1
-        for i in range(3):
-            take_h(i)
-        take_l(0)
-        take_l(1)
+        take_h(0, 0, SUB)
+        take_h(1, CUT[1], CUT[2])
+        take_h(0, SUB, CUT[1], "v")
+        take_l(0, 0, CUT[1])
+        take_h(2, CUT[2], CUT[3])
         quant_y(0)
         layers(0)
         relus(0, 0, 4)
-        take_h(3)
-        take_l(2)
+        take_l(1, CUT[1], CUT[2])
         adds(0, 0, 4)
         quant_y(1)
         quant_x(n, 0)
@@ -625,7 +700,7 @@ def rank_program(g, core, T, topo):
         relus(1, 0, 1)
         scores(n, 0)
         relus(1, 1, 4)
-        take_l(3)
+        take_l(2, CUT[2], CUT[3])
         rows(n, 0)
         adds(1, 0, 1)
         quant_y(2)

@@ -1,25 +1,21 @@
-from concourse.bass import DstId, RemoteDMATransfer
 from concourse.mybir import dt, AluOpType, ActivationFunctionType
 
 ALU = AluOpType
 ACT = ActivationFunctionType
 C, V, R = 384, 16, 3
-NO = 2 * V + 1
-SG = NO + 1
+SG = 2 * V + 1
 XW = C + 2 * V
 ST = 16
 NS = 3
 CUT = [0, 160, 288, 384]
 PLACE = [224, 0, 128]
-SC = [7, 8]
-LAST = (38, 44)
 SUB = 80
 BIG = 1e29
 CORES = 64
-NO_, ODD, EVEN, ALL = (0, 0), (0, 1), (1, 0), (1, 1)
-RUNS = [[(0, 160, NO_), (160, 384, NO_)],
-        [(0, 160, NO_), (160, 288, NO_), (288, 384, NO_)],
-        [(0, 160, ODD), (160, 288, EVEN), (288, 384, ALL)]]
+NEAR = (0, 0, 0, 0)
+RUNS = [[(0, 160, NEAR, NEAR), (160, 384, NEAR, NEAR)],
+        [(0, 160, NEAR, NEAR), (160, 288, NEAR, NEAR), (288, 384, NEAR, NEAR)],
+        [(0, 160, (0, 0, 1, 2), (0, 1, 0, 1)), (160, 288, (1, 0, 2, 0), (0, 0, 1, 1)), (288, 384, (1, 1, 2, 2), (1, 0, 1, 1))]]
 Q4, U8, BF, F32, I32, U16 = "float8_e4m3fn_x4", "uint8", "bfloat16", "float32", "int32", "uint16"
 
 SCRATCH = {"ps": ("psum", [128, 4096], F32)}
@@ -62,21 +58,29 @@ for _n, _w, _t in [
     _sb(_n, _w, _t)
 
 NDMA = 8
-SEMAPHORES = (["v", "a", "t", "g", "sent", "out", "hu"] + ["ua%d" % _r for _r in range(R)]
+SEMAPHORES = (["v", "a", "t", "g", "sent", "out", "hu0", "hu1"] + ["ua%d" % _r for _r in range(R)]
               + ["xa%d%d" % (_r, _k) for _r in range(R) for _k in range(len(RUNS[_r]))]
               + ["h%s%d" % (_c, _k) for _c in "cp" for _k in range(len(RUNS[R - 1]))] + ["d%d" % _k for _k in range(NDMA)])
 
 
-def _helper(T, topo, c, r):
+def _helpers(T, topo, c, r):
     p = T.cores[T.rank_of(c) ^ (1 << r)]
     if topo.chip(p) == topo.chip(c):
-        return None
+        return {}
     mine = [k for k in topo.cores_of(c) if topo.die(k) == topo.die(c)]
     far = [k for k in range(CORES) if topo.mates(topo.chip(k), topo.chip(p)) and topo.die(k) == topo.die(c) and topo.may_write(k, p)]
     able = [k for k in mine if topo.may_write(k, far[0])]
-    if c in able:
-        return far[able.index(c)]
-    return [k for k in topo.cores_of(c) if topo.die(k) != topo.die(c)][mine.index(c)]
+    ways = {1: [k for k in topo.cores_of(c) if topo.die(k) != topo.die(c)][mine.index(c)]}
+    ways[2] = far[able.index(c)] if c in able else ways[1]
+    return ways
+
+
+def _ways(T, topo, c, r):
+    h = _helpers(T, topo, c, r)
+    to = {(k, i): h.get(run[2 + i][T.rank_of(c) % 4]) for k, run in enumerate(RUNS[r]) for i in range(2)}
+    used = sorted(set(x for x in to.values() if x is not None)) or [None]
+    to[-1, 0], to[-1, 1] = used[0], used[-1]
+    return to
 
 
 def _send(g, T, topo, dst, en, out, in_, sem):
@@ -85,39 +89,26 @@ def _send(g, T, topo, dst, en, out, in_, sem):
     return len(en)
 
 
-def _send_u(g, T, topo, dst, en, oq, osc, iq, isc, sem):
-    rid, pid, _ = topo.addr(dst)
-    half = len(en) // 2
-    to = [DstId(rid=rid, pnc=pid)]
-    g.remote_dma_fused([
-        RemoteDMATransfer(dst_ids=to, dma_engine_mask=sum(1 << e for e in en[:half]), remote_sem=sem,
-                          src=iq.bitcast(dt.uint8), dst=oq.bitcast(dt.uint8)),
-        RemoteDMATransfer(dst_ids=to, dma_engine_mask=sum(1 << e for e in en[half:]), remote_sem=sem, src=isc, dst=osc)],
-        local_sem=T.sem.sent)
-    return len(en)
-
-
-def _home(T, topo, c, r):
-    p = T.cores[T.rank_of(c) ^ (1 << r)]
-    en = topo.engines(c, _helper(T, topo, c, r))
-    return [e for e in en if e not in topo.engines(c, p)] or en
+def _sides(T, r, k, i):
+    if k < 0:
+        names = ("urq", "huq", "ulq%d" % r) if i == 0 else ("urs", "hus", "uls%d" % r)
+        a, b, sems = 0, (8, 32)[i], ("hu%d" % i, "ua%d" % r)
+    else:
+        names = ("qx%d" % r, "hq", "lq%d" % r) if i == 0 else ("sx%d" % r, "hs", "ls%d" % r)
+        a, b, sems = RUNS[r][k][0], RUNS[r][k][1], ("h%s%d" % ("cp"[i], k), "xa%d%d" % (r, k))
+    return [T[x][:, a:b].bitcast(dt.uint8) if i == 0 else T[x][:, a:b] for x in names], sems
 
 
 def _hand_on(g, core, T, topo):
     for c in T.cores:
         for r in range(R):
-            if _helper(T, topo, c, r) == core:
-                p = T.cores[T.rank_of(c) ^ (1 << r)]
-                n, en = len(_home(T, topo, c, r)), topo.engines(core, p)
-                g.wait_ge(T.sem.hu, n)
-                sent = _send_u(g, T, topo, p, en, T["ulq%d" % r][:], T["uls%d" % r][:], T.huq[:], T.hus[:], T.sem["ua%d" % r])
-                for k, (a, b, via) in enumerate(RUNS[r]):
-                    if via[T.rank_of(c) % 2]:
-                        sem = T.sem["xa%d%d" % (r, k)]
-                        g.wait_ge(T.sem["hc%d" % k], n)
-                        sent += _send(g, T, topo, p, en, T["lq%d" % r][:, a:b].bitcast(dt.uint8), T.hq[:, a:b].bitcast(dt.uint8), sem)
-                        g.wait_ge(T.sem["hp%d" % k], n)
-                        sent += _send(g, T, topo, p, en, T["ls%d" % r][:, a:b], T.hs[:, a:b], sem)
+            p, to, sent = T.cores[T.rank_of(c) ^ (1 << r)], _ways(T, topo, c, r), 0
+            for k, i in sorted(to):
+                if to[k, i] == core:
+                    (src, held, land), (here, there) = _sides(T, r, k, i)
+                    g.wait_ge(T.sem[here], len(topo.engines(c, core)))
+                    sent += _send(g, T, topo, p, topo.engines(core, p), land, held, T.sem[there])
+            if sent:
                 g.wait_ge(T.sem.sent, sent)
 
 
@@ -251,34 +242,26 @@ def rank_program(g, core, T, topo):
     def landed(r, a, b):
         return ["lx%d%d" % (r, k) for k, run in enumerate(RUNS[r]) if run[0] < b and a < run[1]]
 
+    def send(r, k, i):
+        (src, held, land), (there, end) = _sides(T, r, k, i)
+        h = _ways(T, topo, core, r)[k, i]
+        if h is None:
+            count["sent"] += _send(g, T, topo, mate[r], topo.engines(core, mate[r]), land, src, T.sem[end])
+        else:
+            count["sent"] += _send(g, T, topo, h, topo.engines(core, h), held, src, T.sem[there])
+        h = _ways(T, topo, mate[r], r)[k, i]
+        return len(topo.engines(mate[r] if h is None else h, core))
+
     def ship_u(r):
         order("g", ["urq", "urs"], [])
-        h = _helper(T, topo, core, r)
-        if h is not None:
-            count["sent"] += _send_u(g, T, topo, h, _home(T, topo, core, r), T.huq[:], T.hus[:], T.urq[:, 0:8], T.urs[:, 0:32], T.sem.hu)
-            arrives("ua%d" % r, len(topo.engines(_helper(T, topo, mate[r], r), core)), ["ul%d" % r])
-            return
-        count["sent"] += _send_u(g, T, topo, mate[r], topo.engines(core, mate[r]), T["ulq%d" % r][:], T["uls%d" % r][:],
-                                 T.urq[:, 0:8], T.urs[:, 0:32], T.sem["ua%d" % r])
-        arrives("ua%d" % r, len(topo.engines(mate[r], core)), ["ul%d" % r])
+        arrives("ua%d" % r, send(r, -1, 0) + send(r, -1, 1), ["ul%d" % r])
 
     def ship(r, k, between=None):
-        a, b, via = RUNS[r][k]
-        q, s = T["qx%d" % r], T["sx%d" % r]
-        order("g", xkeys(r, a, b), [])
-        sem = "xa%d%d" % (r, k)
-        if via[rank % 2]:
-            h, en = _helper(T, topo, core, r), _home(T, topo, core, r)
-            count["sent"] += _send(g, T, topo, h, en, raw(T.hq[:, a:b]), raw(q[:, a:b]), T.sem["hc%d" % k])
-            count["sent"] += _send(g, T, topo, h, en, T.hs[:, a:b], s[:, a:b], T.sem["hp%d" % k])
-            arrives(sem, 2 * len(topo.engines(_helper(T, topo, mate[r], r), core)), ["lx%d%d" % (r, k)])
-            return
-        en = topo.engines(core, mate[r])
-        count["sent"] += _send(g, T, topo, mate[r], en, raw(T["lq%d" % r][:, a:b]), raw(q[:, a:b]), T.sem[sem])
+        order("g", xkeys(r, RUNS[r][k][0], RUNS[r][k][1]), [])
+        n = send(r, k, 0)
         if between:
             between()
-        count["sent"] += _send(g, T, topo, mate[r], en, T["ls%d" % r][:, a:b], s[:, a:b], T.sem[sem])
-        arrives(sem, 2 * len(topo.engines(mate[r], core)), ["lx%d%d" % (r, k)])
+        arrives("xa%d%d" % (r, k), n + send(r, k, 1), ["lx%d%d" % (r, k)])
 
     def ship_piece(r, k):
         for i, run in enumerate(RUNS[r]):
@@ -289,7 +272,7 @@ def rank_program(g, core, T, topo):
         cp(words(T["upq%d" % r][:]), words(T["ulq%d" % r][:]).indirect(T.lu1[:]), ["ul%d" % r, "lu1"], ["upq%d" % r])
         act(T["ups%d" % r][:], T["uls%d" % r][:, 0:8].indirect(T.lu1[:]), ACT.Copy, ["ul%d" % r, "lu1"], ["ups%d" % r])
 
-    PL, M0, M1, PA, PB, PM, AM, CD, CY, T1, T2, T3, T4 = [T.col[:, k:k + 1] for k in range(13)]
+    PL, M0, M1, PA, PB, PM, AM, CD, CY, T1, T2, T3, T4, T5 = [T.col[:, k:k + 1] for k in range(14)]
 
     def own_mm(r, k):
         a, b = behind(k)
@@ -319,6 +302,11 @@ def rank_program(g, core, T, topo):
         else:
             act(out, in_, ACT.Identity, ["ps%d" % b, "mask"], ["pw%d" % half], scale=m)
 
+    def far_rows(r, k):
+        far_mm(r, k, 7 - k)
+        far_row(k, 7 - k, 0, "v")
+        far_row(k, 7 - k, 1, "v")
+
     def windows(s):
         tt(T.ba[:, 64 * s:64 * s + 64], T.pw[:].indirect(T.lw[:, 4 * s:4 * s + 4]), T.og[:, 64 * s:64 * s + 64], ALU.add,
            ["pw0", "pw1", "lw", "ogb%d" % s, "oga%d" % s], ["ba%d" % s])
@@ -328,24 +316,27 @@ def rank_program(g, core, T, topo):
             n = min(512, z - i)
             act(t[:, i:i + n], T.ie[:, 0:n], ACT.Identity, ["ie"], w if i + n == z else [], scale=0.0)
 
-    def every16(i):
-        ts(T.kd[:, i:C:16], T.ir[:], T.ca[:, i:i + 1], T.cd[:, i:i + 1], ALU.mult, ALU.add, keys("ir", 3) + ["ca", "cdd"], ["kd%d" % i])
+    def every16(i, q):
+        if q == "v":
+            ts(T.kd[:, i:C:16], T.ir[:], T.ca[:, i:i + 1], T.cd[:, i:i + 1], ALU.mult, ALU.add, keys("ir", 3) + ["ca", "cdd"], ["kd%d" % i])
+        else:
+            act(T.kd[:, i:C:16], T.ir[:], ACT.Identity, keys("ir", 3) + ["ca", "cdd"], ["kd%d" % i], scale=T.ca[:, i:i + 1], bias=T.cd[:, i:i + 1])
 
     CHECK = [(256, C), (0, 96), (96, 256)]
 
-    dma("a", [], ["x00"], T.x0[:, 0:4 * CUT[1]], T.x[:, 4 * PLACE[0]:4 * C])
+    dma("s", [], ["x00"], T.x0[:, 0:4 * CUT[1]], T.x[:, 4 * PLACE[0]:4 * C])
     dma("s", [], ["ut"], T.ut[:], T.u[:])
     dma("s", [], ["x01"], T.x0[:, 4 * CUT[1]:4 * C], T.x[:, 0:4 * PLACE[0]])
     iota("pi", T.pi[:], [[0, 8]], 0, 1)
     iota("iw", T.iw[:], [[128, 3], [16, 4]], 0, 1)
     iota("ik", T.ik[:], [[1, 24]], 0, 0)
-    iota("ie", T.ie[:], [[1, 512]], 0, -4)
-    iota("ic", T.ic[:], [[1, 8], [0, 16]], 0, 0)
     iota("im", T.im[:], [[16, SG]], 0, 0)
-    iota("iy", T.iy[:], [[4, 96]], 0, 0)
+    iota("ic", T.ic[:], [[1, 8], [0, 16]], 0, 0)
     fill(T.crow[:], 1.0, ["crow"])
+    ts(T5, T.pi[:, 0:1], -4.0, -1.0, ALU.mult, ALU.add, ["pi"], ["t5"])
     ts(T.pb[:], T.pi[:], 7, None, ALU.bitwise_and, None, ["pi"], ["pb"])
     ts(T.pa[:], T.pi[:], 15, None, ALU.bitwise_and, None, ["pi"], ["pa"])
+    scan(T.ie[:], T.crow[:, 0:512], T.crow[:, 0:512], T5, ALU.mult, ALU.add, ["crow", "t5"], ["ie"])
     ts(T.pc[:], T.pi[:], 3, None, ALU.bitwise_and, None, ["pi"], ["pc"])
     ts(T.pd[:], T.pi[:], 2, 3, ALU.arith_shift_right, ALU.bitwise_and, ["pi"], ["pd"])
     ts(T.lu16[:], T.pb[:], 16.0, None, ALU.mult, None, ["pb"], ["lu16"])
@@ -354,24 +345,24 @@ def rank_program(g, core, T, topo):
     cp(PB, T.pc[:, 0:1], ["pc"], ["pbc"])
     cp(PA, T.pd[:, 0:1], ["pd"], ["pac"])
     ts(T.lsc[:, 0:3], T.iw[:, 0:12:4], 4.0, None, ALU.mult, None, ["iw"], ["lsc"])
-    ts(T.iw[:, 3:12:4], T.iw[:, 3:12:4], -32.0, None, ALU.add, None, ["iw"], ["iw"])
     ts(M0, PL, 8.0, None, ALU.is_lt, None, ["pl"], ["m0"])
-    fill(T.dd[:, 0:48 * SG:SG], BIG, ["fill"])
-    ts(T.wb[:], T.iw[:], float(C), -float(C), ALU.is_ge, ALU.mult, ["iw"], ["wb"])
+    ts(T.iw[:, 3:12:4], T.iw[:, 3:12:4], -32.0, None, ALU.add, None, ["iw"], ["iw"])
     ts(M1, PL, 8.0, None, ALU.is_ge, None, ["pl", "m0"], ["mask"])
-    fill(T.crow[:, 0:ST * SG:SG], -17.0, ["crow"])
-    tt(T.wd[:], T.iw[:], T.wb[:], ALU.add, ["iw", "wb"], ["wd"])
+    fill(T.crow[:, 0:ST * SG:SG], -float(V), ["crow"])
+    ts(T.wb[:], T.iw[:], float(C), -float(C), ALU.is_ge, ALU.mult, ["iw"], ["wb"])
     ts(T1, PL, 0.0, 16.0, ALU.is_equal, ALU.mult, ["pl"], ["t1"])
     ts(T2, PA, 0.0, 4.0, ALU.is_equal, ALU.mult, ["pac"], ["t2"])
+    tt(T.wd[:], T.iw[:], T.wb[:], ALU.add, ["iw", "wb"], ["wd"])
+    ts(T.ca[:], T.ik[:, 0:16], PL, None, ALU.is_equal, None, ["ik", "pl"], ["ca"])
+    ts(PM, PL, T1, -1.0, ALU.add, ALU.add, ["pl", "t1"], ["pm"])
     cp(T.lw[:], T.wd[:], ["wd"], ["lw"])
     cp(T.la[:, 0:6:2], T.wd[:, 3:12:4], ["wd"], ["la"])
-    ts(T.ca[:], T.ik[:, 0:16], PL, None, ALU.is_equal, None, ["ik", "pl"], ["ca"])
-    ts(T.lw[:, 3:12:4], T.wd[:, 3:12:4], float(C), None, ALU.add, None, ["wd"], ["lw"])
     zero(T.pw, 0, 2 * C, ["pw0", "pw1"])
     zero(T.rst, 0, ST * SG, ["rst"])
+    zero(T.ct, 0, 1024, ["ct0", "ct1"])
     quant(T.qx0[:, 0:CUT[1]], T.sx0[:, 0:CUT[1]], T.x0[:, 0:4 * CUT[1]], ["x00"], ["qx00"])
     quant(T.uq[:], T.us[:], T.ut[:], ["ut"], ["uq"])
-    ts(PM, PL, T1, -1.0, ALU.add, ALU.add, ["pl", "t1"], ["pm"])
+    ts(T.lw[:, 3:12:4], T.wd[:, 3:12:4], float(C), None, ALU.add, None, ["wd"], ["lw"])
     ts(AM, PA, T2, -1.0, ALU.add, ALU.add, ["pac", "t2"], ["am"])
     cp(words(T.urq[:]), words(T.uq[:]).indirect(T.lu16[:]), ["uq", "lu16"], ["urq"])
     act(T.urs[:], T.us[:].indirect(T.lu16[:]), ACT.Copy, ["uq", "lu16"], ["urs"])
@@ -379,74 +370,78 @@ def rank_program(g, core, T, topo):
     ts(CD, T1, 64.0, -64.0, ALU.mult, ALU.add, ["t1"], ["cd"])
     ts(CY, T2, 224.0, PB, ALU.mult, ALU.add, ["t2", "pbc"], ["cy0"])
     ts(T.cb[:], T.ik[:, 0:16], PM, -1024.0, ALU.is_equal, ALU.mult, ["ik", "pm"], ["cb"])
+    ts(T3, PL, 80.0, None, ALU.add, None, ["pl"], ["t3"])
     ts(T.ya[:], T.ik[:, 0:4], PA, None, ALU.is_equal, None, ["ik", "pac"], ["ya"])
     ts(T.yb[:], T.ik[:, 0:4], AM, -224.0, ALU.is_equal, ALU.mult, ["ik", "am"], ["yb"])
-    ts(T3, PL, 80.0, None, ALU.add, None, ["pl"], ["t3"])
     ts(T4, PA, 32.0, None, ALU.add, None, ["pac"], ["t4"])
+    ts(T.cc[:], T.ca[:], T3, None, ALU.mult, None, ["ca", "t3"], ["cc"])
     for i, (a, z) in enumerate(CHECK):
         ts(T.ir[:, a // 16:z // 16], T.ik[:, a // 16:z // 16], 16.0, -float(a), ALU.mult, ALU.add, ["ik"], ["ir%d" % i])
+    tt(T.cd[:], T.cc[:], T.cb[:], ALU.add, ["cc", "cb"], ["cdd"])
     quant(T.qx0[:, CUT[1]:C], T.sx0[:, CUT[1]:C], T.x0[:, 4 * CUT[1]:4 * C], ["x01"], ["qx01", "qx02"])
     ship(0, 1)
     ship_u(1)
     ship_u(2)
+    iota("iy", T.iy[:], [[4, 96]], 0, 0)
+    iota("mta", T.mt[:], [[0, 4 * C]], 0, 0)
+    iota("x1z", T.x1[:, 4 * C:4 * XW], [[0, 8 * V]], 0, 0)
+    iota("ytz", T.yt[:, 4 * C:4 * XW], [[0, 8 * V]], 0, 0)
     dma("s", ["ul0"], ["wq"], raw(T.wq[:]), T.wc[:])
     dma("s", [], ["wp"], T.wp[:], T.ws[:])
     dma("s", [], ["vt"], T.vt[:], T.v[:])
-    zero(T.ct, 0, 1024, ["ct0", "ct1"])
     for k in range(NS):
         own_mm(0, k)
         own_row(k)
+        for i in range(4 * k, 4 * k + 3):
+            every16(i, "a")
         own_windows(k)
-    zero(T.mt, 0, 4 * C, ["mta", "mtb"])
-    zero(T.x1, 4 * C, 4 * XW, ["x1z"])
-    zero(T.yt, 4 * C, 4 * XW, ["ytz"])
     ts(CY, CY, -64.0, None, ALU.add, None, ["cy0"], ["cy"])
-    ts(T.cc[:], T.ca[:], T3, None, ALU.mult, None, ["ca", "t3"], ["cc"])
     ts(T.yc[:], T.ya[:], T4, None, ALU.mult, None, ["ya", "t4"], ["yc"])
     fill(T.rst[:, 0:ST * SG:SG], BIG, ["rst"])
-    ts(T.ma[:], T.im[:], PL, None, ALU.add, None, ["im", "pl"], ["ma"])
-    tt(T.cd[:], T.cc[:], T.cb[:], ALU.add, ["cc", "cb"], ["cdd"])
-    tt(T.yd[:], T.yc[:], T.yb[:], ALU.add, ["yc", "yb"], ["yd"])
+    ts(T.ma[:], T.im[:], PL, -16.0, ALU.add, ALU.add, ["im", "pl"], ["ma"])
     tiles = keys("et", 4)
     for b in range(4):
         ts(T.et[:, 512 * b:512 * (b + 1)], T.ie[:], float(b), None, ALU.is_equal, None, ["ie"], ["et%d" % b])
         if b == 0:
-            ts(T.ma[:], T.ma[:], -16.5, 1.0 / SG, ALU.add, ALU.mult, ["ma"], ["ma"])
-        if b == 1:
-            cp(T.mb[:], T.ma[:], ["ma"], ["mb"])
-    ts(T.lm[:], T.mb[:], float(SG), float(NO), ALU.mult, ALU.add, ["mb"], ["lm"])
+            ts(T.mb[:], T.ma[:], 1.0 / SG, None, ALU.mult, None, ["ma"], ["mb"])
+    ts(T.lm[:], T.mb[:], float(SG), SG - 1.0, ALU.mult, ALU.add, ["mb"], ["lm"])
+    tt(T.yd[:], T.yc[:], T.yb[:], ALU.add, ["yc", "yb"], ["yd"])
     ts(T.ct[:, 0:512:4], T.ic[:], 8.0, PL, ALU.add, ALU.is_equal, ["ic", "pl"], ["ct0"])
     ts(T.ct[:, 512:1024:4], T.ic[:], PL, None, ALU.is_equal, None, ["ic", "pl"], ["ct1"])
-    quant(T.eq[:], T.es[:], T.et[:], tiles, ["eq"])
-    quant(T.cq[:], T.cs[:], T.ct[:], ["ct0", "ct1"], ["cq"])
-    for i in range(16):
-        every16(i)
+    for i in (3, 7, 11, 12, 13, 14, 15):
+        every16(i, "v")
     spread_u(0)
 
     def late():
+        quant(T.eq[:], T.es[:], T.et[:], tiles, ["eq"])
+        quant(T.cq[:], T.cs[:], T.ct[:], ["ct0", "ct1"], ["cq"])
+
+    def last():
         for k in (0, 2):
             a, z = PLACE[k] // 4, (PLACE[k] + CUT[k + 1] - CUT[k]) // 4
-            ts(T.iy[:, a:z], T.iy[:, a:z], -float(PLACE[k]), None, ALU.add, None, ["iy"], ["iy%d" % k])
+            act(T.iy[:, a:z], T.iy[:, a:z], ACT.Identity, ["iy"], ["iy%d" % k], bias=-float(PLACE[k]))
+        evac_p(0)
         for i in range(4):
-            ts(T.ky[:, i:C:4], T.iy[:], T.ya[:, i:i + 1], T.yd[:, i:i + 1], ALU.mult, ALU.add, ["iy", "iy0", "iy2", "ya", "yd"], ["ky%d" % i])
+            act(T.ky[:, i:C:4], T.iy[:], ACT.Identity, ["iy", "iy0", "iy2", "ya", "yd"], ["ky%d" % i],
+                scale=T.ya[:, i:i + 1], bias=T.yd[:, i:i + 1])
 
     def diffs(a, b):
         for n in range(a, b):
             s, q = divmod(n, ST)
             o = 64 * s
-            act(T.dd[:, SG * n + 1:SG * n + SG], T.ba[:, o + q:o + q + NO], ACT.Abs, ["ba%d" % s], ["dd%d" % n],
+            act(T.dd[:, SG * n:SG * n + SG], T.ba[:, o + q:o + q + SG], ACT.Abs, ["ba%d" % s], ["dd%d" % n],
                 bias=T.ba[:, o + 48 + q:o + 49 + q], scale=-1.0)
 
     def least(a, b):
         scan(T.pm[:, SG * a:SG * b], T.rst[:, 0:SG * (b - a)], T.dd[:, SG * a:SG * b], 0.0, ALU.add, ALU.min,
-             ["rst", "fill"] + slots("dd", a, b), slots("pm", a, b))
+             ["rst"] + slots("dd", a, b), slots("pm", a, b))
 
     def above(a, b):
-        w = 8 if b - a <= 8 else ST
+        w = ST
         c = (w - b + a) * SG // 32 * 2
         lo = SG * (b - w) + 16 * c
         tt(T.gt[:, lo + b * 8:SG * b + b * 8], T.pm[:, SG * (b - w):SG * b].indirect(T.lm[:, c:w * SG // 16]), T.dd[:, lo:SG * b],
-           ALU.not_equal, slots("pm", b - w, b) + slots("dd", b - w, b) + ["lm", "fill"], ["gt%d" % b])
+           ALU.not_equal, slots("pm", b - w, b) + slots("dd", b - w, b) + ["lm"], ["gt%d" % b])
 
     def back(t, a, b):
         return t[:, b - 1:a - 1:-1] if a else t[:, b - 1::-1]
@@ -457,8 +452,8 @@ def rank_program(g, core, T, topo):
 
     def signs(a, b):
         for n in range(a, b):
-            act(T.sj[:, SG * n + 1:SG * n + SG], T.pm[:, SG * n + 1:SG * n + SG], ACT.Sign, ["pm%d" % n], ["acc%d" % n],
-                bias=T.pm[:, SG * n + NO:SG * n + SG], scale=-1.0, accum_out=T.acc[:, n:n + 1])
+            act(T.sj[:, SG * n:SG * n + SG], T.pm[:, SG * n:SG * n + SG], ACT.Sign, ["pm%d" % n], ["acc%d" % n],
+                bias=T.pm[:, SG * n + SG - 1:SG * n + SG], scale=-1.0, accum_out=T.acc[:, n:n + 1])
 
     def counted(a, b):
         act(T.cnt[:, SG * a:SG * b:SG], T.acc[:, a:b], ACT.Identity, slots("acc", a, b), slots("cnt", a, b),
@@ -592,82 +587,92 @@ def rank_program(g, core, T, topo):
             own_windows(k)
             return
         a, z = CUT[k], CUT[k + 1]
-        act(T.yo[:, a:z], bank(7, z - a, a - behind(k)[0]), ACT.Copy, ["ps7"], ["yo%d" % k])
-        put("a" if k == NS - 1 else "s", ["yo%d" % k], T.y[:, PLACE[k]:PLACE[k] + z - a], T.yo[:, a:z])
+        if k == NS - 1:
+            cp(T.yo[:, a:z], bank(7, z - a, a - behind(k)[0]), ["ps7"], ["yo%d" % k])
+        else:
+            act(T.yo[:, a:z], bank(7, z - a, a - behind(k)[0]), ACT.Copy, ["ps7"], ["yo%d" % k])
+        if k == 0:
+            put("s", ["yo0"], T.y[:, PLACE[0]:C], T.yo[:, a:z])
+        elif k == NS - 1:
+            put("a", ["yo1", "yo2"], T.y[:, 0:PLACE[0]], T.yo[:, CUT[1]:C])
 
     for r in range(R):
-        far_mm(r, 0, 4)
         far_mm(r, 0, 5)
+        far_mm(r, 0, 4)
         far_row(0, 4, 0, "v")
         far_row(0, 5, 1, "a")
-        windows(0)
         if r > 0:
             rows(r, NS - 1)
-        else:
+        windows(0)
+        if r == 0:
             late()
-        for s in range(NS - 1):
-            a, m, z = ST * s, ST * s + SC[s], ST * (s + 1)
-            diffs(a, m)
-            least(a, m)
-            far_mm(r, s + 1, 6 - s)
-            far_row(s + 1, 6 - s, 0, "v")
-            far_row(s + 1, 6 - s, 1, "v")
-            if s > 0:
-                tally(ST * (s - 1) + SC[s - 1], a)
-            windows(s + 1)
-            diffs(m, m + 3)
-            if s > 0:
-                counted(ST * (s - 1), ST * (s - 1) + SC[s - 1])
-            diffs(m + 3, z)
-            least(m, z)
-            signs(a, m)
-            above(m, z)
-        a, (m, e), z = 2 * ST, LAST, 3 * ST
-        diffs(a, a + 3)
-        counted(ST, ST + SC[1])
-        diffs(a + 3, m)
-        tally(ST + SC[1], a)
-        least(a, m)
-        diffs(m, e)
-        unpack(T["lq%d" % r], T["ls%d" % r], landed(r, 0, C))
+        if r == R - 1:
+            quant(T.vq[:], T.vs[:], T.vt[:], ["vt"], ["vq"])
+        diffs(0, 6)
+        least(0, 6)
+        diffs(6, 16)
+        far_rows(r, 1)
+        signs(0, 6)
+        windows(1)
+        least(6, 16)
+        near = r < R - 1
+        if near:
+            far_rows(r, 2)
+        diffs(16, 32)
+        above(6, 16)
+        counted(0, 6)
+        least(16, 22)
+        if near:
+            windows(2)
+        else:
+            far_rows(r, 2)
+        least(22, 32)
+        if not near:
+            windows(2)
+        signs(16, 22)
+        above(22, 32)
+        diffs(32, 38)
+        tally(6, 16)
+        tally(22, 32)
+        counted(16, 22)
+        diffs(38, 48)
+        least(32, 38)
         lay("a")
-        least(m, e)
-        diffs(e, z)
+        least(38, 44)
         pack("a")
-        least(e, z)
-        signs(a, m)
-        above(e, z)
-        signs(m, e)
+        unpack(T["lq%d" % r], T["ls%d" % r], landed(r, 0, C))
+        least(44, 48)
+        signs(32, 44)
+        above(44, 48)
         sixteenth("a")
-        tally(e, z)
-        counted(a, e)
+        tally(44, 48)
+        counted(32, 44)
         theirs("a")
         minus("a", "a")
-        lay("b")
         reach(240, C)
+        lay("b")
         reach(0, 112)
         pack("b")
-        for b in range(2):
-            evac_p(b)
+        if r == 0:
+            last()
+        else:
+            evac_p(0)
         check(0)
         check(1)
         sixteenth("b")
         theirs("b")
         minus("b", "v")
-        kept(256, C, 4, 16)
         reach(112, 240)
         other(256, C)
         other(0, 96)
-        kept(0, 96, 4, 144)
+        kept(256, C, 4, 16)
         check(2)
-        evac_p(2)
-        if r + 1 < R:
-            spread_u(r + 1)
-        else:
-            quant(T.vq[:], T.vs[:], T.vt[:], ["vt"], ["vq"])
+        evac_p(1)
+        kept(0, 96, 4, 144)
         other(96, 256)
-        kept(96, 240, 5, 0)
         kept(240, 256, 4, 0)
+        kept(96, 240, 5, 0)
+        evac_p(2)
         evac_p(3)
         act(T.pp[:, 0:4 * V], T.pp[:, 4 * C:4 * (C + V)], ACT.Copy, keys("pp", 4), ["ppa"])
         act(T.pp[:, 4 * (C + V):4 * XW], T.pp[:, 4 * V:8 * V], ACT.Copy, keys("pp", 4), ["ppz"])
@@ -711,8 +716,10 @@ def rank_program(g, core, T, topo):
         relus(2, 0, 1)
         scores(n, 1)
         relus(2, 1, 4)
-        rows(n, 1)
         adds(2, 0, 4)
+        if n < R:
+            spread_u(n)
+        rows(n, 1)
         quant_x(n, 2)
         onward(n, 2)
         scores(n, 2)

@@ -9,7 +9,7 @@ ST = 16
 NS = 3
 CUT = [0, 160, 288, 384]
 PLACE = [224, 0, 128]
-SUB = 80
+SUB = (32, 112, 160)
 BIG = 1e29
 CORES = 64
 NEAR = (0, 0, 0, 0)
@@ -41,12 +41,12 @@ for _n, _w, _t in [
         ("wq", 512, Q4), ("wp", 512, U8), ("hq", C, Q4), ("hs", C, U8), ("huq", 8, Q4), ("hus", 32, U8),
         ("pi", 8, I32), ("pa", 8, I32), ("pb", 8, I32), ("pc", 8, I32), ("pd", 8, I32),
         ("iw", 12, F32), ("im", SG, F32), ("ik", 24, F32), ("iy", 96, F32),
-        ("ie", 512, BF), ("ic", 128, F32), ("col", 24, F32), ("wb", 12, F32), ("wd", 12, F32),
+        ("ic", 128, F32), ("col", 24, F32), ("wb", 12, F32), ("wd", 12, F32),
         ("ma", SG, F32), ("mb", SG, I32), ("lm", SG, U16), ("crow", ST * SG, BF), ("rst", ST * SG, F32),
         ("ca", 16, F32), ("cb", 16, F32), ("cc", 16, F32), ("cd", 16, F32), ("ir", 24, F32), ("kd", C, F32),
         ("ya", 4, F32), ("yb", 4, F32), ("yc", 4, F32), ("yd", 4, F32), ("ky", C, BF),
         ("lu16", 8, U16), ("lu1", 8, U16), ("lw", 12, U16), ("la", 6, U16), ("lsc", 4, U16),
-        ("et", 2048, BF), ("eq", 512, Q4), ("es", 512, U8), ("ct", 1024, BF), ("cq", 256, Q4), ("cs", 256, U8),
+        ("et", 516, BF), ("eq", 512, Q4), ("es", 512, U8), ("ct", 1024, BF), ("cq", 256, Q4), ("cs", 256, U8),
         ("ow", C, F32), ("pw", 2 * C, F32), ("og", 192, F32), ("ba", 192, F32),
         ("dd", 48 * SG, F32), ("pm", 48 * SG, F32), ("gt", 48 * (SG + 8), BF), ("cnt", 48 * SG, BF), ("sj", 48 * SG, BF), ("acc", 48, F32),
         ("mt", 4 * C, BF), ("mq", C, Q4), ("ms", C, U8),
@@ -278,16 +278,21 @@ def rank_program(g, core, T, topo):
         a, b = behind(k)
         mm(7, b - a, T.urq[:], T.urs[:], T["qx%d" % r][:, a:b], T["sx%d" % r][:, a:b], ["urq", "urs"] + xkeys(r, a, b))
 
-    def own_row(k):
+    def own_row(k, q="a"):
         a, b = CUT[k], CUT[k + 1]
-        act(T.ow[:, a:b], bank(7, b - a, a - behind(k)[0]), ACT.Copy, ["ps7"], ["ow%d" % k])
+        if q == "a":
+            act(T.ow[:, a:b], bank(7, b - a, a - behind(k)[0]), ACT.Copy, ["ps7"], ["ow%d" % k])
+        else:
+            cp(T.ow[:, a:b], bank(7, b - a, a - behind(k)[0]), ["ps7"], ["ow%d" % k])
 
-    def own_windows(s):
+    def own_windows(s, q="a"):
         row = T.ow[:, 0:CUT[s + 1]]
-        act(T.og[:, 64 * s:64 * s + 48], row.indirect(T.lw[:, 4 * s:4 * s + 3]), ACT.Identity,
-            keys("ow", s + 1) + ["lw", "mask"], ["ogb%d" % s], scale=M1)
-        act(T.og[:, 64 * s + 48:64 * s + 64], row.indirect(T.la[:, 2 * s:2 * s + 1]), ACT.Identity,
-            keys("ow", s + 1) + ["la", "mask"], ["oga%d" % s], scale=M0)
+        for a, z, off, m, w in ((0, 48, T.lw[:, 4 * s:4 * s + 3], M1, "ogb%d" % s), (48, 64, T.la[:, 2 * s:2 * s + 1], M0, "oga%d" % s)):
+            out, r = T.og[:, 64 * s + a:64 * s + z], keys("ow", s + 1) + ["lw", "la", "mask"]
+            if q == "a":
+                act(out, row.indirect(off), ACT.Identity, r, [w], scale=m)
+            else:
+                ts(out, row.indirect(off), m, None, ALU.mult, None, r, [w])
 
     def far_mm(r, k, b):
         a, z = behind(k)
@@ -312,15 +317,12 @@ def rank_program(g, core, T, topo):
            ["pw0", "pw1", "lw", "ogb%d" % s, "oga%d" % s], ["ba%d" % s])
 
     def zero(t, a, z, w):
-        for i in range(a, z, 512):
-            n = min(512, z - i)
-            act(t[:, i:i + n], T.ie[:, 0:n], ACT.Identity, ["ie"], w if i + n == z else [], scale=0.0)
+        for i in range(a, z, ST * SG):
+            n = min(ST * SG, z - i)
+            act(t[:, i:i + n], T.crow[:, 0:n], ACT.Identity, ["crow"], w if i + n == z else [], scale=0.0)
 
-    def every16(i, q):
-        if q == "v":
-            ts(T.kd[:, i:C:16], T.ir[:], T.ca[:, i:i + 1], T.cd[:, i:i + 1], ALU.mult, ALU.add, keys("ir", 3) + ["ca", "cdd"], ["kd%d" % i])
-        else:
-            act(T.kd[:, i:C:16], T.ir[:], ACT.Identity, keys("ir", 3) + ["ca", "cdd"], ["kd%d" % i], scale=T.ca[:, i:i + 1], bias=T.cd[:, i:i + 1])
+    def every16(i):
+        act(T.kd[:, i:C:16], T.ir[:], ACT.Identity, keys("ir", 3) + ["ca", "cdd"], ["kd%d" % i], scale=T.ca[:, i:i + 1], bias=T.cd[:, i:i + 1])
 
     CHECK = [(256, C), (0, 96), (96, 256)]
 
@@ -328,93 +330,101 @@ def rank_program(g, core, T, topo):
     dma("s", [], ["ut"], T.ut[:], T.u[:])
     dma("s", [], ["x01"], T.x0[:, 4 * CUT[1]:4 * C], T.x[:, 0:4 * PLACE[0]])
     iota("pi", T.pi[:], [[0, 8]], 0, 1)
-    iota("iw", T.iw[:], [[128, 3], [16, 4]], 0, 1)
     iota("ik", T.ik[:], [[1, 24]], 0, 0)
+    iota("iw", T.iw[:], [[128, 3], [16, 4]], 0, 1)
     iota("im", T.im[:], [[16, SG]], 0, 0)
     iota("ic", T.ic[:], [[1, 8], [0, 16]], 0, 0)
     fill(T.crow[:], 1.0, ["crow"])
-    ts(T5, T.pi[:, 0:1], -4.0, -1.0, ALU.mult, ALU.add, ["pi"], ["t5"])
-    ts(T.pb[:], T.pi[:], 7, None, ALU.bitwise_and, None, ["pi"], ["pb"])
+    op("g", ["crow"], ["et"], lambda e: e.affine_select(T.et[:], T.crow[:, 0:516], [[1, 516]], ALU.is_equal, 0.0, -3, -4))
     ts(T.pa[:], T.pi[:], 15, None, ALU.bitwise_and, None, ["pi"], ["pa"])
-    scan(T.ie[:], T.crow[:, 0:512], T.crow[:, 0:512], T5, ALU.mult, ALU.add, ["crow", "t5"], ["ie"])
-    ts(T.pc[:], T.pi[:], 3, None, ALU.bitwise_and, None, ["pi"], ["pc"])
-    ts(T.pd[:], T.pi[:], 2, 3, ALU.arith_shift_right, ALU.bitwise_and, ["pi"], ["pd"])
-    ts(T.lu16[:], T.pb[:], 16.0, None, ALU.mult, None, ["pb"], ["lu16"])
+    ts(T.pb[:], T.pi[:], 7, None, ALU.bitwise_and, None, ["pi"], ["pb"])
     cp(PL, T.pa[:, 0:1], ["pa"], ["pl"])
-    cp(T.lu1[:], T.pb[:], ["pb"], ["lu1"])
-    cp(PB, T.pc[:, 0:1], ["pc"], ["pbc"])
-    cp(PA, T.pd[:, 0:1], ["pd"], ["pac"])
-    ts(T.lsc[:, 0:3], T.iw[:, 0:12:4], 4.0, None, ALU.mult, None, ["iw"], ["lsc"])
-    ts(M0, PL, 8.0, None, ALU.is_lt, None, ["pl"], ["m0"])
-    ts(T.iw[:, 3:12:4], T.iw[:, 3:12:4], -32.0, None, ALU.add, None, ["iw"], ["iw"])
-    ts(M1, PL, 8.0, None, ALU.is_ge, None, ["pl", "m0"], ["mask"])
-    fill(T.crow[:, 0:ST * SG:SG], -float(V), ["crow"])
-    ts(T.wb[:], T.iw[:], float(C), -float(C), ALU.is_ge, ALU.mult, ["iw"], ["wb"])
     ts(T1, PL, 0.0, 16.0, ALU.is_equal, ALU.mult, ["pl"], ["t1"])
-    ts(T2, PA, 0.0, 4.0, ALU.is_equal, ALU.mult, ["pac"], ["t2"])
-    tt(T.wd[:], T.iw[:], T.wb[:], ALU.add, ["iw", "wb"], ["wd"])
     ts(T.ca[:], T.ik[:, 0:16], PL, None, ALU.is_equal, None, ["ik", "pl"], ["ca"])
+    ts(T3, PL, 80.0, None, ALU.add, None, ["pl"], ["t3"])
+    ts(T.lu16[:], T.pb[:], 16.0, None, ALU.mult, None, ["pb"], ["lu16"])
     ts(PM, PL, T1, -1.0, ALU.add, ALU.add, ["pl", "t1"], ["pm"])
-    cp(T.lw[:], T.wd[:], ["wd"], ["lw"])
-    cp(T.la[:, 0:6:2], T.wd[:, 3:12:4], ["wd"], ["la"])
+    ts(T.cc[:], T.ca[:], T3, None, ALU.mult, None, ["ca", "t3"], ["cc"])
+    ts(T.lsc[:, 0:3], T.iw[:, 0:12:4], 4.0, None, ALU.mult, None, ["iw"], ["lsc"])
+    ts(T.cb[:], T.ik[:, 0:16], PM, -1024.0, ALU.is_equal, ALU.mult, ["ik", "pm"], ["cb"])
+    for i, (a, z) in enumerate(CHECK):
+        ts(T.ir[:, a // 16:z // 16], T.ik[:, a // 16:z // 16], 16.0, -float(a), ALU.mult, ALU.add, ["ik"], ["ir%d" % i])
     zero(T.pw, 0, 2 * C, ["pw0", "pw1"])
     zero(T.rst, 0, ST * SG, ["rst"])
-    zero(T.ct, 0, 1024, ["ct0", "ct1"])
     quant(T.qx0[:, 0:CUT[1]], T.sx0[:, 0:CUT[1]], T.x0[:, 0:4 * CUT[1]], ["x00"], ["qx00"])
+    tt(T.cd[:], T.cc[:], T.cb[:], ALU.add, ["cc", "cb"], ["cdd"])
+    ts(M0, PL, 8.0, None, ALU.is_lt, None, ["pl"], ["m0"])
+    ts(T.iw[:, 3:12:4], T.iw[:, 3:12:4], -32.0, None, ALU.add, None, ["iw"], ["iw"])
+    act(T.rst[:, 0:ST * SG:SG], T.rst[:, 0:ST * SG:SG], ACT.Identity, ["rst"], ["rst"], bias=BIG)
+    zero(T.ct, 0, 512, ["ct0"])
     quant(T.uq[:], T.us[:], T.ut[:], ["ut"], ["uq"])
-    ts(T.lw[:, 3:12:4], T.wd[:, 3:12:4], float(C), None, ALU.add, None, ["wd"], ["lw"])
-    ts(AM, PA, T2, -1.0, ALU.add, ALU.add, ["pac", "t2"], ["am"])
+    ts(T.wb[:], T.iw[:], float(C), -float(C), ALU.is_ge, ALU.mult, ["iw"], ["wb"])
+    ts(M1, PL, 8.0, None, ALU.is_ge, None, ["pl", "m0"], ["mask"])
     cp(words(T.urq[:]), words(T.uq[:]).indirect(T.lu16[:]), ["uq", "lu16"], ["urq"])
     act(T.urs[:], T.us[:].indirect(T.lu16[:]), ACT.Copy, ["uq", "lu16"], ["urs"])
     ship(0, 0, lambda: ship_u(0))
-    ts(CD, T1, 64.0, -64.0, ALU.mult, ALU.add, ["t1"], ["cd"])
-    ts(CY, T2, 224.0, PB, ALU.mult, ALU.add, ["t2", "pbc"], ["cy0"])
-    ts(T.cb[:], T.ik[:, 0:16], PM, -1024.0, ALU.is_equal, ALU.mult, ["ik", "pm"], ["cb"])
-    ts(T3, PL, 80.0, None, ALU.add, None, ["pl"], ["t3"])
-    ts(T.ya[:], T.ik[:, 0:4], PA, None, ALU.is_equal, None, ["ik", "pac"], ["ya"])
-    ts(T.yb[:], T.ik[:, 0:4], AM, -224.0, ALU.is_equal, ALU.mult, ["ik", "am"], ["yb"])
-    ts(T4, PA, 32.0, None, ALU.add, None, ["pac"], ["t4"])
-    ts(T.cc[:], T.ca[:], T3, None, ALU.mult, None, ["ca", "t3"], ["cc"])
-    for i, (a, z) in enumerate(CHECK):
-        ts(T.ir[:, a // 16:z // 16], T.ik[:, a // 16:z // 16], 16.0, -float(a), ALU.mult, ALU.add, ["ik"], ["ir%d" % i])
-    tt(T.cd[:], T.cc[:], T.cb[:], ALU.add, ["cc", "cb"], ["cdd"])
+    iota("crow", T.crow[:, 0:ST * SG:SG], [[0, ST]], -V, 0)
+    tt(T.wd[:], T.iw[:], T.wb[:], ALU.add, ["iw", "wb"], ["wd"])
+    cp(T.lu1[:], T.pb[:], ["pb"], ["lu1"])
+    ts(T.ma[:], T.im[:], PL, -16.0, ALU.add, ALU.add, ["im", "pl"], ["ma"])
+    cp(T.lw[:], T.wd[:], ["wd"], ["lw"])
+    cp(T.la[:, 0:6:2], T.wd[:, 3:12:4], ["wd"], ["la"])
+    for b in range(4):
+        quant(T.eq[:, 128 * b:128 * b + 128], T.es[:, 128 * b:128 * b + 128], T.et[:, 3 - b:515 - b], ["et"], ["eq%d" % b])
+        if b == 0:
+            ts(T.lw[:, 3:12:4], T.wd[:, 3:12:4], float(C), None, ALU.add, None, ["wd"], ["lw"])
     quant(T.qx0[:, CUT[1]:C], T.sx0[:, CUT[1]:C], T.x0[:, 4 * CUT[1]:4 * C], ["x01"], ["qx01", "qx02"])
     ship(0, 1)
+    iota("mta", T.mt[:], [[0, 4 * C]], 0, 0)
     ship_u(1)
     ship_u(2)
     iota("iy", T.iy[:], [[4, 96]], 0, 0)
-    iota("mta", T.mt[:], [[0, 4 * C]], 0, 0)
     iota("x1z", T.x1[:, 4 * C:4 * XW], [[0, 8 * V]], 0, 0)
     iota("ytz", T.yt[:, 4 * C:4 * XW], [[0, 8 * V]], 0, 0)
     dma("s", ["ul0"], ["wq"], raw(T.wq[:]), T.wc[:])
     dma("s", [], ["wp"], T.wp[:], T.ws[:])
     dma("s", [], ["vt"], T.vt[:], T.v[:])
-    for k in range(NS):
-        own_mm(0, k)
-        own_row(k)
-        for i in range(4 * k, 4 * k + 3):
-            every16(i, "a")
-        own_windows(k)
-    ts(CY, CY, -64.0, None, ALU.add, None, ["cy0"], ["cy"])
-    ts(T.yc[:], T.ya[:], T4, None, ALU.mult, None, ["ya", "t4"], ["yc"])
-    fill(T.rst[:, 0:ST * SG:SG], BIG, ["rst"])
-    ts(T.ma[:], T.im[:], PL, -16.0, ALU.add, ALU.add, ["im", "pl"], ["ma"])
-    tiles = keys("et", 4)
-    for b in range(4):
-        ts(T.et[:, 512 * b:512 * (b + 1)], T.ie[:], float(b), None, ALU.is_equal, None, ["ie"], ["et%d" % b])
-        if b == 0:
-            ts(T.mb[:], T.ma[:], 1.0 / SG, None, ALU.mult, None, ["ma"], ["mb"])
-    ts(T.lm[:], T.mb[:], float(SG), SG - 1.0, ALU.mult, ALU.add, ["mb"], ["lm"])
-    tt(T.yd[:], T.yc[:], T.yb[:], ALU.add, ["yc", "yb"], ["yd"])
+    own_mm(0, 0)
+    for i in range(6):
+        every16(i)
+    own_row(0)
+    for i in range(6, 9):
+        every16(i)
+    own_windows(0)
+    zero(T.ct, 512, 1024, ["ct1"])
+    own_mm(0, 1)
+    ts(T.mb[:], T.ma[:], 1.0 / SG, None, ALU.mult, None, ["ma"], ["mb"])
     ts(T.ct[:, 0:512:4], T.ic[:], 8.0, PL, ALU.add, ALU.is_equal, ["ic", "pl"], ["ct0"])
-    ts(T.ct[:, 512:1024:4], T.ic[:], PL, None, ALU.is_equal, None, ["ic", "pl"], ["ct1"])
-    for i in (3, 7, 11, 12, 13, 14, 15):
-        every16(i, "v")
     spread_u(0)
+    for i in range(9, 16):
+        every16(i)
+    ts(T.ct[:, 512:1024:4], T.ic[:], PL, None, ALU.is_equal, None, ["ic", "pl"], ["ct1"])
+    ts(T.lm[:], T.mb[:], float(SG), SG - 1.0, ALU.mult, ALU.add, ["mb"], ["lm"])
+    ts(T.pd[:], T.pi[:], 2, 3, ALU.arith_shift_right, ALU.bitwise_and, ["pi"], ["pd"])
 
-    def late():
-        quant(T.eq[:], T.es[:], T.et[:], tiles, ["eq"])
-        quant(T.cq[:], T.cs[:], T.ct[:], ["ct0", "ct1"], ["cq"])
+    def later(i):
+        if i == 0:
+            cp(PA, T.pd[:, 0:1], ["pd"], ["pac"])
+            ts(T.pc[:], T.pi[:], 3, None, ALU.bitwise_and, None, ["pi"], ["pc"])
+        elif i == 1:
+            ts(T2, PA, 0.0, 4.0, ALU.is_equal, ALU.mult, ["pac"], ["t2"])
+            own_mm(0, NS - 1)
+            own_row(NS - 1, "v")
+            quant(T.cq[:], T.cs[:], T.ct[:], ["ct0", "ct1"], ["cq"])
+            own_windows(NS - 1, "v")
+            ts(PB, T.pc[:, 0:1], -64.0, None, ALU.add, None, ["pc"], ["pbc"])
+        elif i == 2:
+            ts(AM, PA, T2, -1.0, ALU.add, ALU.add, ["pac", "t2"], ["am"])
+            ts(T4, PA, 32.0, None, ALU.add, None, ["pac"], ["t4"])
+        elif i == 3:
+            ts(T.ya[:], T.ik[:, 0:4], PA, None, ALU.is_equal, None, ["ik", "pac"], ["ya"])
+            ts(T.yb[:], T.ik[:, 0:4], AM, -224.0, ALU.is_equal, ALU.mult, ["ik", "am"], ["yb"])
+        elif i == 4:
+            ts(T.yc[:], T.ya[:], T4, None, ALU.mult, None, ["ya", "t4"], ["yc"])
+            ts(CD, T1, 64.0, -64.0, ALU.mult, ALU.add, ["t1"], ["cd"])
+        else:
+            tt(T.yd[:], T.yc[:], T.yb[:], ALU.add, ["yc", "yb"], ["yd"])
+            ts(CY, T2, 224.0, PB, ALU.mult, ALU.add, ["t2", "pbc"], ["cy"])
 
     def last():
         for k in (0, 2):
@@ -507,7 +517,7 @@ def rank_program(g, core, T, topo):
 
     def unpack(q, s, r):
         for b in range(4):
-            mm(b, C, T.eq[:, 128 * b:128 * b + 128], T.es[:, 128 * b:128 * b + 128], q[:, 0:C], s[:, 0:C], ["eq"] + r)
+            mm(b, C, T.eq[:, 128 * b:128 * b + 128], T.es[:, 128 * b:128 * b + 128], q[:, 0:C], s[:, 0:C], ["eq%d" % b] + r)
 
     def evac_p(b):
         act(T.pp[:, 4 * V + b:4 * (V + C):4], bank(b, C), ACT.Identity, ["ps%d" % b], ["pp%d" % b], scale=0.5)
@@ -601,11 +611,12 @@ def rank_program(g, core, T, topo):
         far_mm(r, 0, 4)
         far_row(0, 4, 0, "v")
         far_row(0, 5, 1, "a")
-        if r > 0:
-            rows(r, NS - 1)
+        rows(r, NS - 1 if r else 1)
+        if r == 0:
+            later(0)
         windows(0)
         if r == 0:
-            late()
+            later(1)
         if r == R - 1:
             quant(T.vq[:], T.vs[:], T.vt[:], ["vt"], ["vq"])
         diffs(0, 6)
@@ -613,36 +624,44 @@ def rank_program(g, core, T, topo):
         diffs(6, 16)
         far_rows(r, 1)
         signs(0, 6)
+        if r == 0:
+            later(2)
         windows(1)
         least(6, 16)
-        near = r < R - 1
+        near = topo.chip(mate[r]) == topo.chip(core)
         if near:
             far_rows(r, 2)
         diffs(16, 32)
         above(6, 16)
         counted(0, 6)
-        least(16, 22)
+        least(16, 23)
         if near:
             windows(2)
         else:
             far_rows(r, 2)
-        least(22, 32)
+        if r == 0:
+            later(3)
+        least(23, 32)
         if not near:
             windows(2)
-        signs(16, 22)
-        above(22, 32)
+        unpack(T["lq%d" % r], T["ls%d" % r], landed(r, 0, C))
+        signs(16, 23)
+        if r == 0:
+            later(4)
+        above(23, 32)
         diffs(32, 38)
         tally(6, 16)
-        tally(22, 32)
-        counted(16, 22)
+        tally(23, 32)
+        counted(16, 23)
         diffs(38, 48)
         least(32, 38)
         lay("a")
         least(38, 44)
         pack("a")
-        unpack(T["lq%d" % r], T["ls%d" % r], landed(r, 0, C))
         least(44, 48)
         signs(32, 44)
+        if r == 0:
+            later(5)
         above(44, 48)
         sixteenth("a")
         tally(44, 48)
@@ -688,10 +707,14 @@ def rank_program(g, core, T, topo):
         if r == R - 1:
             dma("g", ["l", "h"], [], T.od[:], T.lh[0:128:16, :])
         n = r + 1
-        take_h(0, 0, SUB)
+        a, m, z = SUB
+        take_h(0, 0, a)
+        take_h(0, a, m)
         take_h(1, CUT[1], CUT[2])
-        take_h(0, SUB, CUT[1], "v")
-        take_l(0, 0, CUT[1])
+        take_h(0, m, z, "v")
+        take_l(0, 0, a)
+        take_l(0, m, z)
+        take_l(0, a, m)
         take_h(2, CUT[2], CUT[3])
         quant_y(0)
         layers(0)

@@ -3,19 +3,44 @@ from concourse.mybir import dt, AluOpType, ActivationFunctionType
 ALU = AluOpType
 ACT = ActivationFunctionType
 C, V, R = 384, 16, 3
-SG = 2 * V + 1
 XW = C + 2 * V
-ST = 16
-NS = 3
+NB = C // 16
+W = 3 * V
 CUT = [0, 160, 288, 384]
-PLACE = [224, 0, 128]
-SUB = (32, 112, 160)
-BIG = 1e29
+NS = len(CUT) - 1
+PAD = max(C, CUT[NS - 1] + 128)
+STATE = "m0 l0 m1 s0 l1 m2 t0 s1 l2 t1 s2 t2".split()
+TELL = "aav"
+TAKES = [(0, 32, "a"), (32, 112, "a"), (112, 160, "v"), (160, 288, "a"), (288, 384, "a")]
+PARTS = [(0, 10), (10, 18), (18, 24)]
+BOTH = 24
+MATCH = [[(1, 4, "a"), (4, 10, "a"), (0, 1, "a")], [(10, 14, "a"), (14, 18, "a")], [(18, 20, "a"), (20, 22, "a"), (22, 24, "v")]]
+OWN = [[], [], []]
+CHECK = [[], [], [(0, 10), (10, 18), (18, 24)]]
+THEIRS = "aav"
+EVAC = "avav"
+ONE = 6
+AT, END, TURNED = [], [], []
+for _k in range(NS):
+    _a, _z = CUT[_k], CUT[_k + 1]
+    AT.append((END[-1] + 7) // 8 * 8 if END else 0)
+    _c = AT[-1] + (_z - _a) // 16
+    _f = max(_a, (16 * BOTH - V) // 32 * 32)
+    TURNED.append([])
+    for _x, _y, _o in [(0, 32, C + V)] * (_k == 0) + [(_f, _z, _f + V)] * (_f < _z):
+        if BOTH < NB:
+            TURNED[-1].append((_x, _y, _c, _o))
+            _c += (_y - _x) // 16
+    END.append(_c)
+DW = (END[-1] + 7) // 8 * 8
+BIG = 2.0 ** 90
+TIMES = (0.00083, 0.2, 0.3, 1.8, 1.55, 1e-9, 3, 1.5)
+CYCLE, WAKE, ISSUE, HOP, DMA, SLACK, TURNS, FIRST = TIMES
 CORES = 64
 NEAR = (0, 0, 0, 0)
 RUNS = [[(0, 160, NEAR, NEAR), (160, 384, NEAR, NEAR)],
         [(0, 160, NEAR, NEAR), (160, 288, NEAR, NEAR), (288, 384, NEAR, NEAR)],
-        [(0, 160, (0, 0, 1, 2), (0, 1, 0, 1)), (160, 288, (1, 0, 2, 0), (0, 0, 1, 1)), (288, 384, (1, 1, 2, 2), (1, 0, 1, 1))]]
+        [(0, 160, (0, 1, 2, 2), (1, 1, 1, 1)), (160, 288, (1, 1, 2, 2), (1, 1, 1, 1)), (288, 384, NEAR, NEAR)]]
 Q4, U8, BF, F32, I32, U16 = "float8_e4m3fn_x4", "uint8", "bfloat16", "float32", "int32", "uint16"
 
 SCRATCH = {"ps": ("psum", [128, 4096], F32)}
@@ -26,40 +51,37 @@ def _sb(name, n, ty):
 
 
 for _r in range(R + 1):
-    _sb("qx%d" % _r, XW, Q4)
-    _sb("sx%d" % _r, XW, U8)
+    _sb("qx%d" % _r, PAD, Q4)
+    _sb("sx%d" % _r, PAD, U8)
 for _r in range(R):
     _sb("lq%d" % _r, C, Q4)
     _sb("ls%d" % _r, C, U8)
-    _sb("ulq%d" % _r, 8, Q4)
-    _sb("uls%d" % _r, 32, U8)
-    _sb("upq%d" % _r, 128, Q4)
-    _sb("ups%d" % _r, 128, U8)
 for _n, _w, _t in [
-        ("x0", 4 * C, BF), ("x1", 4 * XW, BF), ("ut", 512, BF), ("vt", 512, BF),
+        ("x0", 4 * C, BF), ("x1", 4 * PAD, BF), ("ut", 512, BF), ("vt", 512, BF),
         ("uq", 128, Q4), ("us", 128, U8), ("urq", 128, Q4), ("urs", 128, U8), ("vq", 128, Q4), ("vs", 128, U8),
-        ("wq", 512, Q4), ("wp", 512, U8), ("hq", C, Q4), ("hs", C, U8), ("huq", 8, Q4), ("hus", 32, U8),
-        ("pi", 8, I32), ("pa", 8, I32), ("pb", 8, I32), ("pc", 8, I32), ("pd", 8, I32),
-        ("iw", 12, F32), ("im", SG, F32), ("ik", 24, F32), ("iy", 96, F32),
-        ("ic", 128, F32), ("col", 24, F32), ("wb", 12, F32), ("wd", 12, F32),
-        ("ma", SG, F32), ("mb", SG, I32), ("lm", SG, U16), ("crow", ST * SG, BF), ("rst", ST * SG, F32),
-        ("ca", 16, F32), ("cb", 16, F32), ("cc", 16, F32), ("cd", 16, F32), ("ir", 24, F32), ("kd", C, F32),
+        ("wq", 512, Q4), ("wp", 512, U8), ("hq", C, Q4), ("hs", C, U8),
+        ("pi", 8, I32), ("pa", 8, I32), ("pc", 8, I32), ("pd", 8, I32), ("li", 8, I32), ("lu", 8, U16),
+        ("ik", 24, F32), ("iy", 96, F32), ("col", 24, F32), ("i16", 160, F32), ("dm", 160, F32), ("rs", 160, F32),
+        ("t48", 8 * W, F32), ("ta", 8 * W, F32), ("mk", 8 * W, F32), ("rst", 8 * W, F32), ("one", 516, BF),
+        ("c1", NB, F32), ("cyc", 512, BF), ("cdv", W, BF),
         ("ya", 4, F32), ("yb", 4, F32), ("yc", 4, F32), ("yd", 4, F32), ("ky", C, BF),
-        ("lu16", 8, U16), ("lu1", 8, U16), ("lw", 12, U16), ("la", 6, U16), ("lsc", 4, U16),
-        ("et", 516, BF), ("eq", 512, Q4), ("es", 512, U8), ("ct", 1024, BF), ("cq", 256, Q4), ("cs", 256, U8),
-        ("ow", C, F32), ("pw", 2 * C, F32), ("og", 192, F32), ("ba", 192, F32),
-        ("dd", 48 * SG, F32), ("pm", 48 * SG, F32), ("gt", 48 * (SG + 8), BF), ("cnt", 48 * SG, BF), ("sj", 48 * SG, BF), ("acc", 48, F32),
-        ("mt", 4 * C, BF), ("mq", C, Q4), ("ms", C, U8),
-        ("dpx", XW, BF), ("nd", C, BF), ("exd", C, F32), ("exh", C, BF), ("exl", C, BF),
-        ("fd", 24, U16), ("fh", 96, U16), ("fl", 96, U16),
+        ("et", 516, BF), ("eq", 512, Q4), ("es", 512, U8),
+        ("msk", C, F32), ("hold", C, F32), ("dgs", R * DW, F32), ("dgl", R * DW, F32), ("ow", XW, F32),
+        ("tr", C, F32), ("bc", C, F32), ("fw", XW + V, F32), ("lj", NB, U16), ("mm", 2 * NB, U16),
+        ("dd", 2 * NB * W, F32), ("pm", 2 * NB * W + 1, F32), ("p2", 2 * NB * W, F32), ("sj", 2 * NB * W, BF),
+        ("nf", 2 * NB * W, BF), ("cnt", 2 * NB * W, BF),
+        ("acc", 2 * NB, F32), ("pf", 2 * NB, F32), ("mo", 2 * R * NB, U16), ("ml", 2 * R * NB, U16), ("rp", XW + V, BF),
+        ("exh", C, BF), ("exl", C, BF), ("fh", 96, U16), ("fl", 96, U16), ("ir", 96, F32),
         ("ok", C, BF), ("nok", C, BF), ("okd", C, BF), ("l1", C, BF), ("h1", C, BF), ("lh", 2 * C, BF),
-        ("pp", 4 * XW, BF), ("gh", 4 * C, BF), ("yt", 4 * XW, BF), ("yq", XW, Q4), ("ys", XW, U8),
+        ("pp", 4 * XW, BF), ("gh", 4 * C, BF), ("yt", 4 * C, BF), ("yq", PAD, Q4), ("ys", PAD, U8),
         ("rb", 4 * C, F32), ("yo", C, F32)]:
     _sb(_n, _w, _t)
 
-NDMA = 8
-SEMAPHORES = (["v", "a", "t", "g", "sent", "out", "hu0", "hu1"] + ["ua%d" % _r for _r in range(R)]
+NDMA = 9
+SEMAPHORES = (["v", "a", "t", "g", "sent", "out"]
               + ["xa%d%d" % (_r, _k) for _r in range(R) for _k in range(len(RUNS[_r]))]
+              + ["da%d%d" % (_r, _k) for _r in range(R) for _k in range(NS)]
+              + ["ma%d%d" % (_r, _k) for _r in range(R) for _k in range(len(PARTS))]
               + ["h%s%d" % (_c, _k) for _c in "cp" for _k in range(len(RUNS[R - 1]))] + ["d%d" % _k for _k in range(NDMA)])
 
 
@@ -77,10 +99,7 @@ def _helpers(T, topo, c, r):
 
 def _ways(T, topo, c, r):
     h = _helpers(T, topo, c, r)
-    to = {(k, i): h.get(run[2 + i][T.rank_of(c) % 4]) for k, run in enumerate(RUNS[r]) for i in range(2)}
-    used = sorted(set(x for x in to.values() if x is not None)) or [None]
-    to[-1, 0], to[-1, 1] = used[0], used[-1]
-    return to
+    return {(k, i): h.get(run[2 + i][T.rank_of(c) % 4]) for k, run in enumerate(RUNS[r]) for i in range(2)}
 
 
 def _send(g, T, topo, dst, en, out, in_, sem):
@@ -90,12 +109,8 @@ def _send(g, T, topo, dst, en, out, in_, sem):
 
 
 def _sides(T, r, k, i):
-    if k < 0:
-        names = ("urq", "huq", "ulq%d" % r) if i == 0 else ("urs", "hus", "uls%d" % r)
-        a, b, sems = 0, (8, 32)[i], ("hu%d" % i, "ua%d" % r)
-    else:
-        names = ("qx%d" % r, "hq", "lq%d" % r) if i == 0 else ("sx%d" % r, "hs", "ls%d" % r)
-        a, b, sems = RUNS[r][k][0], RUNS[r][k][1], ("h%s%d" % ("cp"[i], k), "xa%d%d" % (r, k))
+    names = ("qx%d" % r, "hq", "lq%d" % r) if i == 0 else ("sx%d" % r, "hs", "ls%d" % r)
+    a, b, sems = RUNS[r][k][0], RUNS[r][k][1], ("h%s%d" % ("cp"[i], k), "xa%d%d" % (r, k))
     return [T[x][:, a:b].bitcast(dt.uint8) if i == 0 else T[x][:, a:b] for x in names], sems
 
 
@@ -119,63 +134,60 @@ def rank_program(g, core, T, topo):
         return
     queue = {"v": g.vector, "a": g.scalar, "t": g.tensor, "g": g, "s": g.sync}
     count = {"sent": 0, "out": 0}
-    known = {q: {} for q in queue}
-    writer, readers = {}, {}
-    ndma = [0]
+    calls, writer, readers = [], {}, {}
+    ndma, first = [0], []
 
-    def wait(q, ev):
-        sem, n, seen = ev[0], ev[1], ev[2]
-        if known[q].get(sem, 0) < n:
-            queue[q].wait_ge(T.sem[sem], n)
-            known[q][sem] = n
-            for s in seen:
-                if known[q].get(s, 0) < seen[s]:
-                    known[q][s] = seen[s]
-
-    def order(q, r, w):
-        evs = []
+    def note(q, r, w, busy, late, issue, after=()):
+        before = set(after)
         for k in r:
             if k in writer:
-                evs.append(writer[k])
+                before.add(writer[k])
             if k.startswith("ps"):
-                evs.extend(e for e in readers.get(k, []) if e[0] != q)
+                before.update(e for e in readers.get(k, []) if calls[e][0] != q)
         for k in w:
             if k in writer:
-                evs.append(writer[k])
-            evs.extend(readers.get(k, []))
-        evs.sort(key=lambda e: -e[1])
-        for e in evs:
-            wait(q, e)
-
-    def note(ev, r, w):
+                before.add(writer[k])
+            before.update(readers.get(k, []))
+        calls.append((q, before, busy, late, issue))
         for k in r:
-            readers.setdefault(k, []).append(ev)
+            readers.setdefault(k, []).append(len(calls) - 1)
         for k in w:
-            writer[k] = ev
+            writer[k] = len(calls) - 1
             readers[k] = []
+        return len(calls) - 1
 
-    def op(q, r, w, call):
-        order(q, r, w)
-        call(queue[q]).then_inc(T.sem[q], 1)
-        count[q] = count.get(q, 0) + 1
-        note((q, count[q], dict(known[q])), r, w)
+    def op(q, r, w, time, call):
+        def issue():
+            call(queue[q]).then_inc(T.sem[q], 1)
+            count[q] = count.get(q, 0) + 1
+            return q, count[q]
+        note(q, r, w, time, time, issue)
 
-    def dma(q, r, w, out, in_):
-        order(q, r, w)
+    def dma(q, r, w, out, in_, late=DMA):
         s = "d%d" % ndma[0]
         ndma[0] += 1
-        queue[q].dma_start(out, in_).then_inc(T.sem[s], 16)
-        count[s] = 16
-        note((s, 16, dict(known[q])), r, w)
+
+        def issue():
+            queue[q].dma_start(out, in_).then_inc(T.sem[s], 16)
+        time = ISSUE if q == "g" else 64 * CYCLE
+        arrives(s, 16, w, late, [note(q, r, ["loads"], time, time - WAKE, issue)])
 
     def put(q, r, out, in_):
-        order(q, r, [])
-        queue[q].dma_start(out, in_).then_inc(T.sem.out, 16)
-        count["out"] += 16
+        def issue():
+            queue[q].dma_start(out, in_).then_inc(T.sem.out, 16)
+            count["out"] += 16
+        note(q, r, [], 64 * CYCLE, DMA, issue)
 
-    def arrives(sem, n, w):
+    def write(r, dst, out, in_, sem, w=()):
+        def issue():
+            count["sent"] += _send(g, T, topo, dst, topo.engines(core, dst), out, in_, T.sem[sem])
+        time = ISSUE + (0.0 if first else FIRST)
+        first.append(1)
+        return note("g", r, w, time, time - WAKE, issue)
+
+    def arrives(sem, n, w, late, after):
         count[sem] = n
-        note((sem, n, {}), [], w)
+        note(None, [], w, 0.0, late, lambda: (sem, n), after)
 
     def words(ap):
         return ap.bitcast(dt.uint32)
@@ -186,38 +198,102 @@ def rank_program(g, core, T, topo):
     def bank(b, n, a=0):
         return T.ps[:, 512 * b + a:512 * b + a + n]
 
+    def cycles(out, per, by_list=False):
+        return CYCLE * (70 + 1.56 * out.shape[1] if by_list else max(64, per * out.shape[1]))
+
     def ts(out, in0, s1, s2, o0, o1, r, w):
         if o1 is None:
-            op("v", r, w, lambda e: e.tensor_scalar(out, in0, s1, None, o0))
+            op("v", r, w, cycles(out, 1), lambda e: e.tensor_scalar(out, in0, s1, None, o0))
         else:
-            op("v", r, w, lambda e: e.tensor_scalar(out, in0, s1, s2, o0, o1))
+            op("v", r, w, cycles(out, 1), lambda e: e.tensor_scalar(out, in0, s1, s2, o0, o1))
 
-    def tt(out, in0, in1, o, r, w):
-        op("v", r, w, lambda e: e.tensor_tensor(out, in0, in1, o))
+    def tt(out, in0, in1, o, r, w, by_list=False):
+        op("v", r, w, cycles(out, 1 if any(k.startswith("ps") for k in r) else 2, by_list), lambda e: e.tensor_tensor(out, in0, in1, o))
 
-    def cp(out, in_, r, w):
-        op("v", r, w, lambda e: e.tensor_copy(out, in_))
+    def cp(out, in_, r, w, by_list=False):
+        op("v", r, w, cycles(out, 1, by_list), lambda e: e.tensor_copy(out, in_))
 
     def fill(out, c, w):
-        op("v", [], w, lambda e: e.memset(out, c))
+        op("v", [], w, cycles(out, 0.5), lambda e: e.memset(out, c))
 
-    def scan(out, d0, d1, init, o0, o1, r, w):
-        op("v", r, w, lambda e: e.tensor_tensor_scan(out, d0, d1, init, o0, o1))
+    def scan(out, d0, d1, init, o0, o1, r, w, per=1):
+        op("v", r, w, cycles(out, per), lambda e: e.tensor_tensor_scan(out, d0, d1, init, o0, o1))
 
     def quant(q, s, in_, r, w):
-        op("v", r, w, lambda e: e.quantize_mx(q, s, in_))
+        op("v", r, w, cycles(q, 1.1), lambda e: e.quantize_mx(q, s, in_))
 
-    def act(out, in_, f, r, w, **kw):
-        op("a", r, w, lambda e: e.activation(out, in_, f, **kw))
+    def act(out, in_, f, r, w, by_list=False, **kw):
+        op("a", r, w, cycles(out, 1, by_list) + ("accum_out" in kw) * 24 * CYCLE, lambda e: e.activation(out, in_, f, **kw))
+
+    def move(q, out, in_, r, w, by_list=False):
+        if q == "a":
+            act(out, in_, ACT.Copy, r, w, by_list)
+        else:
+            cp(out, in_, r, w, by_list)
 
     def mm(b, n, lq, ls, rq, rs, r):
-        op("t", r, ["ps%d" % b], lambda e: e.matmul_mx(bank(b, n), lq, ls, rq, rs, True, True))
+        op("t", r, ["ps%d" % b], 0.76 * CYCLE * (n + 16), lambda e: e.matmul_mx(bank(b, n), lq, ls, rq, rs, True, True))
 
     def iota(name, out, pattern, base, cm):
-        if name == "pi":
-            op("g", [], [name], lambda e: e.iota(out, pattern, base, cm))
+        time = CYCLE * (150 + 2 * out.shape[1])
+        if name in ("pi", "li"):
+            op("g", [], [name], time, lambda e: e.iota(out, pattern, base, cm))
         else:
-            op("g", [], [name], lambda e: e.iota(out, pattern, base, cm, allow_small_or_imprecise_dtypes=True))
+            op("g", [], [name], time, lambda e: e.iota(out, pattern, base, cm, allow_small_or_imprecise_dtypes=True))
+
+    def issue_all():
+        n = len(calls)
+        behind_it = [[] for _ in calls]
+        for i in range(n):
+            for j in calls[i][1]:
+                behind_it[j].append(i)
+
+        def gap(j, i):
+            return calls[j][3] + WAKE if calls[i][0] else calls[j][2]
+
+        def lay(first, back):
+            at, taken = [0.0] * n, {q: [] for q in queue}
+            for i in sorted(range(n), key=lambda i: (first[i], -i if back else i)):
+                q, busy = calls[i][0], calls[i][2]
+                if back:
+                    t = max([at[j] + calls[j][2] + gap(i, j) - busy for j in behind_it[i]] + [calls[i][3] - busy])
+                else:
+                    t = max([at[j] + gap(j, i) for j in calls[i][1]] + [0.0])
+                if q:
+                    for a, z in taken[q]:
+                        if t + busy > a + SLACK and t < z:
+                            t = z
+                    taken[q].append((t, t + busy))
+                    taken[q].sort()
+                at[i] = t
+            return at
+
+        chain = [c[3] for c in calls]
+        for i in range(n - 1, -1, -1):
+            for j in calls[i][1]:
+                chain[j] = max(chain[j], gap(j, i) + chain[i])
+        start = best = lay(list(range(n)), False)
+        for _ in range(TURNS):
+            late = lay([-start[i] for i in range(n)], True)
+            start = lay([-late[i] - calls[i][2] for i in range(n)], False)
+            if max(start[i] + calls[i][3] for i in range(n)) < max(best[i] + calls[i][3] for i in range(n)):
+                best = start
+        start = best
+        known = {q: {} for q in queue}
+        done = {}
+        for i in sorted(range(n), key=lambda i: (start[i], i)):
+            q, before = calls[i][:2]
+            for sem, k, seen in sorted((done[j] for j in before if q and done[j]), key=lambda e: -e[1]):
+                if known[q].get(sem, 0) < k:
+                    queue[q].wait_ge(T.sem[sem], k)
+                    known[q][sem] = k
+                    for s in seen:
+                        known[q][s] = max(known[q].get(s, 0), seen[s])
+            ev = calls[i][4]()
+            done[i] = ev and (ev[0], ev[1], dict(known[q]) if q else {})
+        for s in count:
+            if count[s] and max(known[q].get(s, 0) for q in known) < count[s]:
+                g.wait_ge(T.sem[s], count[s])
 
     mate = [T.cores[rank ^ (1 << r)] for r in range(R)]
 
@@ -242,325 +318,224 @@ def rank_program(g, core, T, topo):
     def landed(r, a, b):
         return ["lx%d%d" % (r, k) for k, run in enumerate(RUNS[r]) if run[0] < b and a < run[1]]
 
-    def send(r, k, i):
-        (src, held, land), (there, end) = _sides(T, r, k, i)
-        h = _ways(T, topo, core, r)[k, i]
-        if h is None:
-            count["sent"] += _send(g, T, topo, mate[r], topo.engines(core, mate[r]), land, src, T.sem[end])
-        else:
-            count["sent"] += _send(g, T, topo, h, topo.engines(core, h), held, src, T.sem[there])
-        h = _ways(T, topo, mate[r], r)[k, i]
-        return len(topo.engines(mate[r] if h is None else h, core))
-
-    def ship_u(r):
-        order("g", ["urq", "urs"], [])
-        arrives("ua%d" % r, send(r, -1, 0) + send(r, -1, 1), ["ul%d" % r])
-
     def ship(r, k, between=None):
-        order("g", xkeys(r, RUNS[r][k][0], RUNS[r][k][1]), [])
-        n = send(r, k, 0)
-        if between:
-            between()
-        arrives("xa%d%d" % (r, k), n + send(r, k, 1), ["lx%d%d" % (r, k)])
+        n, sent = 0, []
+        for i in range(2):
+            if i and between:
+                between()
+            (src, held, land), (there, end) = _sides(T, r, k, i)
+            h, rd = _ways(T, topo, core, r)[k, i], xkeys(r, RUNS[r][k][0], RUNS[r][k][1]) + ["told"]
+            sent.append(write(rd, mate[r], land, src, end) if h is None else write(rd, h, held, src, there))
+            h = _ways(T, topo, mate[r], r)[k, i]
+            n += len(topo.engines(mate[r] if h is None else h, core))
+        near = topo.chip(mate[r]) == topo.chip(core)
+        arrives("xa%d%d" % (r, k), n, ["lx%d%d" % (r, k)], HOP + 0.5 if near else 2 * HOP + 2.0, sent)
 
     def ship_piece(r, k):
         for i, run in enumerate(RUNS[r]):
             if CUT[k] < run[1] <= CUT[k + 1]:
                 ship(r, i)
 
-    def spread_u(r):
-        cp(words(T["upq%d" % r][:]), words(T["ulq%d" % r][:]).indirect(T.lu1[:]), ["ul%d" % r, "lu1"], ["upq%d" % r])
-        act(T["ups%d" % r][:], T["uls%d" % r][:, 0:8].indirect(T.lu1[:]), ACT.Copy, ["ul%d" % r, "lu1"], ["ups%d" % r])
+    def swap(r, sem, out, in_, rd, w):
+        near = topo.chip(mate[r]) == topo.chip(core)
+        arrives(sem, len(topo.engines(mate[r], core)), w, HOP + (0.0 if near else WAKE), [write(rd, mate[r], out, in_, sem, ["told"])])
 
-    PL, M0, M1, PA, PB, PM, AM, CD, CY, T1, T2, T3, T4, T5 = [T.col[:, k:k + 1] for k in range(14)]
+    PL, PA, PB, AM, CY, T2, T4, NQ, VQ, C4, CL, T5, T6 = [T.col[:, k:k + 1] for k in range(13)]
 
-    def own_mm(r, k):
-        a, b = behind(k)
-        mm(7, b - a, T.urq[:], T.urs[:], T["qx%d" % r][:, a:b], T["sx%d" % r][:, a:b], ["urq", "urs"] + xkeys(r, a, b))
-
-    def own_row(k, q="a"):
-        a, b = CUT[k], CUT[k + 1]
-        if q == "a":
-            act(T.ow[:, a:b], bank(7, b - a, a - behind(k)[0]), ACT.Copy, ["ps7"], ["ow%d" % k])
-        else:
-            cp(T.ow[:, a:b], bank(7, b - a, a - behind(k)[0]), ["ps7"], ["ow%d" % k])
-
-    def own_windows(s, q="a"):
-        row = T.ow[:, 0:CUT[s + 1]]
-        for a, z, off, m, w in ((0, 48, T.lw[:, 4 * s:4 * s + 3], M1, "ogb%d" % s), (48, 64, T.la[:, 2 * s:2 * s + 1], M0, "oga%d" % s)):
-            out, r = T.og[:, 64 * s + a:64 * s + z], keys("ow", s + 1) + ["lw", "la", "mask"]
-            if q == "a":
-                act(out, row.indirect(off), ACT.Identity, r, [w], scale=m)
-            else:
-                ts(out, row.indirect(off), m, None, ALU.mult, None, r, [w])
-
-    def far_mm(r, k, b):
+    def scores(r, k, b=7):
         a, z = behind(k)
-        mm(b, z - a, T["upq%d" % r][:], T["ups%d" % r][:], T["lq%d" % r][:, a:z], T["ls%d" % r][:, a:z],
-           ["upq%d" % r, "ups%d" % r] + landed(r, a, z))
+        lq, ls, key = (T.urq, T.urs, ["urq", "urs"]) if r < R else (T.vq, T.vs, ["vq"])
+        mm(b, z - a, lq[:], ls[:], T["qx%d" % r][:, a:z], T["sx%d" % r][:, a:z], key + xkeys(r, a, z))
 
-    def far_row(k, b, half, q):
+    def piece(k, b, a=None, z=None):
+        a, z = (CUT[k], CUT[k + 1]) if a is None else (a, z)
+        return bank(b, z - a, a - behind(k)[0])
+
+    def own_row(k, b=7):
+        if k == NS - 1:
+            act(T.ow[:, 0:V], piece(k, b, C - V, C), ACT.Copy, ["ps%d" % b], cols("ow", 0, V))
+        act(T.ow[:, V + CUT[k]:V + CUT[k + 1]], piece(k, b), ACT.Copy, ["ps%d" % b], cols("ow", V + CUT[k], V + CUT[k + 1]))
+        if k == 0:
+            act(T.ow[:, V + C:XW], piece(k, b, 0, V), ACT.Copy, ["ps%d" % b], cols("ow", V + C, XW))
+
+    def mask(k, b=7):
         a, z = CUT[k], CUT[k + 1]
-        out, in_, m = T.pw[:, C * half + a:C * half + z], bank(b, z - a, a - behind(k)[0]), (M0, M1)[half]
-        if q == "v":
-            ts(out, in_, m, None, ALU.mult, None, ["ps%d" % b, "mask"], ["pw%d" % half])
-        else:
-            act(out, in_, ACT.Identity, ["ps%d" % b, "mask"], ["pw%d" % half], scale=m)
+        tt(T.msk[:, a:z], piece(k, b), T.dm[:, 0:z - a], ALU.mult, ["ps%d" % b, "dm"], ["msk%d" % k])
+        turn(k, b)
 
-    def far_rows(r, k):
-        far_mm(r, k, 7 - k)
-        far_row(k, 7 - k, 0, "v")
-        far_row(k, 7 - k, 1, "v")
+    def hold(k):
+        a, z = CUT[k], CUT[k + 1]
+        scan(T.hold[:, a:z], T.rs[:, 0:z - a], T.msk[:, a:z], 0.0, ALU.mult, ALU.add, ["rs", "msk%d" % k], ["hold%d" % k])
 
-    def windows(s):
-        tt(T.ba[:, 64 * s:64 * s + 64], T.pw[:].indirect(T.lw[:, 4 * s:4 * s + 4]), T.og[:, 64 * s:64 * s + 64], ALU.add,
-           ["pw0", "pw1", "lw", "ogb%d" % s, "oga%d" % s], ["ba%d" % s])
+    def tell(r, k, q, k0=None):
+        k0 = k if k0 is None else k0
+        rd = []
+        for i in range(k0, k + 1):
+            a, z, c = CUT[i], CUT[i + 1], DW * r + AT[i]
+            move(q, T.dgs[:, c:c + (z - a) // 16], T.hold[:, a + 15:z:16], ["dgs", "hold%d" % i], ["dgs%d%d" % (r, i)])
+            rd.append("dgs%d%d" % (r, i))
+            for a, z, c, _ in TURNED[i]:
+                move("a", T.dgs[:, DW * r + c:DW * r + c + (z - a) // 16], T.tr[:, a:z:16], ["dgs"] + cols("tr", a, z), ["dgt%d%d" % (r, a)])
+                rd.append("dgt%d%d" % (r, a))
+        c, d = DW * r + AT[k0], DW * r + END[k]
+        swap(r, "da%d%d" % (r, k), T.dgl[:, c:d], T.dgs[:, c:d], rd + ["dgs"], slots("dgl%d_" % r, k0, k + 1))
 
-    def zero(t, a, z, w):
-        for i in range(a, z, ST * SG):
-            n = min(ST * SG, z - i)
-            act(t[:, i:i + n], T.crow[:, 0:n], ACT.Identity, ["crow"], w if i + n == z else [], scale=0.0)
+    def turn(k, b=7):
+        for a, z, _, _ in TURNED[k]:
+            op("v", ["ps%d" % b], cols("tr", a, z), cycles(T.tr[:, a:z], 1), lambda e, a=a, z=z: e.transpose(T.tr[:, a:z], piece(k, b, a, z)))
 
-    def every16(i):
-        act(T.kd[:, i:C:16], T.ir[:], ACT.Identity, keys("ir", 3) + ["ca", "cdd"], ["kd%d" % i], scale=T.ca[:, i:i + 1], bias=T.cd[:, i:i + 1])
+    def far_row(r, k):
+        for a, z, c, x in TURNED[k]:
+            c += DW * r
+            move("a", T.bc[:, a:z], T.dgl[:, c // 8 * 8:c + (z - a) // 16].indirect(T.lj[:, c % 8:c % 8 + (z - a) // 16]),
+                 ["lj", "dgl%d_%d" % (r, k)], cols("bc", a, z), True)
+            op("v", cols("bc", a, z), cols("fw", x, x + z - a), cycles(T.bc[:, a:z], 1),
+               lambda e, a=a, z=z, x=x: e.transpose(T.fw[:, x:x + z - a], T.bc[:, a:z]))
 
-    CHECK = [(256, C), (0, 96), (96, 256)]
-
-    dma("s", [], ["x00"], T.x0[:, 0:4 * CUT[1]], T.x[:, 4 * PLACE[0]:4 * C])
-    dma("s", [], ["ut"], T.ut[:], T.u[:])
-    dma("s", [], ["x01"], T.x0[:, 4 * CUT[1]:4 * C], T.x[:, 0:4 * PLACE[0]])
-    iota("pi", T.pi[:], [[0, 8]], 0, 1)
-    iota("ik", T.ik[:], [[1, 24]], 0, 0)
-    iota("iw", T.iw[:], [[128, 3], [16, 4]], 0, 1)
-    iota("im", T.im[:], [[16, SG]], 0, 0)
-    iota("ic", T.ic[:], [[1, 8], [0, 16]], 0, 0)
-    fill(T.crow[:], 1.0, ["crow"])
-    op("g", ["crow"], ["et"], lambda e: e.affine_select(T.et[:], T.crow[:, 0:516], [[1, 516]], ALU.is_equal, 0.0, -3, -4))
-    ts(T.pa[:], T.pi[:], 15, None, ALU.bitwise_and, None, ["pi"], ["pa"])
-    ts(T.pb[:], T.pi[:], 7, None, ALU.bitwise_and, None, ["pi"], ["pb"])
-    cp(PL, T.pa[:, 0:1], ["pa"], ["pl"])
-    ts(T1, PL, 0.0, 16.0, ALU.is_equal, ALU.mult, ["pl"], ["t1"])
-    ts(T.ca[:], T.ik[:, 0:16], PL, None, ALU.is_equal, None, ["ik", "pl"], ["ca"])
-    ts(T3, PL, 80.0, None, ALU.add, None, ["pl"], ["t3"])
-    ts(T.lu16[:], T.pb[:], 16.0, None, ALU.mult, None, ["pb"], ["lu16"])
-    ts(PM, PL, T1, -1.0, ALU.add, ALU.add, ["pl", "t1"], ["pm"])
-    ts(T.cc[:], T.ca[:], T3, None, ALU.mult, None, ["ca", "t3"], ["cc"])
-    ts(T.lsc[:, 0:3], T.iw[:, 0:12:4], 4.0, None, ALU.mult, None, ["iw"], ["lsc"])
-    ts(T.cb[:], T.ik[:, 0:16], PM, -1024.0, ALU.is_equal, ALU.mult, ["ik", "pm"], ["cb"])
-    for i, (a, z) in enumerate(CHECK):
-        ts(T.ir[:, a // 16:z // 16], T.ik[:, a // 16:z // 16], 16.0, -float(a), ALU.mult, ALU.add, ["ik"], ["ir%d" % i])
-    zero(T.pw, 0, 2 * C, ["pw0", "pw1"])
-    zero(T.rst, 0, ST * SG, ["rst"])
-    quant(T.qx0[:, 0:CUT[1]], T.sx0[:, 0:CUT[1]], T.x0[:, 0:4 * CUT[1]], ["x00"], ["qx00"])
-    tt(T.cd[:], T.cc[:], T.cb[:], ALU.add, ["cc", "cb"], ["cdd"])
-    ts(M0, PL, 8.0, None, ALU.is_lt, None, ["pl"], ["m0"])
-    ts(T.iw[:, 3:12:4], T.iw[:, 3:12:4], -32.0, None, ALU.add, None, ["iw"], ["iw"])
-    act(T.rst[:, 0:ST * SG:SG], T.rst[:, 0:ST * SG:SG], ACT.Identity, ["rst"], ["rst"], bias=BIG)
-    zero(T.ct, 0, 512, ["ct0"])
-    quant(T.uq[:], T.us[:], T.ut[:], ["ut"], ["uq"])
-    ts(T.wb[:], T.iw[:], float(C), -float(C), ALU.is_ge, ALU.mult, ["iw"], ["wb"])
-    ts(M1, PL, 8.0, None, ALU.is_ge, None, ["pl", "m0"], ["mask"])
-    cp(words(T.urq[:]), words(T.uq[:]).indirect(T.lu16[:]), ["uq", "lu16"], ["urq"])
-    act(T.urs[:], T.us[:].indirect(T.lu16[:]), ACT.Copy, ["uq", "lu16"], ["urs"])
-    ship(0, 0, lambda: ship_u(0))
-    iota("crow", T.crow[:, 0:ST * SG:SG], [[0, ST]], -V, 0)
-    tt(T.wd[:], T.iw[:], T.wb[:], ALU.add, ["iw", "wb"], ["wd"])
-    cp(T.lu1[:], T.pb[:], ["pb"], ["lu1"])
-    ts(T.ma[:], T.im[:], PL, -16.0, ALU.add, ALU.add, ["im", "pl"], ["ma"])
-    cp(T.lw[:], T.wd[:], ["wd"], ["lw"])
-    cp(T.la[:, 0:6:2], T.wd[:, 3:12:4], ["wd"], ["la"])
-    for b in range(4):
-        quant(T.eq[:, 128 * b:128 * b + 128], T.es[:, 128 * b:128 * b + 128], T.et[:, 3 - b:515 - b], ["et"], ["eq%d" % b])
-        if b == 0:
-            ts(T.lw[:, 3:12:4], T.wd[:, 3:12:4], float(C), None, ALU.add, None, ["wd"], ["lw"])
-    quant(T.qx0[:, CUT[1]:C], T.sx0[:, CUT[1]:C], T.x0[:, 4 * CUT[1]:4 * C], ["x01"], ["qx01", "qx02"])
-    ship(0, 1)
-    iota("mta", T.mt[:], [[0, 4 * C]], 0, 0)
-    ship_u(1)
-    ship_u(2)
-    iota("iy", T.iy[:], [[4, 96]], 0, 0)
-    iota("x1z", T.x1[:, 4 * C:4 * XW], [[0, 8 * V]], 0, 0)
-    iota("ytz", T.yt[:, 4 * C:4 * XW], [[0, 8 * V]], 0, 0)
-    dma("s", ["ul0"], ["wq"], raw(T.wq[:]), T.wc[:])
-    dma("s", [], ["wp"], T.wp[:], T.ws[:])
-    dma("s", [], ["vt"], T.vt[:], T.v[:])
-    own_mm(0, 0)
-    for i in range(6):
-        every16(i)
-    own_row(0)
-    for i in range(6, 9):
-        every16(i)
-    own_windows(0)
-    zero(T.ct, 512, 1024, ["ct1"])
-    own_mm(0, 1)
-    ts(T.mb[:], T.ma[:], 1.0 / SG, None, ALU.mult, None, ["ma"], ["mb"])
-    ts(T.ct[:, 0:512:4], T.ic[:], 8.0, PL, ALU.add, ALU.is_equal, ["ic", "pl"], ["ct0"])
-    spread_u(0)
-    for i in range(9, 16):
-        every16(i)
-    ts(T.ct[:, 512:1024:4], T.ic[:], PL, None, ALU.is_equal, None, ["ic", "pl"], ["ct1"])
-    ts(T.lm[:], T.mb[:], float(SG), SG - 1.0, ALU.mult, ALU.add, ["mb"], ["lm"])
-    ts(T.pd[:], T.pi[:], 2, 3, ALU.arith_shift_right, ALU.bitwise_and, ["pi"], ["pd"])
-
-    def later(i):
-        if i == 0:
-            cp(PA, T.pd[:, 0:1], ["pd"], ["pac"])
-            ts(T.pc[:], T.pi[:], 3, None, ALU.bitwise_and, None, ["pi"], ["pc"])
-        elif i == 1:
-            ts(T2, PA, 0.0, 4.0, ALU.is_equal, ALU.mult, ["pac"], ["t2"])
-            own_mm(0, NS - 1)
-            own_row(NS - 1, "v")
-            quant(T.cq[:], T.cs[:], T.ct[:], ["ct0", "ct1"], ["cq"])
-            own_windows(NS - 1, "v")
-            ts(PB, T.pc[:, 0:1], -64.0, None, ALU.add, None, ["pc"], ["pbc"])
-        elif i == 2:
-            ts(AM, PA, T2, -1.0, ALU.add, ALU.add, ["pac", "t2"], ["am"])
-            ts(T4, PA, 32.0, None, ALU.add, None, ["pac"], ["t4"])
-        elif i == 3:
-            ts(T.ya[:], T.ik[:, 0:4], PA, None, ALU.is_equal, None, ["ik", "pac"], ["ya"])
-            ts(T.yb[:], T.ik[:, 0:4], AM, -224.0, ALU.is_equal, ALU.mult, ["ik", "am"], ["yb"])
-        elif i == 4:
-            ts(T.yc[:], T.ya[:], T4, None, ALU.mult, None, ["ya", "t4"], ["yc"])
-            ts(CD, T1, 64.0, -64.0, ALU.mult, ALU.add, ["t1"], ["cd"])
-        else:
-            tt(T.yd[:], T.yc[:], T.yb[:], ALU.add, ["yc", "yb"], ["yd"])
-            ts(CY, T2, 224.0, PB, ALU.mult, ALU.add, ["t2", "pbc"], ["cy"])
-
-    def last():
-        for k in (0, 2):
-            a, z = PLACE[k] // 4, (PLACE[k] + CUT[k + 1] - CUT[k]) // 4
-            act(T.iy[:, a:z], T.iy[:, a:z], ACT.Identity, ["iy"], ["iy%d" % k], bias=-float(PLACE[k]))
-        evac_p(0)
-        for i in range(4):
-            act(T.ky[:, i:C:4], T.iy[:], ACT.Identity, ["iy", "iy0", "iy2", "ya", "yd"], ["ky%d" % i],
-                scale=T.ya[:, i:i + 1], bias=T.yd[:, i:i + 1])
-
-    def diffs(a, b):
-        for n in range(a, b):
-            s, q = divmod(n, ST)
-            o = 64 * s
-            act(T.dd[:, SG * n:SG * n + SG], T.ba[:, o + q:o + q + SG], ACT.Abs, ["ba%d" % s], ["dd%d" % n],
-                bias=T.ba[:, o + 48 + q:o + 49 + q], scale=-1.0)
+    def diffs(r, a, b):
+        for i in range(a, b):
+            k = max(k for k in range(NS) if CUT[k] <= 16 * (i % NB))
+            if i < NB:
+                c = DW * r + AT[k] + i - CUT[k] // 16
+                row, mid, rd = T.ow[:, 16 * i:16 * i + W], T.dgl[:, c:c + 1], slots("ow", i, i + 3) + ["dgl%d_%d" % (r, k)]
+            else:
+                j = i - NB
+                row, mid, rd = T.fw[:, 16 * j:16 * j + W], T.hold[:, 16 * j + 15:16 * j + 16], slots("fw", j, j + 3) + ["hold%d" % k]
+            act(T.dd[:, W * i:W * i + W], row, ACT.Abs, rd, ["dd%d" % i], bias=mid, scale=-1.0)
 
     def least(a, b):
-        scan(T.pm[:, SG * a:SG * b], T.rst[:, 0:SG * (b - a)], T.dd[:, SG * a:SG * b], 0.0, ALU.add, ALU.min,
-             ["rst"] + slots("dd", a, b), slots("pm", a, b))
+        scan(T.pm[:, 1 + W * a:1 + W * b], T.dd[:, W * a:W * b], T.mk[:, 0:W * (b - a)], BIG, ALU.min, ALU.max,
+             ["mk"] + slots("dd", a, b), slots("pm", a, b))
 
-    def above(a, b):
-        w = ST
-        c = (w - b + a) * SG // 32 * 2
-        lo = SG * (b - w) + 16 * c
-        tt(T.gt[:, lo + b * 8:SG * b + b * 8], T.pm[:, SG * (b - w):SG * b].indirect(T.lm[:, c:w * SG // 16]), T.dd[:, lo:SG * b],
-           ALU.not_equal, slots("pm", b - w, b) + slots("dd", b - w, b) + ["lm"], ["gt%d" % b])
-
-    def back(t, a, b):
-        return t[:, b - 1:a - 1:-1] if a else t[:, b - 1::-1]
-
-    def tally(a, b):
-        scan(back(T.cnt, SG * a, SG * b), back(T.gt, SG * a + b * 8, SG * b + b * 8), back(T.crow, 0, SG * (b - a)), 0.0,
-             ALU.mult, ALU.add, ["crow", "gt%d" % b], slots("cnt", a, b))
+    def final(a, b):
+        scan(T.p2[:, W * a:W * b], T.rst[:, 0:W * (b - a)], T.pm[:, 1 + W * a:1 + W * b], 0.0, ALU.add, ALU.min,
+             ["rst"] + slots("pm", a, b), slots("p2", a, b))
 
     def signs(a, b):
-        for n in range(a, b):
-            act(T.sj[:, SG * n:SG * n + SG], T.pm[:, SG * n:SG * n + SG], ACT.Sign, ["pm%d" % n], ["acc%d" % n],
-                bias=T.pm[:, SG * n + SG - 1:SG * n + SG], scale=-1.0, accum_out=T.acc[:, n:n + 1])
+        for i in range(a, b):
+            act(T.sj[:, W * i:W * i + W], T.pm[:, 1 + W * i:1 + W * i + W], ACT.Sign, ["pm%d" % i, "p2%d" % i], ["acc%d" % i],
+                bias=T.p2[:, W * i + W - 1:W * i + W], scale=-1.0, accum_out=T.acc[:, i:i + 1])
+
+    def flags(a, b):
+        tt(T.nf[:, W * a:W * b], T.pm[:, 1 + W * a:1 + W * b], T.pm[:, W * a:W * b], ALU.is_ge,
+           slots("pm", a - 1, b), slots("nf", a, b))
+
+    def tally(a, b):
+        scan(T.cnt[:, W * a:W * b], T.nf[:, W * a:W * b], T.one[:, 0:W * (b - a)], 0.0, ALU.mult, ALU.add,
+             ["one"] + slots("nf", a, b), slots("cnt", a, b), 0.5)
 
     def counted(a, b):
-        act(T.cnt[:, SG * a:SG * b:SG], T.acc[:, a:b], ACT.Identity, slots("acc", a, b), slots("cnt", a, b),
-            bias=-float(V), scale=-1.0)
+        ts(T.acc[:, a:b], T.cnt[:, W * a + W - 1:W * b:W], VQ, None, ALU.add, None, slots("cnt", a, b) + ["vq_"], slots("acc", a, b))
 
-    PART = {"a": (0, 256, 0, 2), "b": (256, C, 2, 3)}
-    HELD = {"a": [(240, C, 0), (0, 112, 144)], "b": [(112, 240, 16)]}
+    def lists(t, r, p):
+        a, z = PARTS[p]
+        o = 2 * (NB * r + a)
+        return t[:, o:o + z - a], t[:, o + z - a:o + 2 * (z - a)], t[:, o:o + 2 * (z - a)]
 
-    def lay(p):
-        a, z, s0, s1 = PART[p]
-        cp(T.mt[:, 0:4 * z].indirect(T.lsc[:, s0:s1]), T.cnt[:, ST * SG * s0:ST * SG * s1:SG],
-           slots("cnt", ST * s0, ST * s1) + ["lsc"], ["mta", "mt" + p])
+    def places(t, o, a, z, w):
+        if z - a > ONE:
+            tt(T.pf[:, a:z], T.c1[:, a % NB:a % NB + z - a], T.acc[:, a:z], ALU.subtract, ["c1"] + slots("acc", a, z), slots("pf", a, z))
+            cp(t[:, o:o + z - a], T.pf[:, a:z], slots("pf", a, z), w)
+        else:
+            for i in range(a, z):
+                ts(t[:, o + i - a:o + i - a + 1], T.acc[:, i:i + 1], -1.0, T.c1[:, i % NB:i % NB + 1], ALU.mult, ALU.add,
+                   ["acc%d" % i, "c1"], [w[i - a]])
 
-    def pack(p):
-        a, z, s0, s1 = PART[p]
-        quant(T.mq[:, a:z], T.ms[:, a:z], T.mt[:, 4 * a:4 * z], ["mt" + p], ["mq" + p])
-        a = min(a, 240)
-        for b, c in ((4, 128), (6, 0)):
-            mm(b + (p == "b"), z - a, T.cq[:, c:c + 128], T.cs[:, c:c + 128], T.mq[:, a:z], T.ms[:, a:z], ["cq", "mqa", "mq" + p])
+    def steps(out, a, z, w):
+        ts(out, T.acc[:, a:z], -1.0, 1.0 - V, ALU.mult, ALU.add, slots("acc", a, z), w)
 
-    def sixteenth(p):
-        b = 4 + (p == "b")
-        for a, z, o in HELD[p]:
-            scan(T.exd[:, a:z], bank(b, z - a, o), T.kd[:, a:z], -1024.0, ALU.max, ALU.add, keys("kd", 16) + ["ps%d" % b], cols("exd", a, z))
+    def answer(r, p):
+        a, z = PARTS[p]
+        mf = slots("mf%d_" % r, a, z)
+        places(T.mo, 2 * (NB * r + a), a, z, mf)
+        if a < BOTH:
+            steps(lists(T.mo, r, p)[1], a, z, ["md%d%d" % (r, p)])
+            swap(r, "ma%d%d" % (r, p), lists(T.ml, r, p)[2], lists(T.mo, r, p)[2], mf + ["md%d%d" % (r, p)], ["ml%d%d" % (r, p)])
+        for a, z in OWN[p]:
+            places(T.mm, a, NB + a, NB + z, slots("mm", a, z))
+            steps(T.mm[:, NB + a:NB + z], NB + a, NB + z, slots("mm", NB + a, NB + z))
 
-    def minus(p, q):
-        b = 4 + (p == "b")
-        for a, z, o in HELD[p]:
-            if q == "v":
-                ts(T.nd[:, a:z], bank(b, z - a, o), -1.0, None, ALU.mult, None, ["ps%d" % b], cols("nd", a, z))
-            else:
-                act(T.nd[:, a:z], bank(b, z - a, o), ACT.Identity, ["ps%d" % b], cols("nd", a, z), scale=-1.0)
+    def mine(r, a, z, i):
+        if a >= BOTH:
+            return T.mm[:, NB * i + a:NB * i + z], slots("mm", NB * i + a, NB * i + z)
+        p = max(p for p in range(len(PARTS)) if PARTS[p][0] <= a)
+        o = 2 * (NB * r + PARTS[p][0]) + i * (PARTS[p][1] - PARTS[p][0]) - PARTS[p][0]
+        return T.ml[:, o + a:o + z], ["ml%d%d" % (r, p)]
 
-    def theirs(p):
-        for a, z, o in {"a": [(256, XW, 0), (0, 128, 128)], "b": [(128, 256, 16)]}[p]:
-            act(T.dpx[:, a:z], bank(6 + (p == "b"), z - a, o), ACT.Copy, ["ps%d" % (6 + (p == "b"))], cols("dp", a, z))
+    def theirs(r, p, q):
+        a, z = PARTS[p]
+        f = lists(T.mo, r, p)[0]
+        runs = [(2 * V + 16 * a, 2 * V + 16 * z, f)]
+        if a == 0:
+            runs.append((2 * V + C, 3 * V + C, T.mo[:, 2 * NB * r:2 * NB * r + 1]))
+        if z == NB:
+            o = 2 * (NB * r + a) + z - a
+            runs.insert(0, (0, 2 * V, T.mo[:, o - 2:o]))
+        for x, y, off in runs:
+            move(q, T.rp[:, x:y], T.cyc[:].indirect(off), ["cyc"] + slots("mf%d_" % r, a, z), cols("rp", x, y), True)
 
-    def reach(a, z):
-        ts(T.fd[:, a // 16:z // 16], T.exd[:, a + 15:z:16], CD, None, ALU.add, None, cols("exd", a, z) + ["cd"], cols("fd", a, z))
-
-    def check(i):
-        a, z = CHECK[i]
-        tt(T.ok[:, a:z], T.dpx[:, a:z + 2 * V].indirect(T.fd[:, a // 16:z // 16]), T.nd[:, a:z], ALU.is_equal,
-           cols("dp", a, z + 2 * V) + cols("fd", a, z) + cols("nd", a, z), cols("ok", a, z))
-
-    def kept(a, z, b, o):
-        tt(T.okd[:, a:z], T.ok[:, a:z], bank(b, z - a, o), ALU.mult, cols("ok", a, z) + ["ps%d" % b], cols("okd", a, z))
-
-    def other(a, z):
+    def check(r, i, k):
+        a, z = 16 * i, 16 * k
+        (to, rt), (by, rb) = mine(r, i, k, 0), mine(r, i, k, 1)
+        tt(T.ok[:, a:z], T.rp[:, 0:z + 3 * V].indirect(to), T.cyc[:, 2 * V + a:2 * V + z], ALU.is_equal,
+           cols("rp", 0, z + 3 * V) + rt + ["cyc"], cols("ok", a, z), True)
         act(T.nok[:, a:z], T.ok[:, a:z], ACT.Identity, cols("ok", a, z), cols("nok", a, z), bias=1.0, scale=-1.0)
+        tt(T.okd[:, a:z], T.cdv[:].indirect(by), T.ok[:, a:z], ALU.mult, cols("ok", a, z) + rb + ["cdv"], cols("okd", a, z), True)
 
-    def unpack(q, s, r):
+    def unpack(q, s, b0, r):
         for b in range(4):
-            mm(b, C, T.eq[:, 128 * b:128 * b + 128], T.es[:, 128 * b:128 * b + 128], q[:, 0:C], s[:, 0:C], ["eq%d" % b] + r)
+            mm(b0 + b, C, T.eq[:, 128 * b:128 * b + 128], T.es[:, 128 * b:128 * b + 128], q[:, 0:C], s[:, 0:C], ["eq%d" % b] + r)
 
-    def evac_p(b):
-        act(T.pp[:, 4 * V + b:4 * (V + C):4], bank(b, C), ACT.Identity, ["ps%d" % b], ["pp%d" % b], scale=0.5)
+    def evac_p(b, q):
+        out, r, w = T.pp[:, 4 * V + b:4 * (V + C):4], ["ps%d" % (4 + b)], ["pp%d" % b]
+        if q == "a":
+            act(out, bank(4 + b, C), ACT.Identity, r, w, scale=0.5)
+        else:
+            ts(out, bank(4 + b, C), 0.5, None, ALU.mult, None, r, w)
 
-    def carry(out, init, r, w, rev):
-        a, b = (T.nok[:, ::-1], T.okd[:, ::-1]) if rev else (T.nok[:], T.okd[:])
-        scan(out, a, b, init, ALU.mult, ALU.add, cols("nok", 0, C) + cols("okd", 0, C) + r, w)
+    def ends_p():
+        act(T.pp[:, 0:4 * V], T.pp[:, 4 * C:4 * (C + V)], ACT.Copy, keys("pp", 4), ["ppa"])
+        act(T.pp[:, 4 * (C + V):4 * XW], T.pp[:, 4 * V:8 * V], ACT.Copy, keys("pp", 4), ["ppz"])
 
-    def pick(row, ex, key):
-        scan(T[ex][:], row, T.ky[:], -224.0, ALU.max, ALU.add, keys("ky", 4) + [key], [ex])
+    def carry(t, o, a, z, init, r, rev=False):
+        def run(x, o=0):
+            return x[:, o + a:o + z] if not rev else x[:, o + z - 1:o + a - 1:-1] if o + a else x[:, z - 1::-1]
+        scan(run(T[t], o), run(T.nok), run(T.okd), init, ALU.mult, ALU.add, cols("nok", a, z) + cols("okd", a, z) + r,
+             cols(t, o + a, o + z), 0.5)
+
+    def pick(o, ex):
+        scan(T[ex][:], T.lh[:, o:o + C], T.ky[:], -224.0, ALU.max, ALU.add, keys("ky", 4) + cols("lh", o, o + C), [ex], 0.5)
 
     def offsets(off, ex):
         ts(T[off][:], T[ex][:, 3:C:4], 4.0, CY, ALU.mult, ALU.add, [ex, "cy"], [off])
 
     plane = keys("pp", 4) + ["ppa", "ppz"]
 
-    def source(k, a, z, off):
-        o = PLACE[k] - CUT[k]
-        return T.pp[:, 4 * CUT[k]:4 * (CUT[k + 1] + 2 * V)].indirect(T[off][:, (a + o) // 4:(z + o) // 4])
+    def source(a, z, off):
+        k = max(i for i in range(NS) if CUT[i] <= a)
+        return T.pp[:, 4 * CUT[k]:4 * (CUT[k + 1] + 2 * V)].indirect(T[off][:, a // 4:z // 4])
 
-    def take_h(k, a, z, q="a"):
-        if q == "a":
-            act(T.gh[:, 4 * a:4 * z], source(k, a, z, "fh"), ACT.Copy, plane + ["fh"], cols("gh", a, z))
-        else:
-            cp(T.gh[:, 4 * a:4 * z], source(k, a, z, "fh"), plane + ["fh"], cols("gh", a, z))
+    def take_h(a, z, q="a"):
+        move(q, T.gh[:, 4 * a:4 * z], source(a, z, "fh"), plane + ["fh"], cols("gh", a, z), True)
 
-    def take_l(k, a, z):
-        tt(T.yt[:, 4 * a:4 * z], source(k, a, z, "fl"), T.gh[:, 4 * a:4 * z], ALU.add, plane + ["fl"] + cols("gh", a, z), cols("yt", a, z))
+    def take_l(a, z):
+        tt(T.yt[:, 4 * a:4 * z], source(a, z, "fl"), T.gh[:, 4 * a:4 * z], ALU.add, plane + ["fl"] + cols("gh", a, z), cols("yt", a, z), True)
 
     def quant_y(k):
-        a, z = ahead(k)
-        quant(T.yq[:, a:z], T.ys[:, a:z], T.yt[:, 4 * a:4 * z], ["ytz"] + cols("yt", CUT[k], CUT[k + 1]), ["yq%d" % k])
+        a, z = behind(k)
+        quant(T.yq[:, a:z], T.ys[:, a:z], T.yt[:, 4 * a:4 * z], cols("yt", a, z), cols("yq", a, z))
 
-    def layers(k):
-        a, z = ahead(k)
-        for b in range(4):
-            mm(7 - b, z - a, T.wq[:, 128 * b:128 * b + 128], T.wp[:, 128 * b:128 * b + 128], T.yq[:, a:z], T.ys[:, a:z],
-               ["wq", "wp", "yq%d" % k])
+    def layers(k, b0=0, b1=4):
+        a, z = behind(k)
+        for b in range(b0, b1):
+            mm(4 + (4 * k + b) % 3, z - a, T.wq[:, 128 * b:128 * b + 128], T.wp[:, 128 * b:128 * b + 128], T.yq[:, a:z], T.ys[:, a:z],
+               ["wq", "wp"] + cols("yq", a, z))
 
     def relus(k, b0, b1):
         a, z = CUT[k], CUT[k + 1]
         for b in range(b0, b1):
-            act(T.rb[:, C * b + a:C * b + z], bank(7 - b, z - a), ACT.Relu, ["ps%d" % (7 - b)], ["rb%d%d" % (k, b)], scale=0.03125)
+            c = 4 + (4 * k + b) % 3
+            act(T.rb[:, C * b + a:C * b + z], piece(k, c), ACT.Relu, ["ps%d" % c], ["rb%d%d" % (k, b)], scale=0.03125)
 
     def adds(k, b0, b1):
         a, z = CUT[k], CUT[k + 1]
@@ -570,183 +545,166 @@ def rank_program(g, core, T, topo):
 
     def quant_x(r, k):
         a, z = ahead(k)
-        quant(T["qx%d" % r][:, a:z], T["sx%d" % r][:, a:z], T.x1[:, 4 * a:4 * z], ["x1z"] + keys("x1%d" % k, 4), ["qx%d%d" % (r, k)])
+        over = [i for i in range(k, NS) if CUT[i] < z]
+        quant(T["qx%d" % r][:, a:z], T["sx%d" % r][:, a:z], T.x1[:, 4 * a:4 * z],
+              ["x1z"] + [x for i in over for x in keys("x1%d" % i, 4)], ["qx%d%d" % (r, i) for i in over])
 
     def onward(r, k):
         if r < R:
             ship_piece(r, k)
             return
-        a, z, o = CUT[k], CUT[k + 1], PLACE[k]
-        q, s = T["qx%d" % R], T["sx%d" % R]
-        put("s", xkeys(R, a, z), T.oc[:, 4 * o:4 * (o + z - a)], raw(q[:, a:z]))
-        if k != 1:
-            a, o = (a, o) if k == 0 else (CUT[1], 0)
+        q, s, a, z = T["qx%d" % R], T["sx%d" % R], CUT[k], CUT[k + 1]
+        put("s", xkeys(R, a, z), T.oc[:, 4 * a:4 * z], raw(q[:, a:z]))
+        if k in (0, NS - 1):
+            a = CUT[min(k, 1)]
             for i in range(4):
-                put("sa"[i // 2 * (k > 0)], xkeys(R, a, z), T.osc[4 * i:4 * i + 4, o:o + z - a], s[32 * i:32 * i + 4, a:z])
+                put("sa"[i // 2 * (k > 0)], xkeys(R, a, z), T.osc[4 * i:4 * i + 4, a:z], s[32 * i:32 * i + 4, a:z])
 
-    def scores(r, k):
-        if r < R:
-            own_mm(r, k)
-        else:
-            a, z = behind(k)
-            mm(7, z - a, T.vq[:], T.vs[:], T["qx%d" % R][:, a:z], T["sx%d" % R][:, a:z], ["vq"] + xkeys(R, a, z))
+    def result(k, q, b):
+        move(q, T.yo[:, CUT[k]:CUT[k + 1]], piece(k, b), ["ps%d" % b], ["yo%d" % k])
+        if k in (0, NS - 1):
+            a, z = CUT[min(k, 1)], CUT[k + 1]
+            put("a" if k else "s", keys("yo", k + 1), T.y[:, a:z], T.yo[:, a:z])
 
-    def rows(r, k):
-        if r < R:
-            own_row(k)
-            own_windows(k)
-            return
-        a, z = CUT[k], CUT[k + 1]
-        if k == NS - 1:
-            cp(T.yo[:, a:z], bank(7, z - a, a - behind(k)[0]), ["ps7"], ["yo%d" % k])
-        else:
-            act(T.yo[:, a:z], bank(7, z - a, a - behind(k)[0]), ACT.Copy, ["ps7"], ["yo%d" % k])
-        if k == 0:
-            put("s", ["yo0"], T.y[:, PLACE[0]:C], T.yo[:, a:z])
-        elif k == NS - 1:
-            put("a", ["yo1", "yo2"], T.y[:, 0:PLACE[0]], T.yo[:, CUT[1]:C])
+    dma("s", [], ["x00"], T.x0[:, 0:4 * CUT[1]], T.x[:, 0:4 * CUT[1]], DMA + 0.2)
+    dma("s", [], ["ut"], T.ut[:], T.u[:], DMA + 0.8)
+    dma("s", [], ["x01"], T.x0[:, 4 * CUT[1]:4 * C], T.x[:, 4 * CUT[1]:4 * C], DMA + 1.7)
+    iota("pi", T.pi[:], [[0, 8]], 0, 1)
+    iota("li", T.li[:], [[16, 8]], 0, 0)
+    iota("i16", T.i16[:], [[0, 10], [1, 16]], 0, 0)
+    iota("t48", T.t48[:], [[0, 8], [1, W]], 0, 0)
+    iota("ik", T.ik[:], [[16, NB]], 0, 0)
+    iota("cdv", T.cdv[:], [[1, W]], -V, 0)
+    fill(T.one[:], 1.0, ["one"])
+    ts(T.pa[:], T.pi[:], 15, None, ALU.bitwise_and, None, ["pi"], ["pa"])
+    cp(T.lu[:], T.li[:], ["li"], ["lu"])
+    ts(T.pd[:], T.pi[:], 2, 3, ALU.arith_shift_right, ALU.bitwise_and, ["pi"], ["pd"])
+    cp(PL, T.pa[:, 0:1], ["pa"], ["pl"])
+    ts(T.pc[:], T.pi[:], 3, None, ALU.bitwise_and, None, ["pi"], ["pc"])
+    cp(PA, T.pd[:, 0:1], ["pd"], ["pac"])
+    ts(NQ, PL, -1.0, -float(V), ALU.mult, ALU.add, ["pl"], ["nq"])
+    ts(T.dm[:], T.i16[:], PL, None, ALU.is_equal, None, ["i16", "pl"], ["dm"])
+    ts(T.rs[:], T.i16[:], 0.0, None, ALU.is_gt, None, ["i16"], ["rs"])
+    fill(T.pm[:, 0:1], BIG, ["pm-1"])
+    fill(T.rp[:, 0:2 * V], 0.0, cols("rp", 0, 2 * V))
+    fill(T.dgs[:], 0.0, ["dgs"])
+    if BOTH < NB:
+        fill(T.pm[:, W * (NB + BOTH):W * (NB + BOTH) + 1], BIG, ["pm%d" % (NB + BOTH - 1)])
+        ts(T.lj[:], T.ik[:], 1.0 / 16, None, ALU.mult, None, ["ik"], ["lj"])
+    ts(VQ, PL, 1.0 - 4 * V, None, ALU.add, None, ["pl"], ["vq_"])
+    ts(T2, PA, 0.0, 4.0, ALU.is_equal, ALU.mult, ["pac"], ["t2"])
+    ts(PB, T.pc[:, 0:1], -64.0, None, ALU.add, None, ["pc"], ["pbc"])
+    ts(T4, PA, 32.0, None, ALU.add, None, ["pac"], ["t4"])
+    ts(AM, PA, T2, -1.0, ALU.add, ALU.add, ["pac", "t2"], ["am"])
+    ts(T.ya[:], T.i16[:, 0:4], PA, None, ALU.is_equal, None, ["i16", "pac"], ["ya"])
+    ts(CY, T2, 224.0, PB, ALU.mult, ALU.add, ["t2", "pbc"], ["cy"])
+    ts(T.yb[:], T.i16[:, 0:4], AM, -224.0, ALU.is_equal, ALU.mult, ["i16", "am"], ["yb"])
+    ts(T.yc[:], T.ya[:], T4, None, ALU.mult, None, ["ya", "t4"], ["yc"])
+    ts(T.c1[:], T.ik[:], PL, 1.0, ALU.add, ALU.add, ["ik", "pl"], ["c1"])
+    tt(T.yd[:], T.yc[:], T.yb[:], ALU.add, ["yc", "yb"], ["yd"])
+    act(T.ta[:], T.t48[:], ACT.Abs, ["t48", "nq"], ["ta"], bias=NQ)
+    act(T.rst[:], T.t48[:], ACT.Relu, ["t48"], ["rst"], bias=BIG, scale=-BIG)
+    act(T.mk[:], T.ta[:], ACT.Relu, ["ta"], ["mk"], bias=-V * BIG, scale=BIG)
+    quant(T.uq[:], T.us[:], T.ut[:], ["ut"], ["uq"])
+    quant(T.qx0[:, 0:CUT[1]], T.sx0[:, 0:CUT[1]], T.x0[:, 0:4 * CUT[1]], ["x00"], ["qx00"])
+    act(T.urs[:], T.us[:].indirect(T.lu[:]), ACT.Copy, ["uq", "lu"], ["urs"], True)
+    cp(words(T.urq[:]), words(T.uq[:]).indirect(T.lu[:]), ["uq", "lu"], ["urq"], True)
+    quant(T.qx0[:, CUT[1]:C], T.sx0[:, CUT[1]:C], T.x0[:, 4 * CUT[1]:4 * C], ["x01"], slots("qx0", 1, NS))
+    for k in range(NS):
+        scores(0, k, 7 - k)
+        scores(0, k, 3 - k)
+        mask(k, 7 - k)
+        hold(k)
+        own_row(k, 3 - k)
+    ship(0, 0, lambda: (tell(0, 0, "v"), tell(0, NS - 1, "v", 1)))
+    ship(0, 1)
+    op("g", ["one"], ["et"], 1200 * CYCLE, lambda e: e.affine_select(T.et[:], T.one[:], [[1, 516]], ALU.is_equal, 0.0, -3, -4))
+    iota("cyc", T.cyc[:], [[0, 4], [1, 128]], 0, 0)
+    iota("iy", T.iy[:], [[4, 96]], 0, 0)
+    for k in range(1, NS):
+        a, z = 4 * CUT[k + 1], 4 * ahead(k)[1]
+        if a < z:
+            act(T.x1[:, a:z], T.one[:, 0:z - a], ACT.Identity, ["one", "x1z"], ["x1z"] + keys("x1%d" % (k + 1), 4), scale=0.0)
+    dma("s", ["dgl0_%d" % (NS - 1)], ["wq"], raw(T.wq[:]), T.wc[:])
+    dma("s", ["dgl0_%d" % (NS - 1)], ["wp"], T.wp[:], T.ws[:])
+
+    def patterns():
+        for k in range(NS):
+            a, z = CUT[k] // 4, CUT[k + 1] // 4
+            act(T.ir[:, a:z], T.iy[:, a:z], ACT.Identity, ["iy"], ["ir%d" % k], bias=-float(CUT[k]))
+        for i in range(4):
+            act(T.ky[:, i:C:4], T.ir[:], ACT.Identity, ["ya", "yd"] + keys("ir", NS), ["ky%d" % i],
+                scale=T.ya[:, i:i + 1], bias=T.yd[:, i:i + 1])
 
     for r in range(R):
-        far_mm(r, 0, 5)
-        far_mm(r, 0, 4)
-        far_row(0, 4, 0, "v")
-        far_row(0, 5, 1, "a")
-        rows(r, NS - 1 if r else 1)
+        for p, batches in enumerate(MATCH):
+            far_row(r, p)
+            for a, z, q in batches:
+                diffs(r, a, z)
+                least(a, z)
+                for f in ((final, signs) if q == "a" else (flags, tally, counted)):
+                    f(a, z)
+            answer(r, p)
+            theirs(r, p, THEIRS[p])
+            for a, z in CHECK[p]:
+                check(r, a, z)
         if r == 0:
-            later(0)
-        windows(0)
+            for b in range(4):
+                quant(T.eq[:, 128 * b:128 * b + 128], T.es[:, 128 * b:128 * b + 128], T.et[:, 3 - b:515 - b], ["et"], ["eq%d" % b])
+        unpack(T["lq%d" % r], T["ls%d" % r], 4, landed(r, 0, C))
+        unpack(T["qx%d" % r], T["sx%d" % r], 0, xkeys(r, 0, C))
+        for b in range(4):
+            evac_p(b, EVAC[b])
         if r == 0:
-            later(1)
-        if r == R - 1:
+            patterns()
+        if r == 1:
+            dma("s", ["dgl1_%d" % (NS - 1)], ["vt"], T.vt[:], T.v[:])
             quant(T.vq[:], T.vs[:], T.vt[:], ["vt"], ["vq"])
-        diffs(0, 6)
-        least(0, 6)
-        diffs(6, 16)
-        far_rows(r, 1)
-        signs(0, 6)
-        if r == 0:
-            later(2)
-        windows(1)
-        least(6, 16)
-        near = topo.chip(mate[r]) == topo.chip(core)
-        if near:
-            far_rows(r, 2)
-        diffs(16, 32)
-        above(6, 16)
-        counted(0, 6)
-        least(16, 23)
-        if near:
-            windows(2)
-        else:
-            far_rows(r, 2)
-        if r == 0:
-            later(3)
-        least(23, 32)
-        if not near:
-            windows(2)
-        unpack(T["lq%d" % r], T["ls%d" % r], landed(r, 0, C))
-        signs(16, 23)
-        if r == 0:
-            later(4)
-        above(23, 32)
-        diffs(32, 38)
-        tally(6, 16)
-        tally(23, 32)
-        counted(16, 23)
-        diffs(38, 48)
-        least(32, 38)
-        lay("a")
-        least(38, 44)
-        pack("a")
-        least(44, 48)
-        signs(32, 44)
-        if r == 0:
-            later(5)
-        above(44, 48)
-        sixteenth("a")
-        tally(44, 48)
-        counted(32, 44)
-        theirs("a")
-        minus("a", "a")
-        reach(240, C)
-        lay("b")
-        reach(0, 112)
-        pack("b")
-        if r == 0:
-            last()
-        else:
-            evac_p(0)
-        check(0)
-        check(1)
-        sixteenth("b")
-        theirs("b")
-        minus("b", "v")
-        reach(112, 240)
-        other(256, C)
-        other(0, 96)
-        kept(256, C, 4, 16)
-        check(2)
-        evac_p(1)
-        kept(0, 96, 4, 144)
-        other(96, 256)
-        kept(240, 256, 4, 0)
-        kept(96, 240, 5, 0)
-        evac_p(2)
-        evac_p(3)
-        act(T.pp[:, 0:4 * V], T.pp[:, 4 * C:4 * (C + V)], ACT.Copy, keys("pp", 4), ["ppa"])
-        act(T.pp[:, 4 * (C + V):4 * XW], T.pp[:, 4 * V:8 * V], ACT.Copy, keys("pp", 4), ["ppz"])
-        unpack(T["qx%d" % r], T["sx%d" % r], xkeys(r, 0, C))
-        carry(T.l1[:], 0.0, [], ["l1"], False)
-        carry(T.h1[:, ::-1], 0.0, [], ["h1"], True)
-        carry(T.lh[:, 2 * C - 1:C - 1:-1], T.l1[:, C - 1:C], ["l1"], ["h"], True)
-        carry(T.lh[:, 0:C], T.h1[:, 0:1], ["h1"], ["l"], False)
-        pick(T.lh[:, C:2 * C], "exh", "h")
-        pick(T.lh[:, 0:C], "exl", "l")
+        ends_p()
+        carry("l1", 0, 0, C, 0.0, [])
+        carry("h1", 0, 0, C, 0.0, [], True)
+        carry("lh", C, 0, C, T.l1[:, C - 1:C], cols("l1", C - 16, C), True)
+        carry("lh", 0, 0, C, T.h1[:, 0:1], cols("h1", 0, 16))
+        pick(C, "exh")
+        pick(0, "exl")
         offsets("fh", "exh")
         offsets("fl", "exl")
+        for a, z, q in TAKES:
+            take_h(a, z, q)
         if r == R - 1:
-            dma("g", ["l", "h"], [], T.od[:], T.lh[0:128:16, :])
+            dma("g", cols("lh", 0, 2 * C), [], T.od[:], T.lh[0:128:16, :])
         n = r + 1
-        a, m, z = SUB
-        take_h(0, 0, a)
-        take_h(0, a, m)
-        take_h(1, CUT[1], CUT[2])
-        take_h(0, m, z, "v")
-        take_l(0, 0, a)
-        take_l(0, m, z)
-        take_l(0, a, m)
-        take_h(2, CUT[2], CUT[3])
-        quant_y(0)
-        layers(0)
-        relus(0, 0, 4)
-        take_l(1, CUT[1], CUT[2])
-        adds(0, 0, 4)
-        quant_y(1)
-        quant_x(n, 0)
-        onward(n, 0)
-        layers(1)
-        relus(1, 0, 1)
-        scores(n, 0)
-        relus(1, 1, 4)
-        take_l(2, CUT[2], CUT[3])
-        rows(n, 0)
-        adds(1, 0, 1)
-        quant_y(2)
-        adds(1, 1, 4)
-        quant_x(n, 1)
-        onward(n, 1)
-        layers(2)
-        relus(2, 0, 1)
-        scores(n, 1)
-        relus(2, 1, 4)
-        adds(2, 0, 4)
-        if n < R:
-            spread_u(n)
-        rows(n, 1)
-        quant_x(n, 2)
-        onward(n, 2)
-        scores(n, 2)
-    rows(R, NS - 1)
-    for s in count:
-        if count[s] and max(known[q].get(s, 0) for q in known) < count[s]:
-            g.wait_ge(T.sem[s], count[s])
+
+        def made(k):
+            for a, z, _ in sorted(TAKES, key=lambda t: (t[0] > 0, t[2] == "a")):
+                if CUT[k] <= a < CUT[k + 1]:
+                    take_l(a, z)
+            quant_y(k)
+
+        def layer(k):
+            for b in range(4):
+                layers(k, b, b + 1)
+                relus(k, b, b + 1)
+
+        def state(k):
+            adds(k, 0, 4)
+            quant_x(n, k)
+            scores(n, k)
+
+        def told(k):
+            last = k == NS - 1
+            if n == R:
+                onward(n, k)
+                result(k, "av"[last], 7)
+                return
+            if last:
+                scores(n, k, 5)
+            mask(k)
+            hold(k)
+            tell(n, k, TELL[k])
+            own_row(k, 5 if last else 7)
+            onward(n, k)
+
+        for name, k in STATE:
+            {"m": made, "l": layer, "s": state, "t": told}[name](int(k))
+    issue_all()

@@ -11,14 +11,18 @@ NS = len(CUT) - 1
 PAD = max(C, CUT[NS - 1] + 128)
 STATE = "m0 l0 m1 s0 l1 m2 t0 s1 l2 t1 s2 t2".split()
 TELL = "aav"
+WIN = [0, 160, 288, 384]
+WIDE = max(_z - _a for _a, _z in zip(CUT, CUT[1:]))
 TAKES = [(0, 32, "a"), (32, 112, "a"), (112, 160, "v"), (160, 288, "a"), (288, 384, "a")]
 PARTS = [(0, 10), (10, 18), (18, 24)]
 BOTH = 24
-MATCH = [[(1, 4, "a"), (4, 10, "a"), (0, 1, "a")], [(10, 14, "a"), (14, 18, "a")], [(18, 20, "a"), (20, 22, "a"), (22, 24, "v")]]
+MATCH = [[(0, 3, "a"), (3, 6, "a"), (6, 10, "a")], [(10, 12, "a"), (12, 15, "v"), (15, 18, "a")], [(18, 20, "a"), (20, 22, "a"), (22, 24, "a")]]
+FIRST_MATCH = [[(0, 3, "a"), (3, 6, "a"), (6, 10, "a")], [(10, 13, "v"), (13, 16, "v"), (16, 18, "a")], [(18, 21, "a"), (21, 24, "a")]]
+FILL = ("vq", "eq", "et", "cyc", "x1z", "vt")
 OWN = [[], [], []]
 CHECK = [[], [], [(0, 10), (10, 18), (18, 24)]]
 THEIRS = "aav"
-EVAC = "avav"
+EVAC = "aava"
 ONE = 6
 AT, END, TURNED = [], [], []
 for _k in range(NS):
@@ -34,8 +38,9 @@ for _k in range(NS):
     END.append(_c)
 DW = (END[-1] + 7) // 8 * 8
 BIG = 2.0 ** 90
-TIMES = (0.00083, 0.2, 0.3, 1.8, 1.55, 1e-9, 3, 1.5)
-CYCLE, WAKE, ISSUE, HOP, DMA, SLACK, TURNS, FIRST = TIMES
+TIMES = (0.00083, 0.2, 0.3, 1.8, 1.55, 1.5)
+CYCLE, WAKE, ISSUE, HOP, DMA, FIRST = TIMES
+TURNS = 4000
 CORES = 64
 NEAR = (0, 0, 0, 0)
 RUNS = [[(0, 160, NEAR, NEAR), (160, 384, NEAR, NEAR)],
@@ -61,12 +66,12 @@ for _n, _w, _t in [
         ("uq", 128, Q4), ("us", 128, U8), ("urq", 128, Q4), ("urs", 128, U8), ("vq", 128, Q4), ("vs", 128, U8),
         ("wq", 512, Q4), ("wp", 512, U8), ("hq", C, Q4), ("hs", C, U8),
         ("pi", 8, I32), ("pa", 8, I32), ("pc", 8, I32), ("pd", 8, I32), ("li", 8, I32), ("lu", 8, U16),
-        ("ik", 24, F32), ("iy", 96, F32), ("col", 24, F32), ("i16", 160, F32), ("dm", 160, F32), ("rs", 160, F32),
+        ("ik", 24, F32), ("iy", 96, F32), ("col", 24, F32), ("i16", WIDE, F32), ("dm", WIDE, F32), ("rs", WIDE, F32),
         ("t48", 8 * W, F32), ("ta", 8 * W, F32), ("mk", 8 * W, F32), ("rst", 8 * W, F32), ("one", 516, BF),
         ("c1", NB, F32), ("cyc", 512, BF), ("cdv", W, BF),
         ("ya", 4, F32), ("yb", 4, F32), ("yc", 4, F32), ("yd", 4, F32), ("ky", C, BF),
         ("et", 516, BF), ("eq", 512, Q4), ("es", 512, U8),
-        ("msk", C, F32), ("hold", C, F32), ("dgs", R * DW, F32), ("dgl", R * DW, F32), ("ow", XW, F32),
+        ("msk", C, F32), ("hold", C, F32), ("dgs", R * DW, F32), ("dgl", R * DW, F32), ("mw", NB * W, F32),
         ("tr", C, F32), ("bc", C, F32), ("fw", XW + V, F32), ("lj", NB, U16), ("mm", 2 * NB, U16),
         ("dd", 2 * NB * W, F32), ("pm", 2 * NB * W + 1, F32), ("p2", 2 * NB * W, F32), ("sj", 2 * NB * W, BF),
         ("nf", 2 * NB * W, BF), ("cnt", 2 * NB * W, BF),
@@ -127,6 +132,77 @@ def _hand_on(g, core, T, topo):
                 g.wait_ge(T.sem.sent, sent)
 
 
+_laid = []
+
+
+def _lay_out(calls):
+    n = len(calls)
+    queue, busy, late = [c[0] for c in calls], [c[2] for c in calls], [c[3] for c in calls]
+    before = [[(j, late[j] + WAKE if c[0] else busy[j]) for j in c[1]] for c in calls]
+    after = [[] for _ in calls]
+    for i in range(n):
+        for j, gap in before[i]:
+            after[j].append((i, gap + busy[i] - busy[j]))
+
+    def lay(turn, back=False):
+        turn = list(turn)
+        for i in (range(n - 1, -1, -1) if back else range(n)):
+            for j, _ in (after[i] if back else before[i]):
+                if turn[i] <= turn[j]:
+                    turn[i] = turn[j] + 1e-7
+        at, taken = [0.0] * n, {}
+        for i in sorted(range(n), key=lambda i: turn[i]):
+            t = late[i] - busy[i] if back else 0.0
+            for j, gap in (after[i] if back else before[i]):
+                if at[j] + gap > t:
+                    t = at[j] + gap
+            if queue[i]:
+                runs = taken.setdefault(queue[i], [])
+                k = len(runs)
+                while k and runs[k - 1][1] > t:
+                    k -= 1
+                while k < len(runs) and t + busy[i] > runs[k][0] + 1e-9:
+                    t = max(t, runs[k][1])
+                    k += 1
+                runs.insert(k, (t, t + busy[i]))
+            at[i] = t
+        return at
+
+    def worth(at):
+        return max(at[i] + late[i] for i in range(n)) + 0.1 * sum(at) / n
+
+    def mirrored(at):
+        end = lay([-at[i] - busy[i] for i in range(n)], True)
+        return [max(end) - end[i] - busy[i] for i in range(n)]
+
+    best = lay(range(n))
+    for _ in range(3):
+        best = min(best, lay(mirrored(best)), key=worth)
+    least, seed = worth(best), [1]
+
+    def chance():
+        seed[0] = seed[0] * 48271 % 2147483647
+        return seed[0] / 2147483647
+
+    for _ in range(TURNS):
+        kind, mid, wide, far = chance(), chance(), chance(), chance()
+        near = [i for i in range(n) if abs(best[i] - mid * least) < 0.3 + 2.2 * wide]
+        turn = list(best)
+        if kind < 0.2:
+            other = mirrored(best)
+            for i in near:
+                turn[i] = other[i]
+        elif kind < 0.6 and near:
+            turn[near[int(chance() * len(near))]] += 3 * far - 1.5
+        else:
+            for i in near:
+                turn[i] += far * (chance() - 0.5)
+        at = lay(turn)
+        if worth(at) <= least:
+            best, least = at, worth(at)
+    return best
+
+
 def rank_program(g, core, T, topo):
     rank = T.rank_of(core)
     if rank is None:
@@ -148,7 +224,7 @@ def rank_program(g, core, T, topo):
             if k in writer:
                 before.add(writer[k])
             before.update(readers.get(k, []))
-        calls.append((q, before, busy, late, issue))
+        calls.append((q, before, busy, late, issue, any(k.startswith(FILL) for k in w)))
         for k in r:
             readers.setdefault(k, []).append(len(calls) - 1)
         for k in w:
@@ -243,42 +319,9 @@ def rank_program(g, core, T, topo):
 
     def issue_all():
         n = len(calls)
-        behind_it = [[] for _ in calls]
-        for i in range(n):
-            for j in calls[i][1]:
-                behind_it[j].append(i)
-
-        def gap(j, i):
-            return calls[j][3] + WAKE if calls[i][0] else calls[j][2]
-
-        def lay(first, back):
-            at, taken = [0.0] * n, {q: [] for q in queue}
-            for i in sorted(range(n), key=lambda i: (first[i], -i if back else i)):
-                q, busy = calls[i][0], calls[i][2]
-                if back:
-                    t = max([at[j] + calls[j][2] + gap(i, j) - busy for j in behind_it[i]] + [calls[i][3] - busy])
-                else:
-                    t = max([at[j] + gap(j, i) for j in calls[i][1]] + [0.0])
-                if q:
-                    for a, z in taken[q]:
-                        if t + busy > a + SLACK and t < z:
-                            t = z
-                    taken[q].append((t, t + busy))
-                    taken[q].sort()
-                at[i] = t
-            return at
-
-        chain = [c[3] for c in calls]
-        for i in range(n - 1, -1, -1):
-            for j in calls[i][1]:
-                chain[j] = max(chain[j], gap(j, i) + chain[i])
-        start = best = lay(list(range(n)), False)
-        for _ in range(TURNS):
-            late = lay([-start[i] for i in range(n)], True)
-            start = lay([-late[i] - calls[i][2] for i in range(n)], False)
-            if max(start[i] + calls[i][3] for i in range(n)) < max(best[i] + calls[i][3] for i in range(n)):
-                best = start
-        start = best
+        if not _laid:
+            _laid.append(_lay_out(calls))
+        start = _laid[0]
         known = {q: {} for q in queue}
         done = {}
         for i in sorted(range(n), key=lambda i: (start[i], i)):
@@ -340,7 +383,7 @@ def rank_program(g, core, T, topo):
         near = topo.chip(mate[r]) == topo.chip(core)
         arrives(sem, len(topo.engines(mate[r], core)), w, HOP + (0.0 if near else WAKE), [write(rd, mate[r], out, in_, sem, ["told"])])
 
-    PL, PA, PB, AM, CY, T2, T4, NQ, VQ, C4, CL, T5, T6 = [T.col[:, k:k + 1] for k in range(13)]
+    PL, PA, PB, AM, CY, T2, T4, NQ, MQ, WQ = [T.col[:, k:k + 1] for k in range(10)]
 
     def scores(r, k, b=7):
         a, z = behind(k)
@@ -351,12 +394,13 @@ def rank_program(g, core, T, topo):
         a, z = (CUT[k], CUT[k + 1]) if a is None else (a, z)
         return bank(b, z - a, a - behind(k)[0])
 
-    def own_row(k, b=7):
-        if k == NS - 1:
-            act(T.ow[:, 0:V], piece(k, b, C - V, C), ACT.Copy, ["ps%d" % b], cols("ow", 0, V))
-        act(T.ow[:, V + CUT[k]:V + CUT[k + 1]], piece(k, b), ACT.Copy, ["ps%d" % b], cols("ow", V + CUT[k], V + CUT[k + 1]))
-        if k == 0:
-            act(T.ow[:, V + C:XW], piece(k, b, 0, V), ACT.Copy, ["ps%d" % b], cols("ow", V + C, XW))
+    def windows(r, a, b):
+        if a == 0:
+            mm(0, C, T.urq[:], T.urs[:], T["qx%d" % r][:, 0:C], T["sx%d" % r][:, 0:C], ["urq", "urs"] + xkeys(r, 0, C))
+        for i in range(a, b):
+            j = 16 * i - V
+            for x, y in ((0, V), (V, W)) if j < 0 else ((0, 2 * V), (2 * V, W)) if j + W > C else ((0, W),):
+                tt(T.mw[:, W * i + x:W * i + y], bank(0, y - x, (j + x) % C), T.mk[:, x:y], ALU.add, ["ps0", "mk"], ["mw%d_%d" % (i, x)])
 
     def mask(k, b=7):
         a, z = CUT[k], CUT[k + 1]
@@ -395,65 +439,58 @@ def rank_program(g, core, T, topo):
     def diffs(r, a, b):
         for i in range(a, b):
             k = max(k for k in range(NS) if CUT[k] <= 16 * (i % NB))
-            if i < NB:
-                c = DW * r + AT[k] + i - CUT[k] // 16
-                row, mid, rd = T.ow[:, 16 * i:16 * i + W], T.dgl[:, c:c + 1], slots("ow", i, i + 3) + ["dgl%d_%d" % (r, k)]
-            else:
-                j = i - NB
-                row, mid, rd = T.fw[:, 16 * j:16 * j + W], T.hold[:, 16 * j + 15:16 * j + 16], slots("fw", j, j + 3) + ["hold%d" % k]
-            act(T.dd[:, W * i:W * i + W], row, ACT.Abs, rd, ["dd%d" % i], bias=mid, scale=-1.0)
+            c = DW * r + AT[k] + i - CUT[k] // 16
+            act(T.dd[:, W * i:W * i + W], T.mw[:, W * i:W * i + W], ACT.Abs, ["mw%d_%d" % (i, x) for x in (0, V, 2 * V)] + ["dgl%d_%d" % (r, k)],
+                ["dd%d" % i], bias=T.dgl[:, c:c + 1], scale=-1.0)
 
     def least(a, b):
-        scan(T.pm[:, 1 + W * a:1 + W * b], T.dd[:, W * a:W * b], T.mk[:, 0:W * (b - a)], BIG, ALU.min, ALU.max,
-             ["mk"] + slots("dd", a, b), slots("pm", a, b))
-
-    def final(a, b):
-        scan(T.p2[:, W * a:W * b], T.rst[:, 0:W * (b - a)], T.pm[:, 1 + W * a:1 + W * b], 0.0, ALU.add, ALU.min,
-             ["rst"] + slots("pm", a, b), slots("p2", a, b))
+        scan(T.p2[:, W * a:W * b], T.rst[:, 0:W * (b - a)], T.dd[:, W * a:W * b], 0.0, ALU.add, ALU.min,
+             ["rst"] + slots("dd", a, b), slots("p2", a, b))
 
     def signs(a, b):
         for i in range(a, b):
-            act(T.sj[:, W * i:W * i + W], T.pm[:, 1 + W * i:1 + W * i + W], ACT.Sign, ["pm%d" % i, "p2%d" % i], ["acc%d" % i],
+            act(T.sj[:, W * i:W * i + W], T.p2[:, W * i:W * i + W], ACT.Sign, ["p2%d" % i], ["acc%d" % i],
                 bias=T.p2[:, W * i + W - 1:W * i + W], scale=-1.0, accum_out=T.acc[:, i:i + 1])
+
+    def fallen(a, b):
+        scan(T.pm[:, 1 + W * a:1 + W * b], T.dd[:, W * a:W * b], T.mk[:, 0:W * (b - a)], BIG, ALU.min, ALU.max,
+             ["mk"] + slots("dd", a, b), slots("pm", a, b))
 
     def flags(a, b):
         tt(T.nf[:, W * a:W * b], T.pm[:, 1 + W * a:1 + W * b], T.pm[:, W * a:W * b], ALU.is_ge,
-           slots("pm", a - 1, b), slots("nf", a, b))
+           ["pm"] + slots("pm", a - 1, b), slots("nf", a, b))
 
     def tally(a, b):
         scan(T.cnt[:, W * a:W * b], T.nf[:, W * a:W * b], T.one[:, 0:W * (b - a)], 0.0, ALU.mult, ALU.add,
              ["one"] + slots("nf", a, b), slots("cnt", a, b), 0.5)
 
     def counted(a, b):
-        ts(T.acc[:, a:b], T.cnt[:, W * a + W - 1:W * b:W], VQ, None, ALU.add, None, slots("cnt", a, b) + ["vq_"], slots("acc", a, b))
+        ts(T.acc[:, a:b], T.cnt[:, W * a + W - 1:W * b:W], -float(W), None, ALU.add, None, slots("cnt", a, b), slots("acc", a, b))
 
     def lists(t, r, p):
         a, z = PARTS[p]
         o = 2 * (NB * r + a)
         return t[:, o:o + z - a], t[:, o + z - a:o + 2 * (z - a)], t[:, o:o + 2 * (z - a)]
 
-    def places(t, o, a, z, w):
-        if z - a > ONE:
-            tt(T.pf[:, a:z], T.c1[:, a % NB:a % NB + z - a], T.acc[:, a:z], ALU.subtract, ["c1"] + slots("acc", a, z), slots("pf", a, z))
-            cp(t[:, o:o + z - a], T.pf[:, a:z], slots("pf", a, z), w)
-        else:
-            for i in range(a, z):
-                ts(t[:, o + i - a:o + i - a + 1], T.acc[:, i:i + 1], -1.0, T.c1[:, i % NB:i % NB + 1], ALU.mult, ALU.add,
-                   ["acc%d" % i, "c1"], [w[i - a]])
-
-    def steps(out, a, z, w):
-        ts(out, T.acc[:, a:z], -1.0, 1.0 - V, ALU.mult, ALU.add, slots("acc", a, z), w)
-
-    def answer(r, p):
+    def answer(r, p, batches):
         a, z = PARTS[p]
-        mf = slots("mf%d_" % r, a, z)
-        places(T.mo, 2 * (NB * r + a), a, z, mf)
-        if a < BOTH:
-            steps(lists(T.mo, r, p)[1], a, z, ["md%d%d" % (r, p)])
-            swap(r, "ma%d%d" % (r, p), lists(T.ml, r, p)[2], lists(T.mo, r, p)[2], mf + ["md%d%d" % (r, p)], ["ml%d%d" % (r, p)])
-        for a, z in OWN[p]:
-            places(T.mm, a, NB + a, NB + z, slots("mm", a, z))
-            steps(T.mm[:, NB + a:NB + z], NB + a, NB + z, slots("mm", NB + a, NB + z))
+        o, mf, md = 2 * (NB * r + a) - a, slots("mf%d_" % r, a, z), slots("md%d_" % r, a, z)
+        if z - a > ONE:
+            for x, y, q in batches:
+                if q == "v":
+                    counted(x, y)
+            tt(T.pf[:, a:z], T.ik[:, a:z], T.acc[:, a:z], ALU.subtract, ["ik"] + slots("acc", a, z), slots("pf", a, z))
+            ts(T.mo[:, o + z:o + 2 * z - a], T.acc[:, a:z], -1.0, MQ, ALU.mult, ALU.add, ["mq"] + slots("acc", a, z), md)
+            cp(T.mo[:, o + a:o + z], T.pf[:, a:z], slots("pf", a, z), mf)
+        else:
+            for x, y, q in batches:
+                def got(i, k):
+                    return T.acc[:, i:k] if q == "a" else T.cnt[:, W * i + W - 1:W * k:W]
+                name, c, col = ("acc", V, MQ) if q == "a" else ("cnt", V + W, WQ)
+                for i in range(x, y):
+                    ts(T.mo[:, o + i:o + i + 1], got(i, i + 1), -1.0, float(16 * i + c), ALU.mult, ALU.add, [name + str(i)], [mf[i - a]])
+                ts(T.mo[:, o + z - a + x:o + z - a + y], got(x, y), -1.0, col, ALU.mult, ALU.add, ["mq"] + slots(name, x, y), md[x - a:y - a])
+        swap(r, "ma%d%d" % (r, p), lists(T.ml, r, p)[2], lists(T.mo, r, p)[2], mf + md, ["ml%d%d" % (r, p)])
 
     def mine(r, a, z, i):
         if a >= BOTH:
@@ -512,8 +549,8 @@ def rank_program(g, core, T, topo):
     plane = keys("pp", 4) + ["ppa", "ppz"]
 
     def source(a, z, off):
-        k = max(i for i in range(NS) if CUT[i] <= a)
-        return T.pp[:, 4 * CUT[k]:4 * (CUT[k + 1] + 2 * V)].indirect(T[off][:, a // 4:z // 4])
+        k = max(i for i in range(len(WIN)) if WIN[i] <= a)
+        return T.pp[:, 4 * WIN[k]:4 * (WIN[k + 1] + 2 * V)].indirect(T[off][:, a // 4:z // 4])
 
     def take_h(a, z, q="a"):
         move(q, T.gh[:, 4 * a:4 * z], source(a, z, "fh"), plane + ["fh"], cols("gh", a, z), True)
@@ -528,13 +565,13 @@ def rank_program(g, core, T, topo):
     def layers(k, b0=0, b1=4):
         a, z = behind(k)
         for b in range(b0, b1):
-            mm(4 + (4 * k + b) % 3, z - a, T.wq[:, 128 * b:128 * b + 128], T.wp[:, 128 * b:128 * b + 128], T.yq[:, a:z], T.ys[:, a:z],
+            mm(4 + b, z - a, T.wq[:, 128 * b:128 * b + 128], T.wp[:, 128 * b:128 * b + 128], T.yq[:, a:z], T.ys[:, a:z],
                ["wq", "wp"] + cols("yq", a, z))
 
     def relus(k, b0, b1):
         a, z = CUT[k], CUT[k + 1]
         for b in range(b0, b1):
-            c = 4 + (4 * k + b) % 3
+            c = 4 + b
             act(T.rb[:, C * b + a:C * b + z], piece(k, c), ACT.Relu, ["ps%d" % c], ["rb%d%d" % (k, b)], scale=0.03125)
 
     def adds(k, b0, b1):
@@ -571,9 +608,9 @@ def rank_program(g, core, T, topo):
     dma("s", [], ["x01"], T.x0[:, 4 * CUT[1]:4 * C], T.x[:, 4 * CUT[1]:4 * C], DMA + 1.7)
     iota("pi", T.pi[:], [[0, 8]], 0, 1)
     iota("li", T.li[:], [[16, 8]], 0, 0)
-    iota("i16", T.i16[:], [[0, 10], [1, 16]], 0, 0)
+    iota("i16", T.i16[:], [[0, WIDE // 16], [1, 16]], 0, 0)
     iota("t48", T.t48[:], [[0, 8], [1, W]], 0, 0)
-    iota("ik", T.ik[:], [[16, NB]], 0, 0)
+    iota("ik", T.ik[:], [[16, NB]], V, 0)
     iota("cdv", T.cdv[:], [[1, W]], -V, 0)
     fill(T.one[:], 1.0, ["one"])
     ts(T.pa[:], T.pi[:], 15, None, ALU.bitwise_and, None, ["pi"], ["pa"])
@@ -585,13 +622,11 @@ def rank_program(g, core, T, topo):
     ts(NQ, PL, -1.0, -float(V), ALU.mult, ALU.add, ["pl"], ["nq"])
     ts(T.dm[:], T.i16[:], PL, None, ALU.is_equal, None, ["i16", "pl"], ["dm"])
     ts(T.rs[:], T.i16[:], 0.0, None, ALU.is_gt, None, ["i16"], ["rs"])
-    fill(T.pm[:, 0:1], BIG, ["pm-1"])
+    fill(T.pm[:, 0:NB * W + 1:W], BIG, ["pm"])
     fill(T.rp[:, 0:2 * V], 0.0, cols("rp", 0, 2 * V))
     fill(T.dgs[:], 0.0, ["dgs"])
-    if BOTH < NB:
-        fill(T.pm[:, W * (NB + BOTH):W * (NB + BOTH) + 1], BIG, ["pm%d" % (NB + BOTH - 1)])
-        ts(T.lj[:], T.ik[:], 1.0 / 16, None, ALU.mult, None, ["ik"], ["lj"])
-    ts(VQ, PL, 1.0 - 4 * V, None, ALU.add, None, ["pl"], ["vq_"])
+    ts(WQ, PL, -1.0, float(W), ALU.mult, ALU.add, ["pl"], ["wq_"])
+    ts(MQ, PL, -1.0, None, ALU.mult, None, ["pl", "wq_"], ["mq"])
     ts(T2, PA, 0.0, 4.0, ALU.is_equal, ALU.mult, ["pac"], ["t2"])
     ts(PB, T.pc[:, 0:1], -64.0, None, ALU.add, None, ["pc"], ["pbc"])
     ts(T4, PA, 32.0, None, ALU.add, None, ["pac"], ["t4"])
@@ -600,7 +635,6 @@ def rank_program(g, core, T, topo):
     ts(CY, T2, 224.0, PB, ALU.mult, ALU.add, ["t2", "pbc"], ["cy"])
     ts(T.yb[:], T.i16[:, 0:4], AM, -224.0, ALU.is_equal, ALU.mult, ["i16", "am"], ["yb"])
     ts(T.yc[:], T.ya[:], T4, None, ALU.mult, None, ["ya", "t4"], ["yc"])
-    ts(T.c1[:], T.ik[:], PL, 1.0, ALU.add, ALU.add, ["ik", "pl"], ["c1"])
     tt(T.yd[:], T.yc[:], T.yb[:], ALU.add, ["yc", "yb"], ["yd"])
     act(T.ta[:], T.t48[:], ACT.Abs, ["t48", "nq"], ["ta"], bias=NQ)
     act(T.rst[:], T.t48[:], ACT.Relu, ["t48"], ["rst"], bias=BIG, scale=-BIG)
@@ -612,10 +646,8 @@ def rank_program(g, core, T, topo):
     quant(T.qx0[:, CUT[1]:C], T.sx0[:, CUT[1]:C], T.x0[:, 4 * CUT[1]:4 * C], ["x01"], slots("qx0", 1, NS))
     for k in range(NS):
         scores(0, k, 7 - k)
-        scores(0, k, 3 - k)
         mask(k, 7 - k)
         hold(k)
-        own_row(k, 3 - k)
     ship(0, 0, lambda: (tell(0, 0, "v"), tell(0, NS - 1, "v", 1)))
     ship(0, 1)
     op("g", ["one"], ["et"], 1200 * CYCLE, lambda e: e.affine_select(T.et[:], T.one[:], [[1, 516]], ALU.is_equal, 0.0, -3, -4))
@@ -629,22 +661,21 @@ def rank_program(g, core, T, topo):
     dma("s", ["dgl0_%d" % (NS - 1)], ["wp"], T.wp[:], T.ws[:])
 
     def patterns():
-        for k in range(NS):
-            a, z = CUT[k] // 4, CUT[k + 1] // 4
-            act(T.ir[:, a:z], T.iy[:, a:z], ACT.Identity, ["iy"], ["ir%d" % k], bias=-float(CUT[k]))
+        for k in range(len(WIN) - 1):
+            a, z = WIN[k] // 4, WIN[k + 1] // 4
+            act(T.ir[:, a:z], T.iy[:, a:z], ACT.Identity, ["iy"], ["ir%d" % k], bias=-float(WIN[k]))
         for i in range(4):
-            act(T.ky[:, i:C:4], T.ir[:], ACT.Identity, ["ya", "yd"] + keys("ir", NS), ["ky%d" % i],
+            act(T.ky[:, i:C:4], T.ir[:], ACT.Identity, ["ya", "yd"] + keys("ir", len(WIN) - 1), ["ky%d" % i],
                 scale=T.ya[:, i:i + 1], bias=T.yd[:, i:i + 1])
 
     for r in range(R):
-        for p, batches in enumerate(MATCH):
-            far_row(r, p)
+        for p, batches in enumerate(MATCH if r else FIRST_MATCH):
             for a, z, q in batches:
+                windows(r, a, z)
                 diffs(r, a, z)
-                least(a, z)
-                for f in ((final, signs) if q == "a" else (flags, tally, counted)):
+                for f in ((least, signs) if q == "a" else (fallen, flags, tally)):
                     f(a, z)
-            answer(r, p)
+            answer(r, p, batches)
             theirs(r, p, THEIRS[p])
             for a, z in CHECK[p]:
                 check(r, a, z)
@@ -658,8 +689,9 @@ def rank_program(g, core, T, topo):
         if r == 0:
             patterns()
         if r == 1:
-            dma("s", ["dgl1_%d" % (NS - 1)], ["vt"], T.vt[:], T.v[:])
-            quant(T.vq[:], T.vs[:], T.vt[:], ["vt"], ["vq"])
+            dma("s", ["ml10"], ["vt"], T.vt[:], T.v[:], DMA + 1.0)
+        if r == R - 1:
+            quant(T.vq[:], T.vs[:], T.vt[:], ["vt", "dgs%d%d" % (r, NS - 1)], ["vq"])
         ends_p()
         carry("l1", 0, 0, C, 0.0, [])
         carry("h1", 0, 0, C, 0.0, [], True)
@@ -681,29 +713,34 @@ def rank_program(g, core, T, topo):
                     take_l(a, z)
             quant_y(k)
 
+        def turn_of(k):
+            return [(max(k - 1, 0) + b) % 4 for b in range(4)]
+
         def layer(k):
-            for b in range(4):
+            for b in turn_of(k):
                 layers(k, b, b + 1)
                 relus(k, b, b + 1)
 
         def state(k):
-            adds(k, 0, 4)
+            for b in turn_of(k):
+                adds(k, b, b + 1)
             quant_x(n, k)
-            scores(n, k)
 
         def told(k):
             last = k == NS - 1
+            b = 4 + k % 4
+            scores(n, k, b)
             if n == R:
                 onward(n, k)
-                result(k, "av"[last], 7)
+                result(k, "av"[last], b)
                 return
-            if last:
-                scores(n, k, 5)
-            mask(k)
+            if not last:
+                onward(n, k)
+            mask(k, b)
             hold(k)
             tell(n, k, TELL[k])
-            own_row(k, 5 if last else 7)
-            onward(n, k)
+            if last:
+                onward(n, k)
 
         for name, k in STATE:
             {"m": made, "l": layer, "s": state, "t": told}[name](int(k))

from concourse.mybir import dt, AluOpType, ActivationFunctionType

ALU = AluOpType
ACT = ActivationFunctionType
C, V, R = 384, 16, 3
XW = C + 2 * V
NB = C // 16
W = 3 * V
CUT = [0, 160, 288, 384]
NS = len(CUT) - 1
PAD = max(C, CUT[NS - 1] + 128)
STATE = "m0 l0 m1 s0 l1 m2 t0 s1 l2 t1 s2 t2".split()
TELL = "aav"
WIN = [0, 160, 288, 384]
WIDE = max(_z - _a for _a, _z in zip(CUT, CUT[1:]))
TAKES = [(0, 32, "a"), (32, 112, "a"), (112, 160, "v"), (160, 288, "a"), (288, 384, "a")]
PARTS = [(0, 10), (10, 18), (18, 24)]
BOTH = 24
MATCH = [[(0, 3, "a"), (3, 6, "a"), (6, 10, "a")], [(10, 12, "a"), (12, 15, "v"), (15, 18, "a")], [(18, 20, "a"), (20, 22, "a"), (22, 24, "a")]]
FIRST_MATCH = [[(0, 3, "a"), (3, 6, "a"), (6, 10, "a")], [(10, 13, "v"), (13, 16, "v"), (16, 18, "a")], [(18, 21, "a"), (21, 24, "a")]]
FILL = ("vq", "eq", "et", "cyc", "x1z", "vt")
OWN = [[], [], []]
CHECK = [[], [], [(0, 10), (10, 18), (18, 24)]]
THEIRS = "aav"
EVAC = "aava"
ONE = 6
AT, END, TURNED = [], [], []
for _k in range(NS):
    _a, _z = CUT[_k], CUT[_k + 1]
    AT.append((END[-1] + 7) // 8 * 8 if END else 0)
    _c = AT[-1] + (_z - _a) // 16
    _f = max(_a, (16 * BOTH - V) // 32 * 32)
    TURNED.append([])
    for _x, _y, _o in [(0, 32, C + V)] * (_k == 0) + [(_f, _z, _f + V)] * (_f < _z):
        if BOTH < NB:
            TURNED[-1].append((_x, _y, _c, _o))
            _c += (_y - _x) // 16
    END.append(_c)
DW = (END[-1] + 7) // 8 * 8
BIG = 2.0 ** 90
TIMES = (0.00083, 0.2, 0.3, 1.8, 1.55, 1.5)
CYCLE, WAKE, ISSUE, HOP, DMA, FIRST = TIMES
TURNS = 4000
CORES = 64
NEAR = (0, 0, 0, 0)
RUNS = [[(0, 160, NEAR, NEAR), (160, 384, NEAR, NEAR)],
        [(0, 160, NEAR, NEAR), (160, 288, NEAR, NEAR), (288, 384, NEAR, NEAR)],
        [(0, 160, (0, 1, 2, 2), (1, 1, 1, 1)), (160, 288, (1, 1, 2, 2), (1, 1, 1, 1)), (288, 384, NEAR, NEAR)]]
Q4, U8, BF, F32, I32, U16 = "float8_e4m3fn_x4", "uint8", "bfloat16", "float32", "int32", "uint16"

SCRATCH = {"ps": ("psum", [128, 4096], F32)}


def _sb(name, n, ty):
    SCRATCH[name] = ("sbuf", [128, n], ty)


for _r in range(R + 1):
    _sb("qx%d" % _r, PAD, Q4)
    _sb("sx%d" % _r, PAD, U8)
for _r in range(R):
    _sb("lq%d" % _r, C, Q4)
    _sb("ls%d" % _r, C, U8)
for _n, _w, _t in [
        ("x0", 4 * C, BF), ("x1", 4 * PAD, BF), ("ut", 512, BF), ("vt", 512, BF),
        ("uq", 128, Q4), ("us", 128, U8), ("urq", 128, Q4), ("urs", 128, U8), ("vq", 128, Q4), ("vs", 128, U8),
        ("wq", 512, Q4), ("wp", 512, U8), ("hq", C, Q4), ("hs", C, U8),
        ("pi", 8, I32), ("pa", 8, I32), ("pc", 8, I32), ("pd", 8, I32), ("li", 8, I32), ("lu", 8, U16),
        ("ik", 24, F32), ("iy", 96, F32), ("col", 24, F32), ("i16", WIDE, F32), ("dm", WIDE, F32), ("rs", WIDE, F32),
        ("t48", 8 * W, F32), ("ta", 8 * W, F32), ("mk", 8 * W, F32), ("rst", 8 * W, F32), ("one", 516, BF),
        ("c1", NB, F32), ("cyc", 512, BF), ("cdv", W, BF),
        ("ya", 4, F32), ("yb", 4, F32), ("yc", 4, F32), ("yd", 4, F32), ("ky", C, BF),
        ("et", 516, BF), ("eq", 512, Q4), ("es", 512, U8),
        ("msk", C, F32), ("hold", C, F32), ("dgs", R * DW, F32), ("dgl", R * DW, F32), ("mw", NB * W, F32),
        ("tr", C, F32), ("bc", C, F32), ("fw", XW + V, F32), ("lj", NB, U16), ("mm", 2 * NB, U16),
        ("dd", 2 * NB * W, F32), ("pm", 2 * NB * W + 1, F32), ("p2", 2 * NB * W, F32), ("sj", 2 * NB * W, BF),
        ("nf", 2 * NB * W, BF), ("cnt", 2 * NB * W, BF),
        ("acc", 2 * NB, F32), ("pf", 2 * NB, F32), ("mo", 2 * R * NB, U16), ("ml", 2 * R * NB, U16), ("rp", XW + V, BF),
        ("exh", C, BF), ("exl", C, BF), ("fh", 96, U16), ("fl", 96, U16), ("ir", 96, F32),
        ("ok", C, BF), ("nok", C, BF), ("okd", C, BF), ("l1", C, BF), ("h1", C, BF), ("lh", 2 * C, BF),
        ("pp", 4 * XW, BF), ("gh", 4 * C, BF), ("yt", 4 * C, BF), ("yq", PAD, Q4), ("ys", PAD, U8),
        ("rb", 4 * C, F32), ("yo", C, F32)]:
    _sb(_n, _w, _t)

NDMA = 9
SEMAPHORES = (["v", "a", "t", "g", "sent", "out"]
              + ["xa%d%d" % (_r, _k) for _r in range(R) for _k in range(len(RUNS[_r]))]
              + ["da%d%d" % (_r, _k) for _r in range(R) for _k in range(NS)]
              + ["ma%d%d" % (_r, _k) for _r in range(R) for _k in range(len(PARTS))]
              + ["h%s%d" % (_c, _k) for _c in "cp" for _k in range(len(RUNS[R - 1]))] + ["d%d" % _k for _k in range(NDMA)])


def _helpers(T, topo, c, r):
    p = T.cores[T.rank_of(c) ^ (1 << r)]
    if topo.chip(p) == topo.chip(c):
        return {}
    mine = [k for k in topo.cores_of(c) if topo.die(k) == topo.die(c)]
    far = [k for k in range(CORES) if topo.mates(topo.chip(k), topo.chip(p)) and topo.die(k) == topo.die(c) and topo.may_write(k, p)]
    able = [k for k in mine if topo.may_write(k, far[0])]
    ways = {1: [k for k in topo.cores_of(c) if topo.die(k) != topo.die(c)][mine.index(c)]}
    ways[2] = far[able.index(c)] if c in able else ways[1]
    return ways


def _ways(T, topo, c, r):
    h = _helpers(T, topo, c, r)
    return {(k, i): h.get(run[2 + i][T.rank_of(c) % 4]) for k, run in enumerate(RUNS[r]) for i in range(2)}


def _send(g, T, topo, dst, en, out, in_, sem):
    rid, pid, _ = topo.addr(dst)
    g.remote_dma(out, in_, sem, T.sem.sent, pid, rid, sum(1 << e for e in en))
    return len(en)


def _sides(T, r, k, i):
    names = ("qx%d" % r, "hq", "lq%d" % r) if i == 0 else ("sx%d" % r, "hs", "ls%d" % r)
    a, b, sems = RUNS[r][k][0], RUNS[r][k][1], ("h%s%d" % ("cp"[i], k), "xa%d%d" % (r, k))
    return [T[x][:, a:b].bitcast(dt.uint8) if i == 0 else T[x][:, a:b] for x in names], sems


def _hand_on(g, core, T, topo):
    for c in T.cores:
        for r in range(R):
            p, to, sent = T.cores[T.rank_of(c) ^ (1 << r)], _ways(T, topo, c, r), 0
            for k, i in sorted(to):
                if to[k, i] == core:
                    (src, held, land), (here, there) = _sides(T, r, k, i)
                    g.wait_ge(T.sem[here], len(topo.engines(c, core)))
                    sent += _send(g, T, topo, p, topo.engines(core, p), land, held, T.sem[there])
            if sent:
                g.wait_ge(T.sem.sent, sent)


_laid = []


def _lay_out(calls):
    n = len(calls)
    queue, busy, late = [c[0] for c in calls], [c[2] for c in calls], [c[3] for c in calls]
    before = [[(j, late[j] + WAKE if c[0] else busy[j]) for j in c[1]] for c in calls]
    after = [[] for _ in calls]
    for i in range(n):
        for j, gap in before[i]:
            after[j].append((i, gap + busy[i] - busy[j]))

    def lay(turn, back=False):
        turn = list(turn)
        for i in (range(n - 1, -1, -1) if back else range(n)):
            for j, _ in (after[i] if back else before[i]):
                if turn[i] <= turn[j]:
                    turn[i] = turn[j] + 1e-7
        at, taken = [0.0] * n, {}
        for i in sorted(range(n), key=lambda i: turn[i]):
            t = late[i] - busy[i] if back else 0.0
            for j, gap in (after[i] if back else before[i]):
                if at[j] + gap > t:
                    t = at[j] + gap
            if queue[i]:
                runs = taken.setdefault(queue[i], [])
                k = len(runs)
                while k and runs[k - 1][1] > t:
                    k -= 1
                while k < len(runs) and t + busy[i] > runs[k][0] + 1e-9:
                    t = max(t, runs[k][1])
                    k += 1
                runs.insert(k, (t, t + busy[i]))
            at[i] = t
        return at

    def worth(at):
        return max(at[i] + late[i] for i in range(n)) + 0.1 * sum(at) / n

    def mirrored(at):
        end = lay([-at[i] - busy[i] for i in range(n)], True)
        return [max(end) - end[i] - busy[i] for i in range(n)]

    best = lay(range(n))
    for _ in range(3):
        best = min(best, lay(mirrored(best)), key=worth)
    least, seed = worth(best), [1]

    def chance():
        seed[0] = seed[0] * 48271 % 2147483647
        return seed[0] / 2147483647

    for _ in range(TURNS):
        kind, mid, wide, far = chance(), chance(), chance(), chance()
        near = [i for i in range(n) if abs(best[i] - mid * least) < 0.3 + 2.2 * wide]
        turn = list(best)
        if kind < 0.2:
            other = mirrored(best)
            for i in near:
                turn[i] = other[i]
        elif kind < 0.6 and near:
            turn[near[int(chance() * len(near))]] += 3 * far - 1.5
        else:
            for i in near:
                turn[i] += far * (chance() - 0.5)
        at = lay(turn)
        if worth(at) <= least:
            best, least = at, worth(at)
    return best


def rank_program(g, core, T, topo):
    rank = T.rank_of(core)
    if rank is None:
        _hand_on(g, core, T, topo)
        return
    queue = {"v": g.vector, "a": g.scalar, "t": g.tensor, "g": g, "s": g.sync}
    count = {"sent": 0, "out": 0}
    calls, writer, readers = [], {}, {}
    ndma, first = [0], []

    def note(q, r, w, busy, late, issue, after=()):
        before = set(after)
        for k in r:
            if k in writer:
                before.add(writer[k])
            if k.startswith("ps"):
                before.update(e for e in readers.get(k, []) if calls[e][0] != q)
        for k in w:
            if k in writer:
                before.add(writer[k])
            before.update(readers.get(k, []))
        calls.append((q, before, busy, late, issue, any(k.startswith(FILL) for k in w)))
        for k in r:
            readers.setdefault(k, []).append(len(calls) - 1)
        for k in w:
            writer[k] = len(calls) - 1
            readers[k] = []
        return len(calls) - 1

    def op(q, r, w, time, call):
        def issue():
            call(queue[q]).then_inc(T.sem[q], 1)
            count[q] = count.get(q, 0) + 1
            return q, count[q]
        note(q, r, w, time, time, issue)

    def dma(q, r, w, out, in_, late=DMA):
        s = "d%d" % ndma[0]
        ndma[0] += 1

        def issue():
            queue[q].dma_start(out, in_).then_inc(T.sem[s], 16)
        time = ISSUE if q == "g" else 64 * CYCLE
        arrives(s, 16, w, late, [note(q, r, ["loads"], time, time - WAKE, issue)])

    def put(q, r, out, in_):
        def issue():
            queue[q].dma_start(out, in_).then_inc(T.sem.out, 16)
            count["out"] += 16
        note(q, r, [], 64 * CYCLE, DMA, issue)

    def write(r, dst, out, in_, sem, w=()):
        def issue():
            count["sent"] += _send(g, T, topo, dst, topo.engines(core, dst), out, in_, T.sem[sem])
        time = ISSUE + (0.0 if first else FIRST)
        first.append(1)
        return note("g", r, w, time, time - WAKE, issue)

    def arrives(sem, n, w, late, after):
        count[sem] = n
        note(None, [], w, 0.0, late, lambda: (sem, n), after)

    def words(ap):
        return ap.bitcast(dt.uint32)

    def raw(ap):
        return ap.bitcast(dt.uint8)

    def bank(b, n, a=0):
        return T.ps[:, 512 * b + a:512 * b + a + n]

    def cycles(out, per, by_list=False):
        return CYCLE * (70 + 1.56 * out.shape[1] if by_list else max(64, per * out.shape[1]))

    def ts(out, in0, s1, s2, o0, o1, r, w):
        if o1 is None:
            op("v", r, w, cycles(out, 1), lambda e: e.tensor_scalar(out, in0, s1, None, o0))
        else:
            op("v", r, w, cycles(out, 1), lambda e: e.tensor_scalar(out, in0, s1, s2, o0, o1))

    def tt(out, in0, in1, o, r, w, by_list=False):
        op("v", r, w, cycles(out, 1 if any(k.startswith("ps") for k in r) else 2, by_list), lambda e: e.tensor_tensor(out, in0, in1, o))

    def cp(out, in_, r, w, by_list=False):
        op("v", r, w, cycles(out, 1, by_list), lambda e: e.tensor_copy(out, in_))

    def fill(out, c, w):
        op("v", [], w, cycles(out, 0.5), lambda e: e.memset(out, c))

    def scan(out, d0, d1, init, o0, o1, r, w, per=1):
        op("v", r, w, cycles(out, per), lambda e: e.tensor_tensor_scan(out, d0, d1, init, o0, o1))

    def quant(q, s, in_, r, w):
        op("v", r, w, cycles(q, 1.1), lambda e: e.quantize_mx(q, s, in_))

    def act(out, in_, f, r, w, by_list=False, **kw):
        op("a", r, w, cycles(out, 1, by_list) + ("accum_out" in kw) * 24 * CYCLE, lambda e: e.activation(out, in_, f, **kw))

    def move(q, out, in_, r, w, by_list=False):
        if q == "a":
            act(out, in_, ACT.Copy, r, w, by_list)
        else:
            cp(out, in_, r, w, by_list)

    def mm(b, n, lq, ls, rq, rs, r):
        op("t", r, ["ps%d" % b], 0.76 * CYCLE * (n + 16), lambda e: e.matmul_mx(bank(b, n), lq, ls, rq, rs, True, True))

    def iota(name, out, pattern, base, cm):
        time = CYCLE * (150 + 2 * out.shape[1])
        if name in ("pi", "li"):
            op("g", [], [name], time, lambda e: e.iota(out, pattern, base, cm))
        else:
            op("g", [], [name], time, lambda e: e.iota(out, pattern, base, cm, allow_small_or_imprecise_dtypes=True))

    def issue_all():
        n = len(calls)
        if not _laid:
            _laid.append(_lay_out(calls))
        start = _laid[0]
        known = {q: {} for q in queue}
        done = {}
        for i in sorted(range(n), key=lambda i: (start[i], i)):
            q, before = calls[i][:2]
            for sem, k, seen in sorted((done[j] for j in before if q and done[j]), key=lambda e: -e[1]):
                if known[q].get(sem, 0) < k:
                    queue[q].wait_ge(T.sem[sem], k)
                    known[q][sem] = k
                    for s in seen:
                        known[q][s] = max(known[q].get(s, 0), seen[s])
            ev = calls[i][4]()
            done[i] = ev and (ev[0], ev[1], dict(known[q]) if q else {})
        for s in count:
            if count[s] and max(known[q].get(s, 0) for q in known) < count[s]:
                g.wait_ge(T.sem[s], count[s])

    mate = [T.cores[rank ^ (1 << r)] for r in range(R)]

    def keys(name, n):
        return ["%s%d" % (name, i) for i in range(n)]

    def slots(name, a, b):
        return ["%s%d" % (name, n) for n in range(a, b)]

    def cols(name, a, b):
        return slots(name, a // 16, b // 16)

    def ahead(k):
        return CUT[k], max(CUT[k + 1], CUT[k] + 128)

    def behind(k):
        return min(CUT[k], CUT[k + 1] - 128), CUT[k + 1]

    def xkeys(r, a, b):
        return ["qx%d%d" % (r, k) for k in range(NS) if CUT[k] < b and a < CUT[k + 1]]

    def landed(r, a, b):
        return ["lx%d%d" % (r, k) for k, run in enumerate(RUNS[r]) if run[0] < b and a < run[1]]

    def ship(r, k, between=None):
        n, sent = 0, []
        for i in range(2):
            if i and between:
                between()
            (src, held, land), (there, end) = _sides(T, r, k, i)
            h, rd = _ways(T, topo, core, r)[k, i], xkeys(r, RUNS[r][k][0], RUNS[r][k][1]) + ["told"]
            sent.append(write(rd, mate[r], land, src, end) if h is None else write(rd, h, held, src, there))
            h = _ways(T, topo, mate[r], r)[k, i]
            n += len(topo.engines(mate[r] if h is None else h, core))
        near = topo.chip(mate[r]) == topo.chip(core)
        arrives("xa%d%d" % (r, k), n, ["lx%d%d" % (r, k)], HOP + 0.5 if near else 2 * HOP + 2.0, sent)

    def ship_piece(r, k):
        for i, run in enumerate(RUNS[r]):
            if CUT[k] < run[1] <= CUT[k + 1]:
                ship(r, i)

    def swap(r, sem, out, in_, rd, w):
        near = topo.chip(mate[r]) == topo.chip(core)
        arrives(sem, len(topo.engines(mate[r], core)), w, HOP + (0.0 if near else WAKE), [write(rd, mate[r], out, in_, sem, ["told"])])

    PL, PA, PB, AM, CY, T2, T4, NQ, MQ, WQ = [T.col[:, k:k + 1] for k in range(10)]

    def scores(r, k, b=7):
        a, z = behind(k)
        lq, ls, key = (T.urq, T.urs, ["urq", "urs"]) if r < R else (T.vq, T.vs, ["vq"])
        mm(b, z - a, lq[:], ls[:], T["qx%d" % r][:, a:z], T["sx%d" % r][:, a:z], key + xkeys(r, a, z))

    def piece(k, b, a=None, z=None):
        a, z = (CUT[k], CUT[k + 1]) if a is None else (a, z)
        return bank(b, z - a, a - behind(k)[0])

    def windows(r, a, b):
        if a == 0:
            mm(0, C, T.urq[:], T.urs[:], T["qx%d" % r][:, 0:C], T["sx%d" % r][:, 0:C], ["urq", "urs"] + xkeys(r, 0, C))
        for i in range(a, b):
            j = 16 * i - V
            for x, y in ((0, V), (V, W)) if j < 0 else ((0, 2 * V), (2 * V, W)) if j + W > C else ((0, W),):
                tt(T.mw[:, W * i + x:W * i + y], bank(0, y - x, (j + x) % C), T.mk[:, x:y], ALU.add, ["ps0", "mk"], ["mw%d_%d" % (i, x)])

    def mask(k, b=7):
        a, z = CUT[k], CUT[k + 1]
        tt(T.msk[:, a:z], piece(k, b), T.dm[:, 0:z - a], ALU.mult, ["ps%d" % b, "dm"], ["msk%d" % k])
        turn(k, b)

    def hold(k):
        a, z = CUT[k], CUT[k + 1]
        scan(T.hold[:, a:z], T.rs[:, 0:z - a], T.msk[:, a:z], 0.0, ALU.mult, ALU.add, ["rs", "msk%d" % k], ["hold%d" % k])

    def tell(r, k, q, k0=None):
        k0 = k if k0 is None else k0
        rd = []
        for i in range(k0, k + 1):
            a, z, c = CUT[i], CUT[i + 1], DW * r + AT[i]
            move(q, T.dgs[:, c:c + (z - a) // 16], T.hold[:, a + 15:z:16], ["dgs", "hold%d" % i], ["dgs%d%d" % (r, i)])
            rd.append("dgs%d%d" % (r, i))
            for a, z, c, _ in TURNED[i]:
                move("a", T.dgs[:, DW * r + c:DW * r + c + (z - a) // 16], T.tr[:, a:z:16], ["dgs"] + cols("tr", a, z), ["dgt%d%d" % (r, a)])
                rd.append("dgt%d%d" % (r, a))
        c, d = DW * r + AT[k0], DW * r + END[k]
        swap(r, "da%d%d" % (r, k), T.dgl[:, c:d], T.dgs[:, c:d], rd + ["dgs"], slots("dgl%d_" % r, k0, k + 1))

    def turn(k, b=7):
        for a, z, _, _ in TURNED[k]:
            op("v", ["ps%d" % b], cols("tr", a, z), cycles(T.tr[:, a:z], 1), lambda e, a=a, z=z: e.transpose(T.tr[:, a:z], piece(k, b, a, z)))

    def far_row(r, k):
        for a, z, c, x in TURNED[k]:
            c += DW * r
            move("a", T.bc[:, a:z], T.dgl[:, c // 8 * 8:c + (z - a) // 16].indirect(T.lj[:, c % 8:c % 8 + (z - a) // 16]),
                 ["lj", "dgl%d_%d" % (r, k)], cols("bc", a, z), True)
            op("v", cols("bc", a, z), cols("fw", x, x + z - a), cycles(T.bc[:, a:z], 1),
               lambda e, a=a, z=z, x=x: e.transpose(T.fw[:, x:x + z - a], T.bc[:, a:z]))

    def diffs(r, a, b):
        for i in range(a, b):
            k = max(k for k in range(NS) if CUT[k] <= 16 * (i % NB))
            c = DW * r + AT[k] + i - CUT[k] // 16
            act(T.dd[:, W * i:W * i + W], T.mw[:, W * i:W * i + W], ACT.Abs, ["mw%d_%d" % (i, x) for x in (0, V, 2 * V)] + ["dgl%d_%d" % (r, k)],
                ["dd%d" % i], bias=T.dgl[:, c:c + 1], scale=-1.0)

    def least(a, b):
        scan(T.p2[:, W * a:W * b], T.rst[:, 0:W * (b - a)], T.dd[:, W * a:W * b], 0.0, ALU.add, ALU.min,
             ["rst"] + slots("dd", a, b), slots("p2", a, b))

    def signs(a, b):
        for i in range(a, b):
            act(T.sj[:, W * i:W * i + W], T.p2[:, W * i:W * i + W], ACT.Sign, ["p2%d" % i], ["acc%d" % i],
                bias=T.p2[:, W * i + W - 1:W * i + W], scale=-1.0, accum_out=T.acc[:, i:i + 1])

    def fallen(a, b):
        scan(T.pm[:, 1 + W * a:1 + W * b], T.dd[:, W * a:W * b], T.mk[:, 0:W * (b - a)], BIG, ALU.min, ALU.max,
             ["mk"] + slots("dd", a, b), slots("pm", a, b))

    def flags(a, b):
        tt(T.nf[:, W * a:W * b], T.pm[:, 1 + W * a:1 + W * b], T.pm[:, W * a:W * b], ALU.is_ge,
           ["pm"] + slots("pm", a - 1, b), slots("nf", a, b))

    def tally(a, b):
        scan(T.cnt[:, W * a:W * b], T.nf[:, W * a:W * b], T.one[:, 0:W * (b - a)], 0.0, ALU.mult, ALU.add,
             ["one"] + slots("nf", a, b), slots("cnt", a, b), 0.5)

    def counted(a, b):
        ts(T.acc[:, a:b], T.cnt[:, W * a + W - 1:W * b:W], -float(W), None, ALU.add, None, slots("cnt", a, b), slots("acc", a, b))

    def lists(t, r, p):
        a, z = PARTS[p]
        o = 2 * (NB * r + a)
        return t[:, o:o + z - a], t[:, o + z - a:o + 2 * (z - a)], t[:, o:o + 2 * (z - a)]

    def answer(r, p, batches):
        a, z = PARTS[p]
        o, mf, md = 2 * (NB * r + a) - a, slots("mf%d_" % r, a, z), slots("md%d_" % r, a, z)
        if z - a > ONE:
            for x, y, q in batches:
                if q == "v":
                    counted(x, y)
            tt(T.pf[:, a:z], T.ik[:, a:z], T.acc[:, a:z], ALU.subtract, ["ik"] + slots("acc", a, z), slots("pf", a, z))
            ts(T.mo[:, o + z:o + 2 * z - a], T.acc[:, a:z], -1.0, MQ, ALU.mult, ALU.add, ["mq"] + slots("acc", a, z), md)
            cp(T.mo[:, o + a:o + z], T.pf[:, a:z], slots("pf", a, z), mf)
        else:
            for x, y, q in batches:
                def got(i, k):
                    return T.acc[:, i:k] if q == "a" else T.cnt[:, W * i + W - 1:W * k:W]
                name, c, col = ("acc", V, MQ) if q == "a" else ("cnt", V + W, WQ)
                for i in range(x, y):
                    ts(T.mo[:, o + i:o + i + 1], got(i, i + 1), -1.0, float(16 * i + c), ALU.mult, ALU.add, [name + str(i)], [mf[i - a]])
                ts(T.mo[:, o + z - a + x:o + z - a + y], got(x, y), -1.0, col, ALU.mult, ALU.add, ["mq"] + slots(name, x, y), md[x - a:y - a])
        swap(r, "ma%d%d" % (r, p), lists(T.ml, r, p)[2], lists(T.mo, r, p)[2], mf + md, ["ml%d%d" % (r, p)])

    def mine(r, a, z, i):
        if a >= BOTH:
            return T.mm[:, NB * i + a:NB * i + z], slots("mm", NB * i + a, NB * i + z)
        p = max(p for p in range(len(PARTS)) if PARTS[p][0] <= a)
        o = 2 * (NB * r + PARTS[p][0]) + i * (PARTS[p][1] - PARTS[p][0]) - PARTS[p][0]
        return T.ml[:, o + a:o + z], ["ml%d%d" % (r, p)]

    def theirs(r, p, q):
        a, z = PARTS[p]
        f = lists(T.mo, r, p)[0]
        runs = [(2 * V + 16 * a, 2 * V + 16 * z, f)]
        if a == 0:
            runs.append((2 * V + C, 3 * V + C, T.mo[:, 2 * NB * r:2 * NB * r + 1]))
        if z == NB:
            o = 2 * (NB * r + a) + z - a
            runs.insert(0, (0, 2 * V, T.mo[:, o - 2:o]))
        for x, y, off in runs:
            move(q, T.rp[:, x:y], T.cyc[:].indirect(off), ["cyc"] + slots("mf%d_" % r, a, z), cols("rp", x, y), True)

    def check(r, i, k):
        a, z = 16 * i, 16 * k
        (to, rt), (by, rb) = mine(r, i, k, 0), mine(r, i, k, 1)
        tt(T.ok[:, a:z], T.rp[:, 0:z + 3 * V].indirect(to), T.cyc[:, 2 * V + a:2 * V + z], ALU.is_equal,
           cols("rp", 0, z + 3 * V) + rt + ["cyc"], cols("ok", a, z), True)
        act(T.nok[:, a:z], T.ok[:, a:z], ACT.Identity, cols("ok", a, z), cols("nok", a, z), bias=1.0, scale=-1.0)
        tt(T.okd[:, a:z], T.cdv[:].indirect(by), T.ok[:, a:z], ALU.mult, cols("ok", a, z) + rb + ["cdv"], cols("okd", a, z), True)

    def unpack(q, s, b0, r):
        for b in range(4):
            mm(b0 + b, C, T.eq[:, 128 * b:128 * b + 128], T.es[:, 128 * b:128 * b + 128], q[:, 0:C], s[:, 0:C], ["eq%d" % b] + r)

    def evac_p(b, q):
        out, r, w = T.pp[:, 4 * V + b:4 * (V + C):4], ["ps%d" % (4 + b)], ["pp%d" % b]
        if q == "a":
            act(out, bank(4 + b, C), ACT.Identity, r, w, scale=0.5)
        else:
            ts(out, bank(4 + b, C), 0.5, None, ALU.mult, None, r, w)

    def ends_p():
        act(T.pp[:, 0:4 * V], T.pp[:, 4 * C:4 * (C + V)], ACT.Copy, keys("pp", 4), ["ppa"])
        act(T.pp[:, 4 * (C + V):4 * XW], T.pp[:, 4 * V:8 * V], ACT.Copy, keys("pp", 4), ["ppz"])

    def carry(t, o, a, z, init, r, rev=False):
        def run(x, o=0):
            return x[:, o + a:o + z] if not rev else x[:, o + z - 1:o + a - 1:-1] if o + a else x[:, z - 1::-1]
        scan(run(T[t], o), run(T.nok), run(T.okd), init, ALU.mult, ALU.add, cols("nok", a, z) + cols("okd", a, z) + r,
             cols(t, o + a, o + z), 0.5)

    def pick(o, ex):
        scan(T[ex][:], T.lh[:, o:o + C], T.ky[:], -224.0, ALU.max, ALU.add, keys("ky", 4) + cols("lh", o, o + C), [ex], 0.5)

    def offsets(off, ex):
        ts(T[off][:], T[ex][:, 3:C:4], 4.0, CY, ALU.mult, ALU.add, [ex, "cy"], [off])

    plane = keys("pp", 4) + ["ppa", "ppz"]

    def source(a, z, off):
        k = max(i for i in range(len(WIN)) if WIN[i] <= a)
        return T.pp[:, 4 * WIN[k]:4 * (WIN[k + 1] + 2 * V)].indirect(T[off][:, a // 4:z // 4])

    def take_h(a, z, q="a"):
        move(q, T.gh[:, 4 * a:4 * z], source(a, z, "fh"), plane + ["fh"], cols("gh", a, z), True)

    def take_l(a, z):
        tt(T.yt[:, 4 * a:4 * z], source(a, z, "fl"), T.gh[:, 4 * a:4 * z], ALU.add, plane + ["fl"] + cols("gh", a, z), cols("yt", a, z), True)

    def quant_y(k):
        a, z = behind(k)
        quant(T.yq[:, a:z], T.ys[:, a:z], T.yt[:, 4 * a:4 * z], cols("yt", a, z), cols("yq", a, z))

    def layers(k, b0=0, b1=4):
        a, z = behind(k)
        for b in range(b0, b1):
            mm(4 + b, z - a, T.wq[:, 128 * b:128 * b + 128], T.wp[:, 128 * b:128 * b + 128], T.yq[:, a:z], T.ys[:, a:z],
               ["wq", "wp"] + cols("yq", a, z))

    def relus(k, b0, b1):
        a, z = CUT[k], CUT[k + 1]
        for b in range(b0, b1):
            c = 4 + b
            act(T.rb[:, C * b + a:C * b + z], piece(k, c), ACT.Relu, ["ps%d" % c], ["rb%d%d" % (k, b)], scale=0.03125)

    def adds(k, b0, b1):
        a, z = CUT[k], CUT[k + 1]
        for b in range(b0, b1):
            tt(T.x1[:, 4 * a + b:4 * z:4], T.rb[:, C * b + a:C * b + z], bank(b, z - a, a), ALU.add,
               ["rb%d%d" % (k, b), "ps%d" % b], ["x1%d%d" % (k, b)])

    def quant_x(r, k):
        a, z = ahead(k)
        over = [i for i in range(k, NS) if CUT[i] < z]
        quant(T["qx%d" % r][:, a:z], T["sx%d" % r][:, a:z], T.x1[:, 4 * a:4 * z],
              ["x1z"] + [x for i in over for x in keys("x1%d" % i, 4)], ["qx%d%d" % (r, i) for i in over])

    def onward(r, k):
        if r < R:
            ship_piece(r, k)
            return
        q, s, a, z = T["qx%d" % R], T["sx%d" % R], CUT[k], CUT[k + 1]
        put("s", xkeys(R, a, z), T.oc[:, 4 * a:4 * z], raw(q[:, a:z]))
        if k in (0, NS - 1):
            a = CUT[min(k, 1)]
            for i in range(4):
                put("sa"[i // 2 * (k > 0)], xkeys(R, a, z), T.osc[4 * i:4 * i + 4, a:z], s[32 * i:32 * i + 4, a:z])

    def result(k, q, b):
        move(q, T.yo[:, CUT[k]:CUT[k + 1]], piece(k, b), ["ps%d" % b], ["yo%d" % k])
        if k in (0, NS - 1):
            a, z = CUT[min(k, 1)], CUT[k + 1]
            put("a" if k else "s", keys("yo", k + 1), T.y[:, a:z], T.yo[:, a:z])

    dma("s", [], ["x00"], T.x0[:, 0:4 * CUT[1]], T.x[:, 0:4 * CUT[1]], DMA + 0.2)
    dma("s", [], ["ut"], T.ut[:], T.u[:], DMA + 0.8)
    dma("s", [], ["x01"], T.x0[:, 4 * CUT[1]:4 * C], T.x[:, 4 * CUT[1]:4 * C], DMA + 1.7)
    iota("pi", T.pi[:], [[0, 8]], 0, 1)
    iota("li", T.li[:], [[16, 8]], 0, 0)
    iota("i16", T.i16[:], [[0, WIDE // 16], [1, 16]], 0, 0)
    iota("t48", T.t48[:], [[0, 8], [1, W]], 0, 0)
    iota("ik", T.ik[:], [[16, NB]], V, 0)
    iota("cdv", T.cdv[:], [[1, W]], -V, 0)
    fill(T.one[:], 1.0, ["one"])
    ts(T.pa[:], T.pi[:], 15, None, ALU.bitwise_and, None, ["pi"], ["pa"])
    cp(T.lu[:], T.li[:], ["li"], ["lu"])
    ts(T.pd[:], T.pi[:], 2, 3, ALU.arith_shift_right, ALU.bitwise_and, ["pi"], ["pd"])
    cp(PL, T.pa[:, 0:1], ["pa"], ["pl"])
    ts(T.pc[:], T.pi[:], 3, None, ALU.bitwise_and, None, ["pi"], ["pc"])
    cp(PA, T.pd[:, 0:1], ["pd"], ["pac"])
    ts(NQ, PL, -1.0, -float(V), ALU.mult, ALU.add, ["pl"], ["nq"])
    ts(T.dm[:], T.i16[:], PL, None, ALU.is_equal, None, ["i16", "pl"], ["dm"])
    ts(T.rs[:], T.i16[:], 0.0, None, ALU.is_gt, None, ["i16"], ["rs"])
    fill(T.pm[:, 0:NB * W + 1:W], BIG, ["pm"])
    fill(T.rp[:, 0:2 * V], 0.0, cols("rp", 0, 2 * V))
    fill(T.dgs[:], 0.0, ["dgs"])
    ts(WQ, PL, -1.0, float(W), ALU.mult, ALU.add, ["pl"], ["wq_"])
    ts(MQ, PL, -1.0, None, ALU.mult, None, ["pl", "wq_"], ["mq"])
    ts(T2, PA, 0.0, 4.0, ALU.is_equal, ALU.mult, ["pac"], ["t2"])
    ts(PB, T.pc[:, 0:1], -64.0, None, ALU.add, None, ["pc"], ["pbc"])
    ts(T4, PA, 32.0, None, ALU.add, None, ["pac"], ["t4"])
    ts(AM, PA, T2, -1.0, ALU.add, ALU.add, ["pac", "t2"], ["am"])
    ts(T.ya[:], T.i16[:, 0:4], PA, None, ALU.is_equal, None, ["i16", "pac"], ["ya"])
    ts(CY, T2, 224.0, PB, ALU.mult, ALU.add, ["t2", "pbc"], ["cy"])
    ts(T.yb[:], T.i16[:, 0:4], AM, -224.0, ALU.is_equal, ALU.mult, ["i16", "am"], ["yb"])
    ts(T.yc[:], T.ya[:], T4, None, ALU.mult, None, ["ya", "t4"], ["yc"])
    tt(T.yd[:], T.yc[:], T.yb[:], ALU.add, ["yc", "yb"], ["yd"])
    act(T.ta[:], T.t48[:], ACT.Abs, ["t48", "nq"], ["ta"], bias=NQ)
    act(T.rst[:], T.t48[:], ACT.Relu, ["t48"], ["rst"], bias=BIG, scale=-BIG)
    act(T.mk[:], T.ta[:], ACT.Relu, ["ta"], ["mk"], bias=-V * BIG, scale=BIG)
    quant(T.uq[:], T.us[:], T.ut[:], ["ut"], ["uq"])
    quant(T.qx0[:, 0:CUT[1]], T.sx0[:, 0:CUT[1]], T.x0[:, 0:4 * CUT[1]], ["x00"], ["qx00"])
    act(T.urs[:], T.us[:].indirect(T.lu[:]), ACT.Copy, ["uq", "lu"], ["urs"], True)
    cp(words(T.urq[:]), words(T.uq[:]).indirect(T.lu[:]), ["uq", "lu"], ["urq"], True)
    quant(T.qx0[:, CUT[1]:C], T.sx0[:, CUT[1]:C], T.x0[:, 4 * CUT[1]:4 * C], ["x01"], slots("qx0", 1, NS))
    for k in range(NS):
        scores(0, k, 7 - k)
        mask(k, 7 - k)
        hold(k)
    ship(0, 0, lambda: (tell(0, 0, "v"), tell(0, NS - 1, "v", 1)))
    ship(0, 1)
    op("g", ["one"], ["et"], 1200 * CYCLE, lambda e: e.affine_select(T.et[:], T.one[:], [[1, 516]], ALU.is_equal, 0.0, -3, -4))
    iota("cyc", T.cyc[:], [[0, 4], [1, 128]], 0, 0)
    iota("iy", T.iy[:], [[4, 96]], 0, 0)
    for k in range(1, NS):
        a, z = 4 * CUT[k + 1], 4 * ahead(k)[1]
        if a < z:
            act(T.x1[:, a:z], T.one[:, 0:z - a], ACT.Identity, ["one", "x1z"], ["x1z"] + keys("x1%d" % (k + 1), 4), scale=0.0)
    dma("s", ["dgl0_%d" % (NS - 1)], ["wq"], raw(T.wq[:]), T.wc[:])
    dma("s", ["dgl0_%d" % (NS - 1)], ["wp"], T.wp[:], T.ws[:])

    def patterns():
        for k in range(len(WIN) - 1):
            a, z = WIN[k] // 4, WIN[k + 1] // 4
            act(T.ir[:, a:z], T.iy[:, a:z], ACT.Identity, ["iy"], ["ir%d" % k], bias=-float(WIN[k]))
        for i in range(4):
            act(T.ky[:, i:C:4], T.ir[:], ACT.Identity, ["ya", "yd"] + keys("ir", len(WIN) - 1), ["ky%d" % i],
                scale=T.ya[:, i:i + 1], bias=T.yd[:, i:i + 1])

    for r in range(R):
        for p, batches in enumerate(MATCH if r else FIRST_MATCH):
            for a, z, q in batches:
                windows(r, a, z)
                diffs(r, a, z)
                for f in ((least, signs) if q == "a" else (fallen, flags, tally)):
                    f(a, z)
            answer(r, p, batches)
            theirs(r, p, THEIRS[p])
            for a, z in CHECK[p]:
                check(r, a, z)
        if r == 0:
            for b in range(4):
                quant(T.eq[:, 128 * b:128 * b + 128], T.es[:, 128 * b:128 * b + 128], T.et[:, 3 - b:515 - b], ["et"], ["eq%d" % b])
        unpack(T["lq%d" % r], T["ls%d" % r], 4, landed(r, 0, C))
        unpack(T["qx%d" % r], T["sx%d" % r], 0, xkeys(r, 0, C))
        for b in range(4):
            evac_p(b, EVAC[b])
        if r == 0:
            patterns()
        if r == 1:
            dma("s", ["ml10"], ["vt"], T.vt[:], T.v[:], DMA + 1.0)
        if r == R - 1:
            quant(T.vq[:], T.vs[:], T.vt[:], ["vt", "dgs%d%d" % (r, NS - 1)], ["vq"])
        ends_p()
        carry("l1", 0, 0, C, 0.0, [])
        carry("h1", 0, 0, C, 0.0, [], True)
        carry("lh", C, 0, C, T.l1[:, C - 1:C], cols("l1", C - 16, C), True)
        carry("lh", 0, 0, C, T.h1[:, 0:1], cols("h1", 0, 16))
        pick(C, "exh")
        pick(0, "exl")
        offsets("fh", "exh")
        offsets("fl", "exl")
        for a, z, q in TAKES:
            take_h(a, z, q)
        if r == R - 1:
            dma("g", cols("lh", 0, 2 * C), [], T.od[:], T.lh[0:128:16, :])
        n = r + 1

        def made(k):
            for a, z, _ in sorted(TAKES, key=lambda t: (t[0] > 0, t[2] == "a")):
                if CUT[k] <= a < CUT[k + 1]:
                    take_l(a, z)
            quant_y(k)

        def turn_of(k):
            return [(max(k - 1, 0) + b) % 4 for b in range(4)]

        def layer(k):
            for b in turn_of(k):
                layers(k, b, b + 1)
                relus(k, b, b + 1)

        def state(k):
            for b in turn_of(k):
                adds(k, b, b + 1)
            quant_x(n, k)

        def told(k):
            last = k == NS - 1
            b = 4 + k % 4
            scores(n, k, b)
            if n == R:
                onward(n, k)
                result(k, "av"[last], b)
                return
            if not last:
                onward(n, k)
            mask(k, b)
            hold(k)
            tell(n, k, TELL[k])
            if last:
                onward(n, k)

        for name, k in STATE:
            {"m": made, "l": layer, "s": state, "t": told}[name](int(k))
    issue_all()
